import numpy as np, ml_dtypes
CORES = [2,6,10,14,18,22,26,30]
N = 8
BF = ml_dtypes.bfloat16
def gentries(a):
    return np.ascontiguousarray(a.reshape(8, 16, -1).transpose(0, 2, 1)).reshape(8, -1)
def gtable(e):
    e = np.asarray(e); return np.ascontiguousarray(e.reshape(8, -1, 16).transpose(0, 2, 1)).reshape(128, -1).astype(np.int32)
NV, YM, P, LG, S, B, D0, D1 = 4096, 1024, 1024, 6, 1, 3, 800, 1000
def lst(a):
    return np.stack([gentries(b) for b in a]).astype(np.int64)
def walk(V, st, x, y, dx, dy, E, kp=None, L=None):
    logs = []
    for j in range(LG):
        for s in range(S):
            v = 64 * (y >> 4) + (x >> 4); e = E >> 6; d = np.zeros_like(E)
            for h in range(N):
                q = (h + j) % N
                a = np.take_along_axis(V[q], v[h][:, None, :], 2)
                d[h] = np.add.reduce(a * np.take_along_axis(st[q], e[h][:, None, :], 2), axis=1)
                if L is not None: L[h] += a * np.take_along_axis(kp[q], e[h][:, None, :], 2)
            E = np.maximum(E - d, 0)
            if j < LG - 1 or s < S - 1:
                t = np.where(d >= D1, 1, np.where(d >= D0, 2, 4))
                x = (x + t * dx) & 1023; y = (y + t * dy) & (YM - 1)
        logs.append(v)
    return E, logs
def verdict(E, F):
    s = np.sign(E - F)
    return np.sign(2 * s + np.add.reduce(s, axis=1, keepdims=True))
def mend(V, cor, logs, t):
    for q in range(N):
        for j in range(LG):
            h = (q - j) % N
            w = np.take_along_axis(cor[q], logs[j][h] // P * P + np.arange(P), 1)[:, None, :]
            a = np.take_along_axis(V[q], w, 2)
            np.put_along_axis(V[q], w, np.where(a > 0, np.minimum(a + t[h][:, None, :], 15), 0).astype(V.dtype), 2)
def parts(rng):
    a = {"V": rng.integers(0, 16, (N, 8, 16, NV)).astype(np.int32), "st": rng.integers(0, 16, (N, 8, 16, 1024)).astype(np.int32), "kp": np.exp2(5 * rng.random((N, 8, 16, 1024)) - 3)}
    for k, hi in (("x", 1024), ("y", YM), ("dx", 1024), ("dy", YM), ("E", 65536)): a[k] = rng.integers(0, hi, (N, 8, B, P))
    a["cor"] = np.ascontiguousarray(np.argsort(rng.random((N, 8, NV)), axis=-1))
    return a
def signs(rng):
    lean = rng.random((B - 1, N, 1, P))
    return np.where(rng.random((B - 1, N, 8, P)) < 0.25, 0, np.where(rng.random((B - 1, N, 8, P)) < lean, 1, -1))
def finish(rng, a, s=None, F=None, one=False, calm=False):
    V = a["V"].copy(); ev = (np.arange(8) % 2 == 0)[None, :, None]; out = []
    if s is None: s = signs(rng)
    for b in range(B if calm else B - 1):
        x, y, dx, dy = [a[k][:, :, b] for k in ("x", "y", "dx", "dy")]; E0 = a["E"][:, :, b]
        if calm:
            w = walk(V, a["st"], x, y, dx, dy, np.where(ev, 63, E0))[0]
            E0 = np.where(ev, np.minimum(63 - w + rng.integers(0, 4, w.shape), 63), E0); a["E"][:, :, b] = E0
            if b == B - 1: break
        E, logs = walk(V, a["st"], x, y, dx, dy, E0)
        if F is None:
            big = np.where(rng.random(E.shape) < 0.4, 1, rng.integers(1, 2000, E.shape))
            m = np.clip(E - s[b] * (1 if one else big), 0, 65535)
            if calm: m = np.where(ev, rng.integers(0, 4, E.shape), m)
        else: m = F[:, :, b]
        out.append(m); mend(V, a["cor"], logs, verdict(E, m))
    g = lambda z: np.stack([gtable(c.reshape(8, -1)) for c in z])
    r = {"slab": a["V"].reshape(N, 128, NV).astype(np.float32).astype(BF), "spow": a["st"].reshape(N, 128, 1024).astype(np.float32).astype(BF), "kap": a["kp"].reshape(N, 128, 1024).astype(np.float32).astype(BF)}
    for n, k in (("px", "x"), ("py", "y"), ("vx", "dx"), ("vy", "dy"), ("en", "E")): r[n] = g(a[k])
    r["fm"] = g(np.stack(out, axis=2)); r["cor"] = g(a["cor"])
    return r
def setup_inputs(rng):
    return finish(rng, parts(rng))
def setup_inputs_spread(rng):
    a = parts(rng); top = np.array([1, 2, 4, 8, 16, 16, 16])
    a["V"] = np.floor(rng.random((N, 8, 16, NV)) * rng.choice(top, (N, 8, 1, NV))).astype(np.int32)
    a["st"] = np.floor(rng.random((N, 8, 16, 1024)) * rng.choice(top, (N, 8, 1, 1024))).astype(np.int32)
    a["kp"] = np.exp2(rng.integers(-3, 2, (N, 8, 1, 1024))) * (1 + rng.random((N, 8, 16, 1024)))
    a["E"] = np.minimum(np.exp2(6 + 10 * rng.random((N, 8, B, P))).astype(np.int64), 65535)
    a["dx"] = np.exp2(9.99 * rng.random((N, 8, B, P))).astype(np.int64)
    return finish(rng, a)
def setup_inputs_ends(rng):
    a = parts(rng)
    def mixed(n):
        k = rng.integers(0, 4, (N, 8, 1, n))
        return np.where(k == 0, 15, np.where(k == 1, 0, 15 * rng.integers(0, 2, (N, 8, 16, n)))).astype(np.int32)
    a["V"] = mixed(NV); a["st"] = mixed(1024); a["kp"] = 4.0 * (rng.random((N, 8, 16, 1024)) < 0.4)
    for k, hi in (("x", 1023), ("y", YM - 1), ("dx", 1023), ("dy", YM - 1)): a[k] = hi * rng.integers(0, 2, (N, 8, B, P))
    a["E"] = 65535 * (rng.random((N, 8, B, P)) < 0.7).astype(np.int64)
    a["st"][:, 7] = np.where(rng.random((N, 1, 1024)) < 0.7, 15, a["st"][:, 7])
    a["st"][:, 7, :, 1023] = 15
    a["st"][:, 3, :, 1023] = 0
    for g in (3, 7):
        a["kp"][:, g, :, 1023] = 4.0
        for v in (0, 63, NV - 64, NV - 1): a["V"][:, g, :, v] = 15
        for p in (0, 1, P - 2, P - 1):
            a["x"][:, g, :, p] = 1023; a["y"][:, g, :, p] = YM - 1; a["dx"][:, g, :, p] = 0; a["dy"][:, g, :, p] = 0; a["E"][:, g, :, p] = 65535
    z = np.zeros(NV, np.int64); z[0::2] = np.arange(NV // 2); z[1::2] = NV - 1 - np.arange(NV // 2)
    for q in range(N):
        for g in range(8): a["cor"][q, g] = np.roll(z, int(rng.integers(0, NV)))
    return finish(rng, a, F=65535 * rng.integers(0, 2, (N, 8, B - 1, P)))
def setup_inputs_corners(rng):
    a = parts(rng); kd = (rng.permutation(8)[None, :] + np.arange(N)[:, None]) % 8
    first = P * np.arange(NV // P); edge = np.concatenate([first, first + P - 1])
    for q in range(N):
        for g in range(8):
            c = int(kd[q, g])
            if c in (0, 1, 2): a["V"][q, g] = (0, 15, 1)[c]
            if c in (3, 4): a["V"][q, g] = rng.integers(0, 2, (16, NV)) + (0 if c == 3 else 14)
            if c in (0, 1):
                a["x"][q, g] = 1023 * c; a["y"][q, g] = (YM - 1) * c; a["dx"][q, g] = 0; a["dy"][q, g] = 0
            if c == 2:
                a["x"][q, g] = 1023 - rng.integers(0, 2, (B, P)); a["y"][q, g] = YM - 1 - rng.integers(0, 2, (B, P)); a["dx"][q, g] = 1; a["dy"][q, g] = 1
            if c == 3:
                v = rng.choice(edge, (B, P))
                a["x"][q, g] = 16 * (v & 63) + rng.integers(0, 16, (B, P)); a["y"][q, g] = 16 * (v >> 6) + rng.integers(0, 16, (B, P)); a["dx"][q, g] = 0; a["dy"][q, g] = 0
            if c == 4: a["dx"][q, g] = 1023; a["dy"][q, g] = YM - 1
            if c == 5: a["E"][q, g] = rng.choice(np.array([0, 1, 63, 64, 65535]), (B, P))
            if c == 6: a["E"][q, g] = rng.integers(0, 3601, (B, P))
            if c == 1: a["cor"][q, g] = np.arange(NV)
            if c == 2: a["cor"][q, g] = np.arange(NV)[::-1]
    t = np.array([[1] * 8, [-1] * 8, [1] * 7 + [0], [-1] * 7 + [0], [1] * 7 + [-1], [-1] * 7 + [1], [1, -1] * 4, [1] + [0] * 7, [-1] + [0] * 7, [0] * 8,
                  [1, -1, -1, -1, 0, 0, 0, 0], [1, -1, -1, -1, -1, 0, 0, 0], [-1, 1, 1, 1, 0, 0, 0, 0], [-1, 1, 1, 1, 1, 0, 0, 0]])
    i = rng.integers(0, 14, (B - 1, N, 1, P)); o = rng.integers(0, 8, (B - 1, N, 1, P))
    return finish(rng, a, s=t[i, (np.arange(8)[None, None, :, None] + o) % 8])
def setup_inputs_ties(rng):
    a = parts(rng); t = rng.choice(np.array([D0 - 1, D0, D1 - 1, D1]), (N, 8, 1024)); t[..., D0 >> 6] = D0
    m = t // 15; k = np.argsort(rng.random((N, 8, 15, 1024)), axis=2)
    st = np.concatenate([(m // 15)[:, :, None] + (k < (m % 15)[:, :, None]), (t - 15 * m)[:, :, None]], axis=2)
    u = np.array([15] * 15 + [1]); pm = np.argsort(rng.random((N, 8, 16)), axis=-1)
    st = np.take_along_axis(st, pm[..., None], 2); v = np.broadcast_to(u[pm][..., None], (N, 8, 16, NV))
    a["V"][:, ::2] = v[:, ::2]; a["st"][:, ::2] = st[:, ::2]
    p = np.arange(P) % 4; E = a["E"]
    E = np.where(p == 0, D0 + rng.integers(-1, 2, E.shape), np.where(p == 1, 64 * rng.integers(1, 1024, E.shape) - rng.integers(0, 2, E.shape), E))
    a["E"][:, ::2] = E[:, ::2]
    return finish(rng, a, one=True)
def setup_inputs_calm(rng):
    a = parts(rng)
    v = np.where(rng.random((N, 8, 16, NV)) < 0.25, rng.integers(1, 4, (N, 8, 16, NV)), 0); a["V"][:, ::2] = v[:, ::2]
    k = np.argsort(rng.random((N, 8, 16)), axis=-1) < 2
    a["st"][:, ::2, :, 0] = k[:, ::2]
    return finish(rng, a, calm=True)
def check_ranges(d):
    bad = []
    for k, lo, hi in (("slab", 0, 15), ("spow", 0, 15), ("kap", 0, 4), ("px", 0, 1023), ("py", 0, YM - 1), ("vx", 0, 1023), ("vy", 0, YM - 1), ("en", 0, 65535), ("fm", 0, 65535), ("cor", 0, NV - 1)):
        a = np.asarray(d[k]).astype(np.float64)
        if not (np.min(a) >= lo and np.max(a) <= hi): bad.append("range of " + k)
        elif k in ("slab", "spow") and np.any(a != np.floor(a)): bad.append("whole numbers of " + k)
    if np.any(np.sort(lst(np.asarray(d["cor"])), axis=-1) != np.arange(NV)): bad.append("each voxel once in cor")
    return bad
def reference(slab, spow, kap, px, py, vx, vy, en, fm, cor):
    V = slab.astype(np.float32).astype(np.int32).reshape(N, 8, 16, NV); st = spow.astype(np.float32).astype(np.int32).reshape(N, 8, 16, 1024)
    kp = kap.astype(np.float64).reshape(N, 8, 16, 1024); x, y, dx, dy, E0 = [lst(a).reshape(N, 8, B, P) for a in (px, py, vx, vy, en)]
    F = lst(fm).reshape(N, 8, B - 1, P); cl = lst(cor); L = np.zeros((N, 8, 16, P)); E = np.zeros((N, 8, B, P), np.int64)
    for b in range(B):
        E[:, :, b], logs = walk(V, st, x[:, :, b], y[:, :, b], dx[:, :, b], dy[:, :, b], E0[:, :, b], kp, L)
        if b < B - 1: mend(V, cl, logs, verdict(E[:, :, b], F[:, :, b]))
    ye = np.stack([gtable((E[r] & 1023).reshape(8, B * P)) for r in range(N)])
    return {"yl": np.exp(L * -0.0078125).reshape(N, 128, P).astype(np.float32), "ye": ye.astype(np.float32)}

def check_inputs(d):
    bad = list(check_ranges(d))
    if not bad:
        for name, y in reference(**d).items():
            for q in range(N):
                v = np.abs(np.asarray(y[q], np.float64))
                if v.max() > 5 * np.sqrt(np.mean(v * v)): bad.append('%s of rank %d is uneven' % (name, q))
    return bad

@@ -1,0 +1,537 @@
+from concourse.bass import DstId, RemoteDMATransfer
+from concourse.mybir import AluOpType as A, ActivationFunctionType as F
+
+N = 8
+NB, LG = 3, 6
+MAGIC = 12582912.0
+OFF = -63.0 / 128.0
+
+PIECES = {"q0": ("bfloat16", 128), "q1": ("bfloat16", 128), "q2": ("bfloat16", 128), "q3": ("bfloat16", 128),
+          "sp": ("bfloat16", 128), "kp": ("bfloat16", 128), "el": ("uint16", 40), "ll": ("uint16", 160),
+          "y0": ("float32", 64), "y1": ("float32", 64), "ee": ("float32", 24)}
+
+
+def _sb(n, d):
+    return ("sbuf", [128, n], d)
+
+
+SCRATCH = {
+    "slabN": _sb(4096, "bfloat16"), "slabP": _sb(4096, "bfloat16"), "slabQ": _sb(4096, "bfloat16"),
+    "stT": _sb(1024, "bfloat16"), "kpT": _sb(1024, "bfloat16"), "amt": _sb(2048, "bfloat16"), "kg": _sb(2048, "bfloat16"),
+    "prod": _sb(1024, "bfloat16"), "pk": _sb(2048, "float32"),
+    "posv": _sb(4096, "float32"), "invrow": _sb(4096, "float32"), "invl": _sb(256, "float32"),
+    "lst": _sb(320, "int32"), "lst2": _sb(768, "int32"), "corI": _sb(256, "int32"),
+    "c1": _sb(256, "int32"), "c2": _sb(256, "int32"), "corT": _sb(256, "uint16"),
+    "e16s": _sb(320, "uint16"), "e16r": _sb(320, "uint16"), "l16s": _sb(1280, "uint16"), "l16r": _sb(1280, "uint16"),
+    "ia": _sb(256, "float32"), "iab": _sb(256, "float32"), "ib": _sb(16, "float32"), "ic": _sb(256, "float32"),
+    "w1": _sb(16, "float32"), "w2": _sb(16, "float32"),
+    "P32": _sb(256, "float32"), "P64": _sb(256, "bfloat16"), "Pb": _sb(256, "bfloat16"), "W": _sb(256, "bfloat16"),
+    "B": _sb(2048, "bfloat16"), "zero": _sb(512, "float32"), "rm": _sb(1536, "bfloat16"),
+    "xy": _sb(384, "int32"), "dxy": _sb(384, "float32"), "En": _sb(192, "float32"),
+    "q0i": _sb(384, "int32"), "v0a": _sb(192, "int32"), "v0b": _sb(192, "int32"),
+    "V16": _sb(1152, "uint16"), "E16": _sb(1152, "uint16"),
+    "mB": _sb(64, "float32"), "qi": _sb(128, "int32"), "qf": _sb(128, "bfloat16"),
+    "Fo": _sb(128, "float32"), "Fn": _sb(128, "float32"), "G": _sb(64, "float32"),
+    "sv": _sb(128, "bfloat16"), "votes0": _sb(512, "bfloat16"), "votes1": _sb(512, "bfloat16"),
+    "t4": _sb(64, "bfloat16"), "vI": _sb(384, "int32"), "kI": _sb(384, "int32"), "M": _sb(1536, "bfloat16"),
+    "tm": _sb(1536, "bfloat16"), "S": _sb(1536, "bfloat16"), "mn": _sb(1536, "bfloat16"), "mx": _sb(1536, "bfloat16"),
+    "U": _sb(256, "bfloat16"), "rb": _sb(4096, "bfloat16"), "yb": _sb(1024, "bfloat16"),
+    "yo": _sb(1024, "float32"), "ea": _sb(192, "float32"), "eb": _sb(192, "int32"), "ec": _sb(192, "int32"),
+    "eo": _sb(192, "float32"),
+}
+for _k in range(8):
+    SCRATCH["ps%d" % _k] = ("psum", [128, 512], "float32")
+for _k, (_d, _n) in PIECES.items():
+    SCRATCH["sg_" + _k] = ("dram", [8, 128, _n], _d)
+    SCRATCH["ld_" + _k] = ("dram", [8, 128, _n], _d)
+
+SEMAPHORES = (["cv", "ca", "ct", "cg", "sent", "inl", "inc", "inf", "own", "ownk", "inv", "votes0", "votes1", "outs"]
+              + ["s_" + k for k in PIECES] + ["a_" + k for k in PIECES] + ["l_" + k for k in PIECES])
+
+
+def ways(T, topo, r):
+    c = T.cores[r]
+    far = [q for q in range(N) if topo.chip(T.cores[q]) != topo.chip(c)]
+    near = [q for q in range(N) if q != r and topo.chip(T.cores[q]) == topo.chip(c)]
+    efar = topo.engines(c, T.cores[far[0]])
+    enear = [e for e in topo.engines(c, T.cores[near[0]]) if e not in efar] if near else []
+    return far, near, efar, enear
+
+
+def bits(es):
+    return sum(1 << e for e in es)
+
+
+def rank_program(g, core, T, topo):
+    me = T.rank_of(core)
+    if me is None:
+        return
+    Q = {"v": g.vector, "a": g.scalar, "t": g.tensor, "g": g, "s": g.sync}
+    own = {"v": "cv", "a": "ca", "t": "ct", "g": "cg"}
+    cnt, know, clock, wr, rd = {}, {q: {} for q in Q}, {}, {}, {}
+
+    def merge(q, ev):
+        k = know[q]
+        for s, v in list(clock.get(ev, {}).items()) + [ev]:
+            if k.get(s, 0) < v:
+                k[s] = v
+
+    def need(q, evs):
+        for ev in sorted(set(evs), key=lambda e: -e[1]):
+            if know[q].get(ev[0], 0) < ev[1]:
+                Q[q].wait_ge(T.sem[ev[0]], ev[1])
+                merge(q, ev)
+
+    def deps(q, R, W):
+        evs = []
+        for k in R:
+            evs += wr.get(k, [])
+        for k in W:
+            evs += wr.get(k, []) + rd.get(k, [])
+        if q == "t":
+            evs = [e for e in evs if e[0] != "ct"]
+        need(q, evs)
+
+    def done(q, ev, R, W):
+        clock[ev] = dict(know[q])
+        for k in W:
+            wr[k], rd[k] = [ev], []
+        for k in R:
+            if k not in W:
+                rd.setdefault(k, []).append(ev)
+
+    def op(q, fns, R, W):
+        deps(q, R, W)
+        for f in (fns if isinstance(fns, list) else [fns]):
+            ins = f()
+        s = own[q]
+        cnt[s] = cnt.get(s, 0) + 1
+        ins.then_inc(T.sem[s], 1)
+        done(q, (s, cnt[s]), R, W)
+
+    def dma(q, sem, moves, R, W):
+        deps(q, R, W)
+        for o, i in moves:
+            Q[q].dma_start(o, i).then_inc(T.sem[sem], 16)
+            cnt[sem] = cnt.get(sem, 0) + 16
+        done(q, (sem, cnt[sem]), R, W)
+
+    far, near, efar, enear = ways(T, topo, me)
+    turn = [0]
+
+    def dst(q):
+        a = topo.addr(T.cores[q])
+        return DstId(rid=a[0], pnc=a[1])
+
+    def arrivals(per_far):
+        n = 0
+        for q in range(N):
+            if q != me:
+                f2, n2, ef2, en2 = ways(T, topo, q)
+                n += per_far(ef2) if me in f2 else len(en2) // len(n2)
+        return n
+
+    def near_mask(k):
+        w = len(enear) // len(near)
+        return enear[k * w:(k + 1) * w]
+
+    def send(k):
+        deps("g", ["sg_" + k], [])
+        tr = []
+        for q in far:
+            e = efar[turn[0] % len(efar)]
+            turn[0] += 1
+            tr.append(RemoteDMATransfer(dst_ids=[dst(q)], dma_engine_mask=1 << e, remote_sem=T.sem["a_" + k],
+                                        src=T["sg_" + k][q], dst=T["ld_" + k][me]))
+            cnt["sent"] = cnt.get("sent", 0) + 1
+        for n, q in enumerate(near):
+            tr.append(RemoteDMATransfer(dst_ids=[dst(q)], dma_engine_mask=bits(near_mask(n)), remote_sem=T.sem["a_" + k],
+                                        src=T["sg_" + k][q], dst=T["ld_" + k][me]))
+            cnt["sent"] = cnt.get("sent", 0) + len(near_mask(n))
+        g.remote_dma_fused(tr, local_sem=T.sem.sent)
+        cnt["a_" + k] = arrivals(lambda ef: 1)
+        wr["ld_" + k] = [("a_" + k, cnt["a_" + k])]
+
+    def unload(q, k, buf, c0, c1, W, sem=None):
+        mv = []
+        if me > 0:
+            mv.append((buf[0:16 * me, c0:c1], T["ld_" + k][0:me]))
+        if me < N - 1:
+            mv.append((buf[16 * me + 16:128, c0:c1], T["ld_" + k][me + 1:N]))
+        dma(q, sem or "l_" + k, mv, ["ld_" + k], W)
+
+    r0, r1 = 16 * me, 16 * me + 16
+    V, S_, PE = g.vector, g.scalar, g.tensor
+
+    def ts(out, in0, s1, s2, o0, o1, R, W):
+        if o1 is None:
+            op("v", lambda: V.tensor_scalar(out, in0, s1, None, o0), R, W)
+        else:
+            op("v", lambda: V.tensor_scalar(out, in0, s1, s2, o0, o1), R, W)
+
+    def tt(out, a, b, o, R, W):
+        op("v", lambda: V.tensor_tensor(out, a, b, o), R, W)
+
+    def cp(out, a, R, W):
+        op("v", lambda: V.tensor_copy(out, a), R, W)
+
+    def act(out, a, f, R, W, bias=None, scale=None):
+        kw = {}
+        if bias is not None:
+            kw["bias"] = bias
+        if scale is not None:
+            kw["scale"] = scale
+        op("a", lambda: S_.activation(out, a, f, **kw), R, W)
+
+    def mm(items, R, W):
+        op("t", [(lambda it=it: PE.matmul(*it)) for it in items], R, W)
+
+    def win(t, o):
+        return t[:, o % 128:o % 128 + 128]
+
+    ps = [T["ps%d" % k] for k in range(8)]
+
+    dma("a", "inc", [(T.corI[:, :], T.cor[:, :])], [], ["corI"])
+    state = (T.px, T.py, T.vx, T.vy, T.en)
+    first = [(T.lst[:, 64 * k:64 * k + 64], t[:, 0:64]) for k, t in enumerate(state)]
+    dma("a", "inl", first[:2], [], ["lst"])
+    wr["lst"] = []
+    dma("s", "inl", first[2:], [], ["lst"])
+
+    def stage(k):
+        dma("a" if k == 0 else "s", "s_q%d" % k, [(T["sg_q%d" % k][:], T.slab[:, 1024 * k:1024 * k + 1024])], [],
+            ["sg_q%d" % k])
+
+    for k in range(3):
+        stage(k)
+
+    op("g", lambda: g.iota(T.ic[:, :], [[1, 256]], 0, 0, allow_small_or_imprecise_dtypes=True), [], ["ic"])
+    op("g", lambda: g.iota(T.ia[:, :], [[0, 2], [-1, 128]], 0, 1, allow_small_or_imprecise_dtypes=True), [], ["ia"])
+    op("g", lambda: g.iota(T.ib[:, :], [[0, 2], [-16, 8]], 0, 1, allow_small_or_imprecise_dtypes=True), [], ["ib"])
+
+    op("v", lambda: V.memset(T.W[:, :], 0.0), [], ["W"])
+    for i in range(16):
+        if i < 7:
+            ts(T.posv[:, i::16], T.ic[:, :], float(256 * i), None, A.add, None, ["ic"], ["posv%d" % i])
+        else:
+            act(T.posv[:, i::16], T.ic[:, :], F.Identity, ["ic"], ["posv%d" % i], bias=float(256 * i))
+    PV = ["posv%d" % i for i in range(16)]
+    cp(T.e16s[:, :], T.lst[:, :], ["lst"], ["e16s"])
+    dma("s", "s_el", [(T.sg_el[:], T.e16s[:, :]), (T.e16r[r0:r1, :], T.e16s[r0:r1, :])], ["e16s"], ["sg_el", "e16r_o"])
+    stage(3)
+    dma("s", "s_sp", [(T.sg_sp[:], T.spow[:, :])], [], ["sg_sp"])
+    dma("s", "own", [(T.slabN[r0:r1, :], T.slab[r0:r1, :]), (T.stT[r0:r1, :], T.spow[r0:r1, :])], [], ["slabN_o"])
+    dma("s", "s_kp", [(T.sg_kp[:], T.kap[:, :])], [], ["sg_kp"])
+
+    ts(T.c1[:, :], T.corI[:, :], 15, None, A.bitwise_and, None, ["corI"], ["c1"])
+    ts(T.c2[:, :], T.corI[:, :], 4, None, A.arith_shift_right, None, ["corI"], ["c2"])
+    ts(T.c1[:, :], T.c1[:, :], 256.0, None, A.mult, None, ["c1"], ["c1"])
+    tt(T.c1[:, :], T.c1[:, :], T.c2[:, :], A.add, ["c1", "c2"], ["c1"])
+    for k in range(4):
+        cp(T.corT[:, k::4], T.c1[:, 64 * k:64 * k + 64], ["c1"], ["corT%d" % k])
+
+    def invert(c0, c1):
+        op("v", lambda: V.tensor_copy(T.invrow[:, :].indirect(T.corT[:, c0:c1]), T.posv[:, 16 * c0:16 * c1]),
+           ["corT%d" % k for k in range(4)] + PV, ["invrow"])
+
+    invert(0, 128)
+
+    act(T.iab[:, :], T.ia[:, :], F.Abs, ["ia"], ["iab"])
+    act(T.P32[:, :], T.iab[:, :], F.Relu, ["iab"], ["P32"], bias=1.0, scale=-1.0)
+    act(T.Pb[:, :], T.iab[:, :], F.Relu, ["iab"], ["Pb"], bias=1.0, scale=-1.0)
+    act(T.P64[:, :], T.iab[:, :], F.Relu, ["iab"], ["P64"], bias=64.0, scale=-64.0)
+    act(T.w1[:, :], T.ib[:, :], F.Abs, ["ib"], ["w1"], bias=-7.5)
+    act(T.w2[:, :], T.w1[:, :], F.Relu, ["w1"], ["w2"], bias=8.0, scale=-1.0)
+    act(T.w1[:, :], T.w2[:, :], F.Sign, ["w2"], ["w1"])
+    act(T.W[:, 0::16], T.w1[:, :], F.Identity, ["w1"], ["W"], scale=1.0 / 64)
+    act(T.zero[:, :], T.posv[:, 0:512], F.Identity, PV, ["zero"], scale=0.0)
+    act(T.B[:, :], T.posv[:, 0:2048], F.Exp, PV, ["B"], scale=0.0)
+    act(T.rm[:, :], T.posv[:, 0:1536], F.Identity, PV, ["rm"], bias=1.0, scale=0.0)
+    act(T.rm[:, 0::6], T.posv[:, 0:256], F.Identity, PV, ["rm"], scale=0.0)
+    for h in range(2):
+        mm([(ps[h][:, :], win(T.P32, 0), T.zero[:, :], True, False)], ["P32", "zero"], ["ps%d" % h])
+
+    for k in ("q0", "q1", "q2", "el", "q3", "sp", "kp"):
+        send(k)
+    op("g", lambda: g.affine_select(T.B[:, :], T.B[:, :], [[-1, 16], [-16, 8], [0, 16]], A.is_equal, 0.0, 0, 1),
+       ["B"], ["B"])
+    unload("s", "q0", T.slabN, 0, 1024, ["slabN0"])
+    unload("s", "q1", T.slabN, 1024, 2048, ["slabN1"])
+    unload("s", "q2", T.slabN, 2048, 3072, ["slabN2"])
+    unload("s", "el", T.e16r, 0, 320, ["e16r"])
+    unload("s", "q3", T.slabN, 3072, 4096, ["slabN3"])
+    unload("s", "sp", T.stT, 0, 1024, ["stT"])
+    dma("s", "ownk", [(T.kpT[r0:r1, :], T.kap[r0:r1, :])], [], ["kpT_o"])
+    unload("s", "kp", T.kpT, 0, 1024, ["kpT"])
+    dma("s", "inf", [(T.lst2[:, 0:128], T.fm[:, :])]
+        + [(T.lst2[:, 128 * k + 128:128 * k + 256], t[:, 64:192]) for k, t in enumerate(state)], [], ["lst2"])
+    for k in range(4):
+        cp(T.l16s[:, k:256:4], T.corI[:, 64 * k:64 * k + 64], ["corI"], ["l16s%d" % k])
+    invert(128, 192)
+
+    def unpack(src, c, b0, b1, R):
+        w, k = 64 * (b1 - b0), "_%d" % b0
+        lo, hi = 64 * b0, 64 * b1
+        cp(T.xy[:, 2 * lo:2 * hi:2], src[:, c:c + w], R, ["xya" + k])
+        cp(T.xy[:, 2 * lo + 1:2 * hi:2], src[:, c + w:c + 2 * w], R, ["xyb" + k])
+        ts(T.En[:, lo:hi], src[:, c + 4 * w:c + 5 * w], 1.0 / 64, OFF, A.mult, A.add, R, ["En%d" % b for b in range(b0, b1)])
+        ts(T.q0i[:, 2 * lo:2 * hi], T.xy[:, 2 * lo:2 * hi], 4, 63, A.arith_shift_right, A.bitwise_and,
+           ["xya" + k, "xyb" + k], ["q0i"] + ["xy%d" % b for b in range(b0, b1)])
+        ts(T.v0a[:, lo:hi], T.q0i[:, 2 * lo + 1:2 * hi:2], 64.0, None, A.mult, None, ["q0i"], ["v0a"])
+        tt(T.v0b[:, lo:hi], T.v0a[:, lo:hi], T.q0i[:, 2 * lo:2 * hi:2], A.add, ["v0a", "q0i"], ["v0b"])
+        for b in range(b0, b1):
+            n = LG * b
+            cp(T.V16[:, 64 * n:64 * n + 64], T.v0b[:, 64 * b:64 * b + 64], ["v0b"], ["V%d" % n])
+            ts(T.E16[:, 64 * n:64 * n + 64], T.En[:, 64 * b:64 * b + 64], MAGIC, MAGIC, A.add, A.subtract,
+               ["En%d" % b], ["E%d" % n])
+        cp(T.dxy[:, 2 * lo:2 * hi], src[:, c + 2 * w:c + 4 * w], R, ["dxy%d" % b for b in range(b0, b1)])
+
+    def dxy(b, u):
+        c = 64 * u if b == 0 else 128 + 128 * u + 64 * (b - 1)
+        return T.dxy[:, c:c + 64]
+
+    unpack(T.e16r, 0, 0, 1, ["e16r", "e16r_o"])
+    invert(192, 256)
+    dma("s", "inv", [(T.invl[:, :], T.invrow[0::16, :])], ["invrow"], ["invl"])
+
+    def late_lists():
+        cp(T.l16s[:, 256:512], T.invl[:, :], ["invl"], ["l16s4"])
+        cp(T.l16s[:, 512:1280], T.lst2[:, :], ["lst2"], ["l16s5"])
+        LS = ["l16s%d" % k for k in range(6)]
+        dma("s", "s_ll", [(T.sg_ll[:], T.l16s[:, :]), (T.l16r[r0:r1, :], T.l16s[r0:r1, :])], LS, ["sg_ll", "l16r_o"])
+        send("ll")
+        unload("s", "ll", T.l16r, 0, 1280, ["l16r"])
+
+    LL = ["l16r", "l16r_o"]
+    SN = ["slabN0", "slabN1", "slabN2", "slabN3", "slabN_o"]
+    I = win(T.Pb, 0)
+
+    pend, pe_pend = [], []
+
+    def amt(n, c0, c1):
+        return T.amt[:, 1024 * (n % 2) + c0:1024 * (n % 2) + c1]
+
+    def akey(n, q):
+        return "amt%d_%d" % (n % 2, q)
+
+    def kp_gather(n, h):
+        c = 1024 * (n % 2) + 512 * h
+        act(T.kg[:, c:c + 512], T.kpT[:, :].indirect(T.E16[:, 64 * n + 32 * h:64 * n + 32 * h + 32]), F.Copy,
+            ["kpT", "kpT_o", "E%d" % n], ["kg%d" % (c // 512)])
+
+    def amt_psum(n, h):
+        mm([(ps[4 + h][:, :], I, amt(n, 512 * h, 512 * h + 512), True, True)],
+           ["Pb", akey(n, 2 * h), akey(n, 2 * h + 1)], ["ps%d" % (4 + h)])
+
+    def kp_half():
+        if pend:
+            n, h = pend.pop(0)
+            c = 1024 * (n % 2) + 512 * h
+            tt(T.pk[:, c:c + 512], T.kg[:, c:c + 512], ps[4 + h][:, :], A.mult,
+               ["kg%d" % (c // 512), "ps%d" % (4 + h)], ["pk%d" % (c // 256), "pk%d" % (c // 256 + 1)])
+            pe_pend.extend([(n, 2 * h), (n, 2 * h + 1)])
+
+    def kp_quarter(n, q):
+        c = 1024 * (n % 2) + 256 * q
+        tt(T.pk[:, c:c + 256], T.kpT[:, :].indirect(T.E16[:, 64 * n + 16 * q:64 * n + 16 * q + 16]),
+           amt(n, 256 * q, 256 * q + 256), A.mult, ["kpT", "kpT_o", "E%d" % n, akey(n, q)], ["pk%d" % (c // 256)])
+        pe_pend.append((n, q))
+
+    def kp_add(most=8):
+        while pe_pend and most:
+            most -= 1
+            n, q = pe_pend.pop(0)
+            c = 1024 * (n % 2) + 256 * q
+            last = n == NB * LG - 1 and q % 2 == 1
+            mm([(ps[q // 2][:, 256 * (q % 2):256 * (q % 2) + 256], win(T.P32, 16 * (n % LG)),
+                 T.pk[:, c:c + 256], False, last)], ["P32", "pk%d" % (c // 256)], ["ps%d" % (q // 2)])
+
+    def order_slab(k):
+        act(T.slabP[:, 1024 * k:1024 * k + 1024], T.slabN[:, :].indirect(T.l16r[:, 64 * k:64 * k + 64]), F.Identity,
+            SN + LL, ["slabP%d" % k], bias=-15.0)
+
+    def st_quarter(n, q):
+        tt(T.prod[:, 256 * q:256 * q + 256], T.stT[:, :].indirect(T.E16[:, 64 * n + 16 * q:64 * n + 16 * q + 16]),
+           amt(n, 256 * q, 256 * q + 256), A.mult, ["stT", "slabN_o", "E%d" % n, akey(n, q)], ["prod%d" % q])
+
+    def losses(j):
+        mm([(ps[2][:, 0:64], win(T.W, 16 * j - i), T.prod[:, i::16], i == 0, i == 15) for i in range(16)],
+           ["W"] + ["prod%d" % q for q in range(4)], ["ps2"])
+
+    D = ps[2][:, 0:64]
+
+    for b in range(NB):
+        En = T.En[:, 64 * b:64 * b + 64]
+        xy = T.xy[:, 128 * b:128 * b + 128]
+        ke, kx = "En%d" % b, "xy%d" % b
+        for j in range(LG):
+            n = LG * b + j
+            for q in range(4):
+                act(amt(n, 256 * q, 256 * q + 256),
+                    T.slabN[:, :].indirect(T.V16[:, 64 * n + 16 * q:64 * n + 16 * q + 16]), F.Copy,
+                    SN + ["V%d" % n], [akey(n, q)])
+            if n == NB * LG - 1:
+                break
+            kp_gather(n, 0)
+            kp_gather(n, 1)
+            kp_half()
+            if n == 1:
+                late_lists()
+            kp_add()
+            amt_psum(n, 0)
+            for q in range(4):
+                st_quarter(n, q)
+            losses(j)
+            kp_half()
+            amt_psum(n, 1)
+            pend.extend([(n, 0), (n, 1)])
+            if j == LG - 1:
+                break
+            mA, mS, pxy = ps[2][:, 64:128], ps[2][:, 128:192], ps[2][:, 256:384]
+            ts(mA, D, 800.0 / 64, 2.0, A.is_lt, A.mult, ["ps2"], ["mA"])
+            ts(T.mB[:, :], D, 1000.0 / 64, 1.0, A.is_lt, A.add, ["ps2"], ["mB"])
+            tt(mS, mA, T.mB[:, :], A.add, ["ps2", "mA", "mB"], ["mm"])
+            tt(ps[2][:, 256:384:2], mS, dxy(b, 0), A.mult, ["ps2", "mm", "dxy%d" % b], ["pxa"])
+            tt(ps[2][:, 257:384:2], mS, dxy(b, 1), A.mult, ["ps2", "mm", "dxy%d" % b], ["pxb"])
+            tt(xy, xy, pxy, A.add, ["ps2", kx, "pxa", "pxb"], [kx])
+            ts(T.qi[:, :], xy, 4, 63, A.arith_shift_right, A.bitwise_and, [kx], ["qi"])
+            cp(T.qf[:, :], T.qi[:, :], ["qi"], ["qf"])
+            tt(En, En, D, A.subtract, [ke, "ps2"], [ke])
+            kp_add(1)
+            o = -16 * (j + 1)
+            mm([(ps[3][:, 0:64], win(T.Pb, o), T.qf[:, 0::2], True, False),
+                (ps[3][:, 0:64], win(T.P64, o), T.qf[:, 1::2], False, True)], ["Pb", "P64", "qf"], ["ps3"])
+            mm([(ps[2][:, 448:512], win(T.P32, o), En, True, True)], ["P32", ke], ["ps2"])
+            kp_add()
+            cp(T.V16[:, 64 * n + 64:64 * n + 128], ps[3][:, 0:64], ["ps3"], ["V%d" % (n + 1)])
+            ts(T.E16[:, 64 * n + 64:64 * n + 128], ps[2][:, 448:512], MAGIC, MAGIC, A.add, A.subtract, ["ps2"],
+               ["E%d" % (n + 1)])
+            if j == LG - 2 and b < NB - 1:
+                if b == 0:
+                    ts(T.Fo[:, :], T.l16r[:, 512:640], 1.0 / 64, OFF, A.mult, A.add, LL, ["Fo"])
+                    ts(T.Fn[:, :], T.l16r[:, 512:640], -1.0 / 64, None, A.mult, None, LL, ["Fn"])
+                tt(T.G[:, :], En, T.Fo[:, 64 * b:64 * b + 64], A.subtract, [ke, "Fo"], ["G"])
+        if b == NB - 1:
+            break
+
+        sv, votes = T.sv[:, 64 * b:64 * b + 64], T["votes%d" % b]
+        u1, u2 = ps[2][:, 64:128], ps[2][:, 128:192]
+        tt(u1, T.G[:, :], D, A.subtract, ["G", "ps2"], ["mA"])
+        tt(u2, u1, T.Fn[:, 64 * b:64 * b + 64], A.max, ["ps2", "mA", "Fn"], ["mm"])
+        ts(sv, u2, -1.0 / 64, 1.0 / 64, A.max, A.min, ["ps2", "mm"], ["sv%d" % b])
+        deps("g", ["sv%d" % b], [])
+        slot = votes[:, 64 * me:64 * me + 64]
+        tr = [RemoteDMATransfer(dst_ids=[dst(q) for q in far], dma_engine_mask=bits(efar), remote_sem=T.sem["votes%d" % b],
+                                srcs=[sv], dsts=[slot for q in far])]
+        cnt["sent"] += len(efar)
+        for k, q in enumerate(near):
+            tr.append(RemoteDMATransfer(dst_ids=[dst(q)], dma_engine_mask=bits(near_mask(k)),
+                                        remote_sem=T.sem["votes%d" % b], src=sv, dst=slot))
+            cnt["sent"] += len(near_mask(k))
+        g.remote_dma_fused(tr, local_sem=T.sem.sent)
+        cnt["votes%d" % b] = arrivals(len)
+        wr["votes"] = [("votes%d" % b, cnt["votes%d" % b])]
+        tt(En, En, D, A.subtract, [ke, "ps2"], [ke])
+        if b == 0:
+            order_slab(0)
+            order_slab(1)
+        kp_add()
+        mm([(ps[3][:, 0:64], I, sv, k == 0, False) for k in range(3)], ["Pb", "sv%d" % b], ["ps3"])
+        while pend:
+            kp_half()
+            kp_add()
+        VS = ["V%d" % n for n in range(LG * b, LG * b + LG)]
+        cp(T.vI[:, :], T.V16[:, 384 * b:384 * b + 384], VS, ["vI"])
+        ts(T.kI[:, :], T.vI[:, :], 10, None, A.arith_shift_right, None, ["vI"], ["kI"])
+        for k in range(4):
+            ts(T.M[:, k::4], T.kI[:, :], float(k), None, A.is_equal, None, ["kI"], ["M%d" % k])
+        if b == 0:
+            unpack(T.l16r, 640, 1, NB, LL)
+        others = [q for q in range(N) if q != me]
+        mm([(ps[3][:, 0:64], I, votes[:, 64 * q:64 * q + 64], False, q == others[-1]) for q in others],
+           ["Pb", "votes"], ["ps3"])
+        act(T.t4[:, :], ps[3][:, 0:64], F.Sign, ["ps3"], ["t4"])
+        if b == 0:
+            order_slab(2)
+            order_slab(3)
+        for h in range(3):
+            mm([(ps[5 + h][:, 256 * u + k:256 * u + 256:4], win(T.Pb, -16 * (2 * h + u)), T.t4[:, :], True, True)
+                for u in range(2) for k in range(4)], ["Pb", "t4"], ["ps%d" % (5 + h)])
+        for j in range(LG):
+            tt(T.tm[:, j::6], T.M[:, 256 * j:256 * j + 256], ps[5 + j // 2][:, 256 * (j % 2):256 * (j % 2) + 256], A.mult,
+               ["M%d" % k for k in range(4)] + ["ps%d" % (5 + j // 2)], ["tm%d" % j])
+        op("v", lambda: V.tensor_tensor_scan(T.S[:, :], T.rm[:, :], T.tm[:, :], 0.0, A.mult, A.add),
+           ["rm"] + ["tm%d" % j for j in range(LG)], ["S"])
+        op("v", lambda: V.tensor_tensor_scan(T.mn[:, :], T.rm[:, :], T.S[:, :], 0.0, A.mult, A.min), ["rm", "S"], ["mn"])
+        op("v", lambda: V.tensor_tensor_scan(T.mx[:, :], T.rm[:, :], T.S[:, :], 0.0, A.mult, A.max), ["rm", "S"], ["mx"])
+        tt(T.U[:, :], T.S[:, 5::6], T.mx[:, 5::6], A.subtract, ["S", "mx"], ["U"])
+
+        def spread(c, bank, par, key, with_amounts):
+            items, R = [], ["B", "Pb", key]
+            for u in range(2):
+                i = 2 * c + u
+                o = ps[bank][:, 256 * u:256 * u + 256]
+                if with_amounts:
+                    items.append((o, I, T.slabP[:, i::16] if b == 0 else T.slabQ[:, 256 * i:256 * i + 256], True, False))
+                items.append((o, T.B[:, 128 * i:128 * i + 128], par, not with_amounts, True))
+            if with_amounts:
+                R += ["slabP%d" % k for k in range(4)] if b == 0 else ["slabQ%d" % c]
+            mm(items, R, ["ps%d" % bank])
+
+        def alive(c):
+            spread(c, 6 + c % 2, T.mn[:, 5::6], "mn", True)
+            act(T.rb[:, 512 * c:512 * c + 512], ps[6 + c % 2][:, :], F.Identity, ["ps%d" % (6 + c % 2)], ["rb%d" % c],
+                bias=225.0, scale=16.0)
+
+        def moved(c):
+            spread(c, 2 + c % 2, T.S[:, 5::6], "S", True)
+
+        def ceiling(c):
+            spread(c, 4 + c % 2, T.U[:, :], "U", False)
+
+        moved(0), alive(0), alive(1), alive(2), ceiling(0), ceiling(1), moved(1), alive(3)
+        for c in range(8):
+            h = c % 2
+            yb = T.yb[:, 512 * h:512 * h + 512]
+            tt(yb, T.rb[:, 512 * c:512 * c + 512], ps[4 + h][:, :], A.min, ["rb%d" % c, "ps%d" % (4 + h)], ["yb%d" % h])
+            tt(T.slabQ[:, 512 * c:512 * c + 512], yb, ps[2 + h][:, :], A.min, ["yb%d" % h, "ps%d" % (2 + h)],
+               ["slabQ%d" % c])
+            if c + 4 < 8:
+                alive(c + 4)
+            if c + 2 < 8:
+                ceiling(c + 2), moved(c + 2)
+        SQ = ["slabQ%d" % c for c in range(8)] + LL
+        act(T.slabN[:, 0:2048], T.slabQ[:, :].indirect(T.l16r[:, 256:384]), F.Relu, SQ, ["slabN0", "slabN1", "slabN_o"],
+            bias=15.0)
+        ts(T.slabN[:, 2048:4096], T.slabQ[:, :].indirect(T.l16r[:, 384:512]), 15.0, 0.0, A.add, A.max, SQ,
+           ["slabN2", "slabN3"])
+
+    n = NB * LG - 1
+    for h in range(2):
+        kp_half()
+        kp_add()
+        for q in (2 * h, 2 * h + 1):
+            kp_quarter(n, q)
+            kp_add()
+    for h in range(2):
+        k, yo = "y%d" % h, T.yo[:, 512 * h:512 * h + 512]
+        act(yo, ps[h][:, :], F.Exp, ["ps%d" % h], ["yo%d" % h], scale=-1.0 / 128)
+        dma("s", "s_" + k, [(T["sg_" + k][:], yo)], ["yo%d" % h], ["sg_" + k])
+        dma("s", "outs", [(T.yl[r0:r1, 512 * h:512 * h + 512], T.yo[r0:r1, 512 * h:512 * h + 512])], ["yo%d" % h], [])
+        send(k)
+    for q in range(4):
+        st_quarter(n, q)
+    losses(LG - 1)
+    tt(En, En, D, A.subtract, [ke, "ps2"], [ke])
+    ts(T.ea[:, :], T.En[:, :], -OFF, 0.0, A.add, A.max, ["En%d" % b for b in range(NB)], ["ea"])
+    ts(T.eb[:, :], T.ea[:, :], 64.0, None, A.mult, None, ["ea"], ["eb"])
+    ts(T.ec[:, :], T.eb[:, :], 1023, None, A.bitwise_and, None, ["eb"], ["ec"])
+    cp(T.eo[:, :], T.ec[:, :], ["ec"], ["eo"])
+    dma("a", "s_ee", [(T.sg_ee[:], T.eo[:, :])], ["eo"], ["sg_ee"])
+    dma("a", "outs", [(T.ye[r0:r1, :], T.eo[r0:r1, :])], ["eo"], [])
+    send("ee")
+    unload("s", "y0", T.yl, 0, 512, [], "outs")
+    unload("s", "y1", T.yl, 512, 1024, [], "outs")
+    unload("a", "ee", T.ye, 0, 192, [], "outs")
+    for s, v in cnt.items():
+        g.wait_ge(T.sem[s], v)

@@ -5,10 +5,16 @@ N = 8
 NB, LG = 3, 6
 MAGIC = 12582912.0
 OFF = -63.0 / 128.0
+XOFF = -15.0 / 32.0
+K64 = 12288.0
+LIFT = 64
+NA, NK, NP = 4, 6, 14
+OPT = {"split": 5, "fw": 128, "aw": 128, "p1": 16, "ab": "64646464", "xb": "23232323", "yb": "57575757", "sb": "56", "sp1": 0,
+       "G": 1.5, "H": 130, "PE": 0.5, "vote": 6000}
 
 PIECES = {"q0": ("bfloat16", 128), "q1": ("bfloat16", 128), "q2": ("bfloat16", 128), "q3": ("bfloat16", 128),
-          "sp": ("bfloat16", 128), "kp": ("bfloat16", 128), "el": ("uint16", 40), "ll": ("uint16", 160),
-          "y0": ("float32", 64), "y1": ("float32", 64), "ee": ("float32", 24)}
+          "sp": ("bfloat16", 128), "kp": ("bfloat16", 128), "el": ("uint16", 80), "s0": ("float32", 48),
+          "s1": ("float32", 224), "y0": ("float32", 64), "y1": ("float32", 64), "ee": ("float32", 24)}
 
 
 def _sb(n, d):
@@ -17,27 +23,28 @@ def _sb(n, d):
 
 SCRATCH = {
     "slabN": _sb(4096, "bfloat16"), "slabP": _sb(4096, "bfloat16"), "slabQ": _sb(4096, "bfloat16"),
-    "stT": _sb(1024, "bfloat16"), "kpT": _sb(1024, "bfloat16"), "amt": _sb(2048, "bfloat16"), "kg": _sb(2048, "bfloat16"),
-    "prod": _sb(1024, "bfloat16"), "pk": _sb(2048, "float32"),
-    "posv": _sb(4096, "float32"), "invrow": _sb(4096, "float32"), "invl": _sb(256, "float32"),
-    "lst": _sb(320, "int32"), "lst2": _sb(768, "int32"), "corI": _sb(256, "int32"),
-    "c1": _sb(256, "int32"), "c2": _sb(256, "int32"), "corT": _sb(256, "uint16"),
-    "e16s": _sb(320, "uint16"), "e16r": _sb(320, "uint16"), "l16s": _sb(1280, "uint16"), "l16r": _sb(1280, "uint16"),
-    "ia": _sb(256, "float32"), "iab": _sb(256, "float32"), "ib": _sb(16, "float32"), "ic": _sb(256, "float32"),
-    "w1": _sb(16, "float32"), "w2": _sb(16, "float32"),
-    "P32": _sb(256, "float32"), "P64": _sb(256, "bfloat16"), "Pb": _sb(256, "bfloat16"), "W": _sb(256, "bfloat16"),
-    "B": _sb(2048, "bfloat16"), "zero": _sb(512, "float32"), "rm": _sb(1536, "bfloat16"),
-    "xy": _sb(384, "int32"), "dxy": _sb(384, "float32"), "En": _sb(192, "float32"),
-    "q0i": _sb(384, "int32"), "v0a": _sb(192, "int32"), "v0b": _sb(192, "int32"),
-    "V16": _sb(1152, "uint16"), "E16": _sb(1152, "uint16"),
-    "mB": _sb(64, "float32"), "qi": _sb(128, "int32"), "qf": _sb(128, "bfloat16"),
-    "Fo": _sb(128, "float32"), "Fn": _sb(128, "float32"), "G": _sb(64, "float32"),
-    "sv": _sb(128, "bfloat16"), "votes0": _sb(512, "bfloat16"), "votes1": _sb(512, "bfloat16"),
-    "t4": _sb(64, "bfloat16"), "vI": _sb(384, "int32"), "kI": _sb(384, "int32"), "M": _sb(1536, "bfloat16"),
+    "stT": _sb(1024, "bfloat16"), "kpT": _sb(1024, "bfloat16"), "amt": _sb(1024 * NA, "bfloat16"),
+    "kg": _sb(512 * NK, "bfloat16"), "prod": _sb(1024, "bfloat16"), "pk": _sb(512 * NP, "float32"),
+    "pos0": _sb(512, "float32"), "posv": _sb(2048, "float32"), "invA": _sb(4096, "float32"),
+    "invB": _sb(4096, "float32"), "inv": _sb(256, "uint16"), "z32": _sb(256, "float32"),
+    "lst": _sb(1088, "int32"), "raw": _sb(1088, "float32"), "corI": _sb(256, "int32"),
+    "c1": _sb(256, "int32"), "c2": _sb(256, "int32"), "c3": _sb(256, "int32"), "corT": _sb(256, "uint16"),
+    "e16s": _sb(640, "uint16"), "e16r": _sb(640, "uint16"), "SS": _sb(2176, "float32"), "SR": _sb(2176, "float32"),
+    "ia": _sb(256, "float32"), "iab": _sb(256, "float32"), "ib": _sb(16, "float32"),
+    "ir": _sb(128, "float32"), "it": _sb(64, "float32"), "ita": _sb(128, "float32"), "w1": _sb(16, "float32"),
+    "w2": _sb(16, "float32"), "w3": _sb(16, "float32"), "r0": _sb(128, "float32"), "r1": _sb(128, "float32"),
+    "r2": _sb(128, "float32"),
+    "P32": _sb(256, "float32"), "Pb": _sb(256, "bfloat16"), "Pn": _sb(128, "bfloat16"), "W": _sb(256, "bfloat16"),
+    "Re": _sb(256, "float16"), "Rq": _sb(256, "float16"), "Rk": _sb(256, "bfloat16"), "Reb": _sb(256, "bfloat16"),
+    "Tx": _sb(272, "float32"), "B": _sb(2048, "bfloat16"), "rm": _sb(768, "bfloat16"), "zb": _sb(512, "bfloat16"),
+    "qa": _sb(384, "int32"), "qb": _sb(192, "int32"), "qc": _sb(192, "int32"), "qd": _sb(192, "int32"),
+    "VE": _sb(1920, "uint16"), "ri": _sb(128, "int32"), "Qh": _sb(256, "float16"), "Kk": _sb(256, "bfloat16"),
+    "G": _sb(128, "float32"), "sv": _sb(256, "bfloat16"), "votes0": _sb(1024, "bfloat16"),
+    "votes1": _sb(1024, "bfloat16"), "t4": _sb(64, "bfloat16"), "kf": _sb(384, "bfloat16"), "M": _sb(1536, "bfloat16"),
     "tm": _sb(1536, "bfloat16"), "S": _sb(1536, "bfloat16"), "mn": _sb(1536, "bfloat16"), "mx": _sb(1536, "bfloat16"),
-    "U": _sb(256, "bfloat16"), "rb": _sb(4096, "bfloat16"), "yb": _sb(1024, "bfloat16"),
-    "yo": _sb(1024, "float32"), "ea": _sb(192, "float32"), "eb": _sb(192, "int32"), "ec": _sb(192, "int32"),
-    "eo": _sb(192, "float32"),
+    "U": _sb(768, "bfloat16"), "ro": _sb(1024, "bfloat16"), "rb": _sb(4096, "bfloat16"), "yb": _sb(1024, "bfloat16"),
+    "yo": _sb(1024, "float32"), "ea": _sb(384, "float32"), "eb": _sb(384, "int32"), "ec": _sb(384, "int32"),
+    "ed": _sb(384, "float16"), "eo": _sb(192, "float32"),
 }
 for _k in range(8):
     SCRATCH["ps%d" % _k] = ("psum", [128, 512], "float32")
@@ -45,8 +52,20 @@ for _k, (_d, _n) in PIECES.items():
     SCRATCH["sg_" + _k] = ("dram", [8, 128, _n], _d)
     SCRATCH["ld_" + _k] = ("dram", [8, 128, _n], _d)
 
-SEMAPHORES = (["cv", "ca", "ct", "cg", "sent", "inl", "inc", "inf", "own", "ownk", "inv", "votes0", "votes1", "outs"]
+SEMAPHORES = (["cv", "ca", "ct", "cg", "sent", "inl", "zer", "inf", "own", "ownk", "inv", "votes0", "votes1", "outs"]
               + ["s_" + k for k in PIECES] + ["a_" + k for k in PIECES] + ["l_" + k for k in PIECES])
+
+
+def cST(b):
+    return 128 + 256 * b
+
+
+def cDX(b):
+    return 768 + 128 * b if b else 0
+
+
+def cF(b):
+    return 1152 + 128 * b
 
 
 def ways(T, topo, r):
@@ -62,6 +81,53 @@ def bits(es):
     return sum(1 << e for e in es)
 
 
+def arrange(jobs):
+    hand = OPT["H"]
+    wr, rd, last, before = {}, {}, {}, []
+    for n, (q, c, lag, R, W, banks, dma) in enumerate(jobs):
+        p = {}
+        for k in R:
+            p.update((m, True) for m in wr.get(k, []))
+        for k in W:
+            p.update((m, True) for m in wr.get(k, []) + rd.get(k, []))
+        for k in [("bank", k) for k in banks if k > 1] + ([("dma", q)] if dma else []):
+            if k in last:
+                p.setdefault(last[k], jobs[last[k]][0] != q)
+            last[k] = n
+        for k in W:
+            wr[k], rd[k] = [n], []
+        for k in R:
+            if k not in W:
+                rd.setdefault(k, []).append(n)
+        before.append({m: (jobs[m][2] + hand if w and not q == jobs[m][0] == "t" else 0) for m, w in p.items()})
+    tail, after = [0] * len(jobs), [[] for _ in jobs]
+    for n in range(len(jobs) - 1, -1, -1):
+        tail[n] += jobs[n][1]
+        for m, gap in before[n].items():
+            tail[m] = max(tail[m], gap + tail[n])
+            after[m].append(n)
+    left, ready = [len(p) for p in before], [0] * len(jobs)
+    free, end, order = {}, {}, []
+    open_ = [n for n in range(len(jobs)) if not left[n]]
+    while open_:
+        start = {n: max(ready[n], free.get(jobs[n][0], 0)) for n in open_}
+        n = min(open_, key=lambda m: (start[m], -tail[m], m))
+        q, t = jobs[n][0], start[n]
+        for m in open_:
+            if jobs[m][0] == q and start[m] < t + jobs[n][1] and tail[m] > tail[n]:
+                if max(start[m] + tail[m], start[m] + jobs[m][1] + tail[n]) < start[n] + jobs[n][1] + tail[m]:
+                    n = m
+        open_.remove(n)
+        order.append(n)
+        free[q] = end[n] = start[n] + jobs[n][1]
+        for m in after[n]:
+            ready[m] = max(ready[m], end[n] + before[m][n])
+            left[m] -= 1
+            if not left[m]:
+                open_.append(m)
+    return order
+
+
 def rank_program(g, core, T, topo):
     me = T.rank_of(core)
     if me is None:
@@ -69,6 +135,8 @@ def rank_program(g, core, T, topo):
     Q = {"v": g.vector, "a": g.scalar, "t": g.tensor, "g": g, "s": g.sync}
     own = {"v": "cv", "a": "ca", "t": "ct", "g": "cg"}
     cnt, know, clock, wr, rd = {}, {q: {} for q in Q}, {}, {}, {}
+    bank = [{} for _ in range(8)]
+    jobs, calls = [], []
 
     def merge(q, ev):
         k = know[q]
@@ -76,45 +144,56 @@ def rank_program(g, core, T, topo):
             if k.get(s, 0) < v:
                 k[s] = v
 
-    def need(q, evs):
-        for ev in sorted(set(evs), key=lambda e: -e[1]):
-            if know[q].get(ev[0], 0) < ev[1]:
-                Q[q].wait_ge(T.sem[ev[0]], ev[1])
-                merge(q, ev)
-
-    def deps(q, R, W):
+    def deps(q, R, W, banks=()):
         evs = []
         for k in R:
             evs += wr.get(k, [])
         for k in W:
             evs += wr.get(k, []) + rd.get(k, [])
+        for k in banks:
+            evs += [e for p, e in bank[k].items() if p != q]
         if q == "t":
             evs = [e for e in evs if e[0] != "ct"]
-        need(q, evs)
+        for ev in sorted(set(evs), key=lambda e: -e[1]):
+            if know[q].get(ev[0], 0) < ev[1]:
+                Q[q].wait_ge(T.sem[ev[0]], ev[1])
+                merge(q, ev)
 
-    def done(q, ev, R, W):
-        clock[ev] = dict(know[q])
+    def done(q, ev, R, W, banks=()):
+        if q != "g" or ev[0] == "cg":
+            clock[ev] = dict(know[q])
         for k in W:
             wr[k], rd[k] = [ev], []
         for k in R:
             if k not in W:
                 rd.setdefault(k, []).append(ev)
+        for k in banks:
+            bank[k][q] = ev
 
-    def op(q, fns, R, W):
-        deps(q, R, W)
-        for f in (fns if isinstance(fns, list) else [fns]):
-            ins = f()
-        s = own[q]
-        cnt[s] = cnt.get(s, 0) + 1
-        ins.then_inc(T.sem[s], 1)
-        done(q, (s, cnt[s]), R, W)
+    def job(q, call, cycles, lag, R, W, banks=(), dma=False):
+        jobs.append((q, cycles, lag, R, W, banks, dma))
 
-    def dma(q, sem, moves, R, W):
-        deps(q, R, W)
-        for o, i in moves:
-            Q[q].dma_start(o, i).then_inc(T.sem[sem], 16)
-            cnt[sem] = cnt.get(sem, 0) + 16
-        done(q, (sem, cnt[sem]), R, W)
+        def issue():
+            deps(q, R, W, banks)
+            done(q, call(), R, W, banks)
+        calls.append(issue)
+
+    def op(q, fns, cycles, R, W, banks=()):
+        def call():
+            for f in (fns if isinstance(fns, list) else [fns]):
+                ins = f()
+            cnt[own[q]] = cnt.get(own[q], 0) + 1
+            ins.then_inc(T.sem[own[q]], 1)
+            return own[q], cnt[own[q]]
+        job(q, call, cycles, 0, R, W, banks, q == "g")
+
+    def dma(q, sem, moves, R, W, lag=3000):
+        def call():
+            for o, i in moves:
+                Q[q].dma_start(o, i).then_inc(T.sem[sem], 16)
+                cnt[sem] = cnt.get(sem, 0) + 16
+            return sem, cnt[sem]
+        job(q, call, 100, lag, R, W, (), True)
 
     far, near, efar, enear = ways(T, topo, me)
     turn = [0]
@@ -135,22 +214,24 @@ def rank_program(g, core, T, topo):
         w = len(enear) // len(near)
         return enear[k * w:(k + 1) * w]
 
-    def send(k):
-        deps("g", ["sg_" + k], [])
+    def remote(tr, engines, sem, count, R, W, lag):
+        def call():
+            g.remote_dma_fused(tr, local_sem=T.sem.sent)
+            cnt["sent"] = cnt.get("sent", 0) + engines
+            cnt[sem] = count
+            return sem, count
+        job("g", call, 1200, lag, R, W, (), True)
+
+    def send(k, lag=5000):
         tr = []
         for q in far:
-            e = efar[turn[0] % len(efar)]
+            tr.append(RemoteDMATransfer(dst_ids=[dst(q)], dma_engine_mask=1 << efar[turn[0] % len(efar)],
+                                        remote_sem=T.sem["a_" + k], src=T["sg_" + k][q], dst=T["ld_" + k][me]))
             turn[0] += 1
-            tr.append(RemoteDMATransfer(dst_ids=[dst(q)], dma_engine_mask=1 << e, remote_sem=T.sem["a_" + k],
-                                        src=T["sg_" + k][q], dst=T["ld_" + k][me]))
-            cnt["sent"] = cnt.get("sent", 0) + 1
         for n, q in enumerate(near):
             tr.append(RemoteDMATransfer(dst_ids=[dst(q)], dma_engine_mask=bits(near_mask(n)), remote_sem=T.sem["a_" + k],
                                         src=T["sg_" + k][q], dst=T["ld_" + k][me]))
-            cnt["sent"] = cnt.get("sent", 0) + len(near_mask(n))
-        g.remote_dma_fused(tr, local_sem=T.sem.sent)
-        cnt["a_" + k] = arrivals(lambda ef: 1)
-        wr["ld_" + k] = [("a_" + k, cnt["a_" + k])]
+        remote(tr, len(far) + len(near) * len(near_mask(0)), "a_" + k, arrivals(lambda ef: 1), ["sg_" + k], ["ld_" + k], lag)
 
     def unload(q, k, buf, c0, c1, W, sem=None):
         mv = []
@@ -163,375 +244,411 @@ def rank_program(g, core, T, topo):
     r0, r1 = 16 * me, 16 * me + 16
     V, S_, PE = g.vector, g.scalar, g.tensor
 
-    def ts(out, in0, s1, s2, o0, o1, R, W):
+    def picks(n):
+        return 70 + int(OPT["G"] * n)
+
+    def ts(n, out, in0, s1, s2, o0, o1, R, W, banks=()):
         if o1 is None:
-            op("v", lambda: V.tensor_scalar(out, in0, s1, None, o0), R, W)
+            op("v", lambda: V.tensor_scalar(out, in0, s1, None, o0), n, R, W, banks)
         else:
-            op("v", lambda: V.tensor_scalar(out, in0, s1, s2, o0, o1), R, W)
+            op("v", lambda: V.tensor_scalar(out, in0, s1, s2, o0, o1), n, R, W, banks)
 
-    def tt(out, a, b, o, R, W):
-        op("v", lambda: V.tensor_tensor(out, a, b, o), R, W)
+    def tt(n, out, a, b, o, R, W, banks=()):
+        op("v", lambda: V.tensor_tensor(out, a, b, o), n, R, W, banks)
 
-    def cp(out, a, R, W):
-        op("v", lambda: V.tensor_copy(out, a), R, W)
+    def cp(n, out, a, R, W, banks=()):
+        op("v", lambda: V.tensor_copy(out, a), n, R, W, banks)
 
-    def act(out, a, f, R, W, bias=None, scale=None):
+    def fill(n, out, c, W):
+        op("v", lambda: V.memset(out, c), n, [], W)
+
+    def scan(n, out, d0, d1, o1, R, W):
+        op("v", lambda: V.tensor_tensor_scan(out, d0, d1, 0.0, A.mult, o1), n, R, W)
+
+    def act(n, out, a, f, R, W, banks=(), bias=None, scale=None):
         kw = {}
         if bias is not None:
             kw["bias"] = bias
         if scale is not None:
             kw["scale"] = scale
-        op("a", lambda: S_.activation(out, a, f, **kw), R, W)
+        op("a", lambda: S_.activation(out, a, f, **kw), n, R, W, banks)
 
-    def mm(items, R, W):
-        op("t", [(lambda it=it: PE.matmul(*it)) for it in items], R, W)
+    def mm(n, items, R, banks, W=()):
+        op("t", [(lambda it=it: PE.matmul(*it)) for it in items], int(OPT["PE"] * n), R, list(W), banks)
 
     def win(t, o):
         return t[:, o % 128:o % 128 + 128]
 
     ps = [T["ps%d" % k] for k in range(8)]
 
-    dma("a", "inc", [(T.corI[:, :], T.cor[:, :])], [], ["corI"])
-    state = (T.px, T.py, T.vx, T.vy, T.en)
-    first = [(T.lst[:, 64 * k:64 * k + 64], t[:, 0:64]) for k, t in enumerate(state)]
-    dma("a", "inl", first[:2], [], ["lst"])
-    wr["lst"] = []
-    dma("s", "inl", first[2:], [], ["lst"])
+    def stage(q, k, src):
+        dma(q, "s_" + k, [(T["sg_" + k][:], src)], [], ["sg_" + k])
 
-    def stage(k):
-        dma("a" if k == 0 else "s", "s_q%d" % k, [(T["sg_q%d" % k][:], T.slab[:, 1024 * k:1024 * k + 1024])], [],
-            ["sg_q%d" % k])
+    def hand(k, src, dstbuf, c0, c1, R):
+        dma("s", "s_" + k, [(T["sg_" + k][:], src[:, c0:c1]), (dstbuf[r0:r1, c0:c1], src[r0:r1, c0:c1])], R,
+            ["sg_" + k, k + "_o"])
 
-    for k in range(3):
-        stage(k)
-
-    op("g", lambda: g.iota(T.ic[:, :], [[1, 256]], 0, 0, allow_small_or_imprecise_dtypes=True), [], ["ic"])
-    op("g", lambda: g.iota(T.ia[:, :], [[0, 2], [-1, 128]], 0, 1, allow_small_or_imprecise_dtypes=True), [], ["ia"])
-    op("g", lambda: g.iota(T.ib[:, :], [[0, 2], [-16, 8]], 0, 1, allow_small_or_imprecise_dtypes=True), [], ["ib"])
-
-    op("v", lambda: V.memset(T.W[:, :], 0.0), [], ["W"])
-    for i in range(16):
-        if i < 7:
-            ts(T.posv[:, i::16], T.ic[:, :], float(256 * i), None, A.add, None, ["ic"], ["posv%d" % i])
-        else:
-            act(T.posv[:, i::16], T.ic[:, :], F.Identity, ["ic"], ["posv%d" % i], bias=float(256 * i))
-    PV = ["posv%d" % i for i in range(16)]
-    cp(T.e16s[:, :], T.lst[:, :], ["lst"], ["e16s"])
-    dma("s", "s_el", [(T.sg_el[:], T.e16s[:, :]), (T.e16r[r0:r1, :], T.e16s[r0:r1, :])], ["e16s"], ["sg_el", "e16r_o"])
-    stage(3)
-    dma("s", "s_sp", [(T.sg_sp[:], T.spow[:, :])], [], ["sg_sp"])
+    state = (T.px, T.py, T.en, T.vx, T.vy, T.fm)
+    loads = [(T.lst[:, 192 * k:192 * k + t.shape[1]], t[:, :]) for k, t in enumerate(state)]
+    dma("a", "inl", loads[:3] + [(T.corI[:, :], T.cor[:, :])], [], ["lst", "corI"], 5000)
+    stage("s", "q0", T.slab[:, 0:1024])
+    dma("s", "inf", loads[3:], [], ["lst2"], 5000)
+    for k in range(1, 4):
+        stage("s", "q%d" % k, T.slab[:, 1024 * k:1024 * k + 1024])
+    stage("s", "sp", T.spow[:, :])
     dma("s", "own", [(T.slabN[r0:r1, :], T.slab[r0:r1, :]), (T.stT[r0:r1, :], T.spow[r0:r1, :])], [], ["slabN_o"])
-    dma("s", "s_kp", [(T.sg_kp[:], T.kap[:, :])], [], ["sg_kp"])
 
-    ts(T.c1[:, :], T.corI[:, :], 15, None, A.bitwise_and, None, ["corI"], ["c1"])
-    ts(T.c2[:, :], T.corI[:, :], 4, None, A.arith_shift_right, None, ["corI"], ["c2"])
-    ts(T.c1[:, :], T.c1[:, :], 256.0, None, A.mult, None, ["c1"], ["c1"])
-    tt(T.c1[:, :], T.c1[:, :], T.c2[:, :], A.add, ["c1", "c2"], ["c1"])
-    for k in range(4):
-        cp(T.corT[:, k::4], T.c1[:, 64 * k:64 * k + 64], ["c1"], ["corT%d" % k])
+    def iota(n, out, pattern, base, cm, W):
+        op("g", lambda: g.iota(out, pattern, base, cm, allow_small_or_imprecise_dtypes=True), 160 + 2 * n, [], W)
 
-    def invert(c0, c1):
-        op("v", lambda: V.tensor_copy(T.invrow[:, :].indirect(T.corT[:, c0:c1]), T.posv[:, 16 * c0:16 * c1]),
-           ["corT%d" % k for k in range(4)] + PV, ["invrow"])
+    iota(64, T.it[:, :], [[-16, 8], [-1, 8]], 0, 1, ["it"])
+    iota(128, T.ir[:, :], [[-16, 8], [-1000, 2], [-2, 8]], 0, 1, ["ir"])
+    iota(16, T.ib[:, :], [[0, 2], [-16, 8]], 0, 1, ["ib"])
+    iota(256, T.ia[:, :], [[0, 2], [-1, 128]], 0, 1, ["ia"])
+    iota(512, T.pos0[:, :], [[1, 32], [128, 16]], LIFT, 0, ["pos0"])
 
-    invert(0, 128)
+    fill(256, T.z32[:, :], 0.0, ["z32"])
+    dma("a", "zer", [(T.invA[0::16, :], T.z32[:, :]), (T.invB[0::16, :], T.z32[:, :])], ["z32"], ["invA", "invB"])
+    fill(272, T.Tx[:, :], 0.0, ["Tx0", "Tx1"])
+    fill(128, T.W[:, :], 0.0, ["W0", "W1"])
+    fill(128, T.Kk[:, :], K64, ["K0", "K1"])
+    fill(256, T.zb[:, :], 0.0, ["zb"])
+    fill(1024, T.B[:, :], 1.0, ["B"])
+    fill(384, T.rm[:, :], 1.0, ["rm"])
+    fill(64, T.rm[:, 0::6], 0.0, ["rm"])
 
-    act(T.iab[:, :], T.ia[:, :], F.Abs, ["ia"], ["iab"])
-    act(T.P32[:, :], T.iab[:, :], F.Relu, ["iab"], ["P32"], bias=1.0, scale=-1.0)
-    act(T.Pb[:, :], T.iab[:, :], F.Relu, ["iab"], ["Pb"], bias=1.0, scale=-1.0)
-    act(T.P64[:, :], T.iab[:, :], F.Relu, ["iab"], ["P64"], bias=64.0, scale=-64.0)
-    act(T.w1[:, :], T.ib[:, :], F.Abs, ["ib"], ["w1"], bias=-7.5)
-    act(T.w2[:, :], T.w1[:, :], F.Relu, ["w1"], ["w2"], bias=8.0, scale=-1.0)
-    act(T.w1[:, :], T.w2[:, :], F.Sign, ["w2"], ["w1"])
-    act(T.W[:, 0::16], T.w1[:, :], F.Identity, ["w1"], ["W"], scale=1.0 / 64)
-    act(T.zero[:, :], T.posv[:, 0:512], F.Identity, PV, ["zero"], scale=0.0)
-    act(T.B[:, :], T.posv[:, 0:2048], F.Exp, PV, ["B"], scale=0.0)
-    act(T.rm[:, :], T.posv[:, 0:1536], F.Identity, PV, ["rm"], bias=1.0, scale=0.0)
-    act(T.rm[:, 0::6], T.posv[:, 0:256], F.Identity, PV, ["rm"], scale=0.0)
+    for hh in range(2):
+        ita = T.ita[:, 64 * hh:64 * hh + 64]
+        act(64, ita, T.it[:, :], F.Abs, ["it"], ["ita%d" % hh], bias=-8.0 * hh)
+        act(64, T.Tx[:, 136 * hh + 1:136 * hh + 129:2], ita, F.Relu, ["ita%d" % hh], ["Tx%d" % hh], bias=1.0, scale=-1.0)
+    act(64, T.w1[:, :], T.ib[:, :], F.Abs, ["ib"], ["w1"], bias=-7.5)
+    act(64, T.w2[:, :], T.w1[:, :], F.Relu, ["w1"], ["w2"], bias=8.0, scale=-1.0)
+    act(64, T.w3[:, :], T.w2[:, :], F.Sign, ["w2"], ["w3"])
+    act(256, T.iab[:, :], T.ia[:, :], F.Abs, ["ia"], ["iab"])
+    act(256, T.P32[:, :], T.iab[:, :], F.Relu, ["iab"], ["P32"], bias=1.0, scale=-1.0)
+    act(256, T.Pb[:, :], T.iab[:, :], F.Relu, ["iab"], ["Pb"], bias=1.0, scale=-1.0)
+    act(128, T.Pn[:, :], T.P32[:, 0:128], F.Identity, ["P32"], ["Pn"], scale=-1.0)
+    for c in range(2):
+        act(64, T.W[:, c::16], T.w3[:, :], F.Identity, ["w3"], ["W%d" % c], scale=-1.0 / 64)
+    I = win(T.Pb, 0)
     for h in range(2):
-        mm([(ps[h][:, :], win(T.P32, 0), T.zero[:, :], True, False)], ["P32", "zero"], ["ps%d" % h])
+        mm(512, [(ps[h][:, :], I, T.zb[:, :], True, False)], ["Pb", "zb"], [h], ["L%d" % h])
+    ts(128, T.r0[:, :], T.ir[:, :], 0.0, None, A.is_equal, None, ["ir"], ["r0"])
+    ts(128, T.r2[:, :], T.ir[:, :], 1.0, 64.0, A.is_equal, A.mult, ["ir"], ["r2"])
+    tt(256, T.r1[:, :], T.r2[:, :], T.r0[:, :], A.add, ["r0", "r2"], ["r1"])
+    for u in range(2):
+        cp(128, T.Re[:, 128 * u:128 * u + 128], T.r0[:, :], ["r0"], ["Re%d" % u])
+        cp(128, T.Rq[:, 128 * u:128 * u + 128], T.r1[:, :], ["r1"], ["Rq%d" % u])
+        act(128, T.Reb[:, 128 * u:128 * u + 128], T.r0[:, :], F.Identity, ["r0"], ["Reb%d" % u])
+        act(128, T.Rk[:, 128 * u:128 * u + 128], T.r1[:, :], F.Identity, ["r1"], ["Rk%d" % u], scale=-1.0)
+    RR = ["Re0", "Re1", "Rq0", "Rq1", "Rk0", "Rk1", "Reb0", "Reb1"]
 
-    for k in ("q0", "q1", "q2", "el", "q3", "sp", "kp"):
+    ts(384, T.qa[:, :], T.lst[:, 0:384], 4, None, A.arith_shift_right, None, ["lst"], ["qa"])
+    ts(192, T.qc[:, :], T.lst[:, 384:576], 6, None, A.arith_shift_right, None, ["lst"], ["qc"])
+    ts(192, T.qb[:, :], T.qa[:, 192:384], 64.0, None, A.mult, None, ["qa"], ["qb"])
+    cp(192, T.e16s[:, 192:384], T.qc[:, :], ["qc"], ["e16se"])
+    tt(384, T.qd[:, :], T.qb[:, :], T.qa[:, 0:192], A.add, ["qa", "qb"], ["qd"])
+    for k in range(4):
+        cp(64, T.e16s[:, 384 + k:640:4], T.corI[:, 64 * k:64 * k + 64], ["corI"], ["e16s%d" % k])
+    cp(192, T.e16s[:, 0:192], T.qd[:, :], ["qd"], ["e16sv"])
+    hand("el", T.e16s, T.e16r, 0, 640, ["e16sv", "e16se"] + ["e16s%d" % k for k in range(4)])
+    cp(1088, T.raw[:, :], T.lst[:, :], ["lst", "lst2"], ["raw"])
+
+    def settle(b, k):
+        x, y, E, dx, dy = [T.raw[:, 192 * u + 64 * b:192 * u + 64 * b + 64] for u in range(5)]
+        items = []
+        for hh in range(2):
+            t0, t1 = T.Tx[:, 136 * hh + 1:136 * hh + 129], T.Tx[:, 136 * hh:136 * hh + 128]
+            pX, pE, pD = ps[k][:, 2 * hh:256:4], ps[k][:, 2 * hh + 1:256:4], ps[k][:, 256 + hh:384:2]
+            items += [(pX, t0, x, True, False), (pX, t1, y, False, True), (pE, t0, E, True, True),
+                      (pD, t0, dx, True, False), (pD, t1, dy, False, True)]
+            if b < NB - 1:
+                items.append((ps[k][:, 384 + hh:512:2], t0, T.raw[:, 960 + 64 * b:1024 + 64 * b], True, True))
+        mm(3072, items, ["Tx0", "Tx1", "raw"], [k])
+        c = cST(b)
+        act(128, T.SS[:, c:c + 256:2], ps[k][:, 0:256:2], F.Identity, [], ["SSx%d" % b], [k], bias=XOFF, scale=1.0 / 16)
+        act(128, T.SS[:, c + 1:c + 256:2], ps[k][:, 1:256:2], F.Identity, [], ["SSe%d" % b], [k], bias=OFF, scale=1.0 / 64)
+        act(128, T.SS[:, cDX(b):cDX(b) + 128], ps[k][:, 256:384], F.Identity, [], ["SSd%d" % b], [k], scale=1.0 / 8)
+        if b < NB - 1:
+            act(128, T.SS[:, cF(b):cF(b) + 128], ps[k][:, 384:512], F.Identity, [], ["SSf%d" % b], [k], bias=OFF,
+                scale=1.0 / 64)
+            act(128, T.SS[:, cF(b) + 256:cF(b) + 384], ps[k][:, 384:512], F.Sign, [], ["SSl%d" % b], [k], scale=-1.0)
+
+    settle(0, 2)
+    hand("s0", T.SS, T.SR, 0, 384, ["SSx0", "SSe0", "SSd0"])
+    stage("s", "kp", T.kap[:, :])
+    settle(1, 6)
+    settle(2, 7)
+
+    ts(256, T.c1[:, :], T.corI[:, :], 15, None, A.bitwise_and, None, ["corI"], ["c1"])
+    ts(256, T.c2[:, :], T.corI[:, :], 4, None, A.arith_shift_right, None, ["corI"], ["c2"])
+    ts(256, T.c3[:, :], T.c1[:, :], 256.0, None, A.mult, None, ["c1"], ["c3"])
+    tt(512, T.c1[:, :], T.c3[:, :], T.c2[:, :], A.add, ["c3", "c2"], ["c1"])
+    for k in range(4):
+        cp(64, T.corT[:, k::4], T.c1[:, 64 * k:64 * k + 64], ["c1"], ["corT%d" % k])
+    CT = ["corT%d" % k for k in range(4)]
+    base = [float(2048 * (u // 4) + 32 * (u % 4)) for u in range(8)]
+    split = OPT["split"]
+    for u in range(split, 8):
+        act(512, T.posv[:, 512 * (u - split):512 * (u - split) + 512], T.pos0[:, :], F.Identity, ["pos0"], ["posv%d" % u],
+            bias=base[u])
+    for u in range(split):
+        ts(2000, T.invA[:, :].indirect(T.corT[:, 32 * u:32 * u + 32]), T.pos0[:, :], 1.0, base[u], A.mult, A.add,
+           CT + ["pos0"], ["invA"])
+    act(1600 + 2000 * (8 - split), T.invB[:, :].indirect(T.corT[:, 32 * split:256]), T.posv[:, 0:512 * (8 - split)], F.Silu,
+        CT + ["posv%d" % u for u in range(split, 8)], ["invB", "w2"])
+    act(1800, T.w2[:, :], T.w3[:, :], F.Exp, ["w3"], ["w2", "warm"])
+
+    for k in ("q0", "q1", "q2", "q3", "el", "sp", "s0", "kp"):
         send(k)
-    op("g", lambda: g.affine_select(T.B[:, :], T.B[:, :], [[-1, 16], [-16, 8], [0, 16]], A.is_equal, 0.0, 0, 1),
+    op("g", lambda: g.affine_select(T.B[:, :], T.B[:, :], [[-1, 16], [-16, 8], [0, 16]], A.is_equal, 0.0, 0, 1), 4300,
        ["B"], ["B"])
-    unload("s", "q0", T.slabN, 0, 1024, ["slabN0"])
-    unload("s", "q1", T.slabN, 1024, 2048, ["slabN1"])
-    unload("s", "q2", T.slabN, 2048, 3072, ["slabN2"])
-    unload("s", "el", T.e16r, 0, 320, ["e16r"])
-    unload("s", "q3", T.slabN, 3072, 4096, ["slabN3"])
+    for k in range(4):
+        unload("s", "q%d" % k, T.slabN, 1024 * k, 1024 * k + 1024, ["slabN%d" % k])
+    unload("s", "el", T.e16r, 0, 640, ["el"])
     unload("s", "sp", T.stT, 0, 1024, ["stT"])
+    unload("s", "s0", T.SR, 0, 384, ["s0"])
     dma("s", "ownk", [(T.kpT[r0:r1, :], T.kap[r0:r1, :])], [], ["kpT_o"])
     unload("s", "kp", T.kpT, 0, 1024, ["kpT"])
-    dma("s", "inf", [(T.lst2[:, 0:128], T.fm[:, :])]
-        + [(T.lst2[:, 128 * k + 128:128 * k + 256], t[:, 64:192]) for k, t in enumerate(state)], [], ["lst2"])
-    for k in range(4):
-        cp(T.l16s[:, k:256:4], T.corI[:, 64 * k:64 * k + 64], ["corI"], ["l16s%d" % k])
-    invert(128, 192)
-
-    def unpack(src, c, b0, b1, R):
-        w, k = 64 * (b1 - b0), "_%d" % b0
-        lo, hi = 64 * b0, 64 * b1
-        cp(T.xy[:, 2 * lo:2 * hi:2], src[:, c:c + w], R, ["xya" + k])
-        cp(T.xy[:, 2 * lo + 1:2 * hi:2], src[:, c + w:c + 2 * w], R, ["xyb" + k])
-        ts(T.En[:, lo:hi], src[:, c + 4 * w:c + 5 * w], 1.0 / 64, OFF, A.mult, A.add, R, ["En%d" % b for b in range(b0, b1)])
-        ts(T.q0i[:, 2 * lo:2 * hi], T.xy[:, 2 * lo:2 * hi], 4, 63, A.arith_shift_right, A.bitwise_and,
-           ["xya" + k, "xyb" + k], ["q0i"] + ["xy%d" % b for b in range(b0, b1)])
-        ts(T.v0a[:, lo:hi], T.q0i[:, 2 * lo + 1:2 * hi:2], 64.0, None, A.mult, None, ["q0i"], ["v0a"])
-        tt(T.v0b[:, lo:hi], T.v0a[:, lo:hi], T.q0i[:, 2 * lo:2 * hi:2], A.add, ["v0a", "q0i"], ["v0b"])
-        for b in range(b0, b1):
-            n = LG * b
-            cp(T.V16[:, 64 * n:64 * n + 64], T.v0b[:, 64 * b:64 * b + 64], ["v0b"], ["V%d" % n])
-            ts(T.E16[:, 64 * n:64 * n + 64], T.En[:, 64 * b:64 * b + 64], MAGIC, MAGIC, A.add, A.subtract,
-               ["En%d" % b], ["E%d" % n])
-        cp(T.dxy[:, 2 * lo:2 * hi], src[:, c + 2 * w:c + 4 * w], R, ["dxy%d" % b for b in range(b0, b1)])
-
-    def dxy(b, u):
-        c = 64 * u if b == 0 else 128 + 128 * u + 64 * (b - 1)
-        return T.dxy[:, c:c + 64]
-
-    unpack(T.e16r, 0, 0, 1, ["e16r", "e16r_o"])
-    invert(192, 256)
-    dma("s", "inv", [(T.invl[:, :], T.invrow[0::16, :])], ["invrow"], ["invl"])
-
-    def late_lists():
-        cp(T.l16s[:, 256:512], T.invl[:, :], ["invl"], ["l16s4"])
-        cp(T.l16s[:, 512:1280], T.lst2[:, :], ["lst2"], ["l16s5"])
-        LS = ["l16s%d" % k for k in range(6)]
-        dma("s", "s_ll", [(T.sg_ll[:], T.l16s[:, :]), (T.l16r[r0:r1, :], T.l16s[r0:r1, :])], LS, ["sg_ll", "l16r_o"])
-        send("ll")
-        unload("s", "ll", T.l16r, 0, 1280, ["l16r"])
-
-    LL = ["l16r", "l16r_o"]
+    dma("s", "inv", [(T.SS[:, 1664:1920], T.invA[0::16, :]), (T.SS[:, 1920:2176], T.invB[0::16, :])], ["invA", "invB"],
+        ["invl"])
+    hand("s1", T.SS, T.SR, 384, 2176, ["invl", "SSf0", "SSl0", "SSf1", "SSl1"]
+         + ["SS%s%d" % (u, b) for u in "xed" for b in (1, 2)])
+    send("s1")
+    unload("s", "s1", T.SR, 384, 2176, ["s1"])
+    EL, S0, S1 = ["el", "el_o", "warm"], ["s0", "s0_o"], ["s1", "s1_o"]
     SN = ["slabN0", "slabN1", "slabN2", "slabN3", "slabN_o"]
-    I = win(T.Pb, 0)
 
-    pend, pe_pend = [], []
+    def lists(n, h, u, c0=0, c1=32):
+        b, j = divmod(n, LG)
+        if j:
+            c = 128 * (5 * b + j - 1) + 64 * h + 32 * u
+            return T.VE[:, c + c0:c + c1], ["VE%d_%d" % (n, h)]
+        c = 192 * u + 64 * b + 32 * h
+        return T.e16r[:, c + c0:c + c1], EL
+
+    def st(b, h, u=None):
+        c = cST(b) + 128 * h
+        return T.SR[:, c:c + 128] if u is None else T.SR[:, c + u:c + 128:2]
 
     def amt(n, c0, c1):
-        return T.amt[:, 1024 * (n % 2) + c0:1024 * (n % 2) + c1]
+        return T.amt[:, 1024 * (n % NA) + c0:1024 * (n % NA) + c1]
 
-    def akey(n, q):
-        return "amt%d_%d" % (n % 2, q)
+    def akey(n, h, u):
+        return "amt%d_%d%d" % (n % NA, h, u)
 
-    def kp_gather(n, h):
-        c = 1024 * (n % 2) + 512 * h
-        act(T.kg[:, c:c + 512], T.kpT[:, :].indirect(T.E16[:, 64 * n + 32 * h:64 * n + 32 * h + 32]), F.Copy,
-            ["kpT", "kpT_o", "E%d" % n], ["kg%d" % (c // 512)])
+    cuts = ((0, OPT["p1"]), (OPT["p1"], 32))
 
-    def amt_psum(n, h):
-        mm([(ps[4 + h][:, :], I, amt(n, 512 * h, 512 * h + 512), True, True)],
-           ["Pb", akey(n, 2 * h), akey(n, 2 * h + 1)], ["ps%d" % (4 + h)])
+    def amounts(n, h):
+        for u, (c0, c1) in enumerate(cuts):
+            o, R = lists(n, h, 0, c0, c1)
+            act(picks(16 * (c1 - c0)), amt(n, 512 * h + 16 * c0, 512 * h + 16 * c1), T.slabN[:, :].indirect(o), F.Copy,
+                SN + R, [akey(n, h, u)])
 
-    def kp_half():
-        if pend:
-            n, h = pend.pop(0)
-            c = 1024 * (n % 2) + 512 * h
-            tt(T.pk[:, c:c + 512], T.kg[:, c:c + 512], ps[4 + h][:, :], A.mult,
-               ["kg%d" % (c // 512), "ps%d" % (4 + h)], ["pk%d" % (c // 256), "pk%d" % (c // 256 + 1)])
-            pe_pend.extend([(n, 2 * h), (n, 2 * h + 1)])
+    def losses(n, h):
+        for u, (c0, c1) in enumerate(cuts):
+            o, R = lists(n, h, 1, c0, c1)
+            c0, c1 = 512 * h + 16 * c0, 512 * h + 16 * c1
+            tt(picks(c1 - c0), T.prod[:, c0:c1], T.stT[:, :].indirect(o), amt(n, c0, c1), A.mult,
+               ["stT", "slabN_o", akey(n, h, u)] + R, ["prod%d%d" % (h, u)])
+        mm(512, [(ps[2 + h][:, 1:128:2], win(T.W, 16 * (n % LG) - 2 * i), T.prod[:, 512 * h + i:512 * h + 512:8], i == 0,
+                  i == 7) for i in range(8)], ["W0", "W1", "prod%d0" % h, "prod%d1" % h], [2 + h])
 
-    def kp_quarter(n, q):
-        c = 1024 * (n % 2) + 256 * q
-        tt(T.pk[:, c:c + 256], T.kpT[:, :].indirect(T.E16[:, 64 * n + 16 * q:64 * n + 16 * q + 16]),
-           amt(n, 256 * q, 256 * q + 256), A.mult, ["kpT", "kpT_o", "E%d" % n, akey(n, q)], ["pk%d" % (c // 256)])
-        pe_pend.append((n, q))
+    def move(n, h):
+        b, j = divmod(n, LG)
+        p, k, ks, SB = ps[2 + h], [2 + h], "ST%d%d" % (b, h), S1 if b else S0
+        ri, c = T.ri[:, 64 * h:64 * h + 64], 128 * h
+        ts(64, ri, p[:, 1:128:2], 0.32, 5.4975, A.mult, A.add, [], ["ri%d" % h], k)
+        ts(64, p[:, 128:192], ri, 0.5, 2.0, A.max, A.min, ["ri%d" % h], ["m%d" % h], k)
+        tt(64, p[:, 0:128:2], p[:, 128:192], T.SR[:, cDX(b) + 64 * h:cDX(b) + 64 * h + 64], A.mult, ["m%d" % h] + SB,
+           ["P%d" % h], k)
+        tt(128, st(b, h), st(b, h), p[:, 0:128], A.add, [ks, "P%d" % h] + SB, [ks], k)
+        ts(64, T.Kk[:, c:c + 64], st(b, h, 0), K64 - 31.5, None, A.add, None, [ks], ["K%d" % h])
+        ts(128, T.Qh[:, c:c + 128], st(b, h), MAGIC, MAGIC, A.add, A.subtract, [ks], ["Q%d" % h])
+        o = [-16 * (j + 1) - 8 * hh for hh in range(2)]
+        mm(384, [(p[:, 192:256], win(T.Rk, o[hh]), T.Kk[:, c + hh:c + 128:2], hh == 0, False) for hh in range(2)]
+           + [(p[:, 192:224], win(T.Rq, o[hh]), T.Qh[:, c + 2 * hh:c + 128:4], False, False) for hh in range(2)]
+           + [(p[:, 224:256], win(T.Re, o[hh]), T.Qh[:, c + 2 * hh + 1:c + 128:4], False, hh == 1) for hh in range(2)],
+           RR + ["Q%d" % h, "K%d" % h], k)
+        c = 128 * (5 * b + j) + 64 * h
+        ts(64, T.VE[:, c:c + 64], p[:, 192:256], 65 * K64, None, A.add, None, [], ["VE%d_%d" % (n + 1, h)], k)
 
-    def kp_add(most=8):
-        while pe_pend and most:
-            most -= 1
-            n, q = pe_pend.pop(0)
-            c = 1024 * (n % 2) + 256 * q
-            last = n == NB * LG - 1 and q % 2 == 1
-            mm([(ps[q // 2][:, 256 * (q % 2):256 * (q % 2) + 256], win(T.P32, 16 * (n % LG)),
-                 T.pk[:, c:c + 256], False, last)], ["P32", "pk%d" % (c // 256)], ["ps%d" % (q // 2)])
+    def spend(b, h):
+        ks = "ST%d%d" % (b, h)
+        tt(64, st(b, h, 1), st(b, h, 1), ps[2 + h][:, 1:128:2], A.add, [ks], [ks], [2 + h])
 
-    def order_slab(k):
-        act(T.slabP[:, 1024 * k:1024 * k + 1024], T.slabN[:, :].indirect(T.l16r[:, 64 * k:64 * k + 64]), F.Identity,
-            SN + LL, ["slabP%d" % k], bias=-15.0)
+    def vote(b, h):
+        p, k, G = ps[2 + h], [2 + h], T.G[:, 64 * h:64 * h + 64]
+        tt(128, G, st(b, h, 1), T.SR[:, cF(b) + 64 * h:cF(b) + 64 * h + 64], A.subtract, ["ST%d%d" % (b, h)] + S1,
+           ["G%d" % h])
+        tt(64, p[:, 128:192], G, p[:, 1:128:2], A.add, ["G%d" % h], ["m%d" % h], k)
+        ts(64, p[:, 192:256], p[:, 128:192], 64.0, 1.0, A.mult, A.min, ["m%d" % h], ["P%d" % h], k)
+        tt(64, T.sv[:, 128 * b + 64 * h:128 * b + 64 * h + 64], T.SR[:, cF(b) + 256 + 64 * h:cF(b) + 320 + 64 * h],
+           p[:, 192:256], A.max, ["P%d" % h] + S1, ["sv%d%d" % (b, h)], k)
+        spend(b, h)
 
-    def st_quarter(n, q):
-        tt(T.prod[:, 256 * q:256 * q + 256], T.stT[:, :].indirect(T.E16[:, 64 * n + 16 * q:64 * n + 16 * q + 16]),
-           amt(n, 256 * q, 256 * q + 256), A.mult, ["stT", "slabN_o", "E%d" % n, akey(n, q)], ["prod%d" % q])
+    def add_terms(n, h, c0, c1, close=False):
+        p = 512 * ((2 * n + h) % NP)
+        key = ["L%d" % h]
+        mm(4 * (c1 - c0), [(ps[h][:, c0:c1], win(T.P32, 16 * (n % LG)), T.pk[:, p + c0:p + c1], False, close)],
+           ["P32"] + ["pk%d" % ((p + c) // 128) for c in range(c0, c1, 128)] + ([] if close else key), [h],
+           key if close else [])
 
-    def losses(j):
-        mm([(ps[2][:, 0:64], win(T.W, 16 * j - i), T.prod[:, i::16], i == 0, i == 15) for i in range(16)],
-           ["W"] + ["prod%d" % q for q in range(4)], ["ps2"])
+    def terms(n, h):
+        s, p, k = (2 * n + h) % NK, 512 * ((2 * n + h) % NP), 4 + h
+        o, R = lists(n, h, 1)
+        act(picks(512), T.kg[:, 512 * s:512 * s + 512], T.kpT[:, :].indirect(o), F.Copy, ["kpT", "kpT_o"] + R, ["kg%d" % s])
+        mm(512, [(ps[k][:, :], I, amt(n, 512 * h, 512 * h + 512), True, True)], ["Pb", akey(n, h, 0), akey(n, h, 1)], [k])
+        w = OPT["fw"]
+        for c in range(0, 512, w):
+            tt(w, T.pk[:, p + c:p + c + w], T.kg[:, 512 * s + c:512 * s + c + w], ps[k][:, c:c + w], A.mult, ["kg%d" % s],
+               ["pk%d" % ((p + e) // 128) for e in range(c, c + w, 128)], [k])
+        for c in range(0, 512, OPT["aw"]):
+            add_terms(n, h, c, c + OPT["aw"])
 
-    D = ps[2][:, 0:64]
+    for k in range(8):
+        act(picks(512), T.slabP[:, 512 * k:512 * k + 512], T.slabN[:, :].indirect(T.e16r[:, 384 + 32 * k:416 + 32 * k]),
+            F.Identity, SN + EL, ["slabP%d" % k], bias=-15.0)
+    tt(512, T.SS[:, 0:256], T.SR[:, 1664:1920], T.SR[:, 1920:2176], A.add, S1, ["SSx0", "SSe0", "SSd0"])
+    ts(256, T.inv[:, :], T.SS[:, 0:256], MAGIC - LIFT, MAGIC, A.add, A.subtract, ["SSx0"], ["inv"])
 
     for b in range(NB):
-        En = T.En[:, 64 * b:64 * b + 64]
-        xy = T.xy[:, 128 * b:128 * b + 128]
-        ke, kx = "En%d" % b, "xy%d" % b
         for j in range(LG):
             n = LG * b + j
-            for q in range(4):
-                act(amt(n, 256 * q, 256 * q + 256),
-                    T.slabN[:, :].indirect(T.V16[:, 64 * n + 16 * q:64 * n + 16 * q + 16]), F.Copy,
-                    SN + ["V%d" % n], [akey(n, q)])
-            if n == NB * LG - 1:
-                break
-            kp_gather(n, 0)
-            kp_gather(n, 1)
-            kp_half()
-            if n == 1:
-                late_lists()
-            kp_add()
-            amt_psum(n, 0)
-            for q in range(4):
-                st_quarter(n, q)
-            losses(j)
-            kp_half()
-            amt_psum(n, 1)
-            pend.extend([(n, 0), (n, 1)])
-            if j == LG - 1:
-                break
-            mA, mS, pxy = ps[2][:, 64:128], ps[2][:, 128:192], ps[2][:, 256:384]
-            ts(mA, D, 800.0 / 64, 2.0, A.is_lt, A.mult, ["ps2"], ["mA"])
-            ts(T.mB[:, :], D, 1000.0 / 64, 1.0, A.is_lt, A.add, ["ps2"], ["mB"])
-            tt(mS, mA, T.mB[:, :], A.add, ["ps2", "mA", "mB"], ["mm"])
-            tt(ps[2][:, 256:384:2], mS, dxy(b, 0), A.mult, ["ps2", "mm", "dxy%d" % b], ["pxa"])
-            tt(ps[2][:, 257:384:2], mS, dxy(b, 1), A.mult, ["ps2", "mm", "dxy%d" % b], ["pxb"])
-            tt(xy, xy, pxy, A.add, ["ps2", kx, "pxa", "pxb"], [kx])
-            ts(T.qi[:, :], xy, 4, 63, A.arith_shift_right, A.bitwise_and, [kx], ["qi"])
-            cp(T.qf[:, :], T.qi[:, :], ["qi"], ["qf"])
-            tt(En, En, D, A.subtract, [ke, "ps2"], [ke])
-            kp_add(1)
-            o = -16 * (j + 1)
-            mm([(ps[3][:, 0:64], win(T.Pb, o), T.qf[:, 0::2], True, False),
-                (ps[3][:, 0:64], win(T.P64, o), T.qf[:, 1::2], False, True)], ["Pb", "P64", "qf"], ["ps3"])
-            mm([(ps[2][:, 448:512], win(T.P32, o), En, True, True)], ["P32", ke], ["ps2"])
-            kp_add()
-            cp(T.V16[:, 64 * n + 64:64 * n + 128], ps[3][:, 0:64], ["ps3"], ["V%d" % (n + 1)])
-            ts(T.E16[:, 64 * n + 64:64 * n + 128], ps[2][:, 448:512], MAGIC, MAGIC, A.add, A.subtract, ["ps2"],
-               ["E%d" % (n + 1)])
-            if j == LG - 2 and b < NB - 1:
-                if b == 0:
-                    ts(T.Fo[:, :], T.l16r[:, 512:640], 1.0 / 64, OFF, A.mult, A.add, LL, ["Fo"])
-                    ts(T.Fn[:, :], T.l16r[:, 512:640], -1.0 / 64, None, A.mult, None, LL, ["Fn"])
-                tt(T.G[:, :], En, T.Fo[:, 64 * b:64 * b + 64], A.subtract, [ke, "Fo"], ["G"])
+            for h in range(2):
+                amounts(n, h)
+                if n == NB * LG - 1:
+                    continue
+                losses(n, h)
+                if j < LG - 1:
+                    move(n, h)
+                else:
+                    vote(b, h)
+                terms(n, h)
         if b == NB - 1:
             break
 
-        sv, votes = T.sv[:, 64 * b:64 * b + 64], T["votes%d" % b]
-        u1, u2 = ps[2][:, 64:128], ps[2][:, 128:192]
-        tt(u1, T.G[:, :], D, A.subtract, ["G", "ps2"], ["mA"])
-        tt(u2, u1, T.Fn[:, 64 * b:64 * b + 64], A.max, ["ps2", "mA", "Fn"], ["mm"])
-        ts(sv, u2, -1.0 / 64, 1.0 / 64, A.max, A.min, ["ps2", "mm"], ["sv%d" % b])
-        deps("g", ["sv%d" % b], [])
-        slot = votes[:, 64 * me:64 * me + 64]
+        sv, votes = T.sv[:, 128 * b:128 * b + 128], T["votes%d" % b]
+        SV = ["sv%d0" % b, "sv%d1" % b]
+        place = votes[:, 128 * me:128 * me + 128]
         tr = [RemoteDMATransfer(dst_ids=[dst(q) for q in far], dma_engine_mask=bits(efar), remote_sem=T.sem["votes%d" % b],
-                                srcs=[sv], dsts=[slot for q in far])]
-        cnt["sent"] += len(efar)
+                                srcs=[sv], dsts=[place for q in far])]
         for k, q in enumerate(near):
             tr.append(RemoteDMATransfer(dst_ids=[dst(q)], dma_engine_mask=bits(near_mask(k)),
-                                        remote_sem=T.sem["votes%d" % b], src=sv, dst=slot))
-            cnt["sent"] += len(near_mask(k))
-        g.remote_dma_fused(tr, local_sem=T.sem.sent)
-        cnt["votes%d" % b] = arrivals(len)
-        wr["votes"] = [("votes%d" % b, cnt["votes%d" % b])]
-        tt(En, En, D, A.subtract, [ke, "ps2"], [ke])
-        if b == 0:
-            order_slab(0)
-            order_slab(1)
-        kp_add()
-        mm([(ps[3][:, 0:64], I, sv, k == 0, False) for k in range(3)], ["Pb", "sv%d" % b], ["ps3"])
-        while pend:
-            kp_half()
-            kp_add()
-        VS = ["V%d" % n for n in range(LG * b, LG * b + LG)]
-        cp(T.vI[:, :], T.V16[:, 384 * b:384 * b + 384], VS, ["vI"])
-        ts(T.kI[:, :], T.vI[:, :], 10, None, A.arith_shift_right, None, ["vI"], ["kI"])
-        for k in range(4):
-            ts(T.M[:, k::4], T.kI[:, :], float(k), None, A.is_equal, None, ["kI"], ["M%d" % k])
-        if b == 0:
-            unpack(T.l16r, 640, 1, NB, LL)
-        others = [q for q in range(N) if q != me]
-        mm([(ps[3][:, 0:64], I, votes[:, 64 * q:64 * q + 64], False, q == others[-1]) for q in others],
-           ["Pb", "votes"], ["ps3"])
-        act(T.t4[:, :], ps[3][:, 0:64], F.Sign, ["ps3"], ["t4"])
-        if b == 0:
-            order_slab(2)
-            order_slab(3)
-        for h in range(3):
-            mm([(ps[5 + h][:, 256 * u + k:256 * u + 256:4], win(T.Pb, -16 * (2 * h + u)), T.t4[:, :], True, True)
-                for u in range(2) for k in range(4)], ["Pb", "t4"], ["ps%d" % (5 + h)])
+                                        remote_sem=T.sem["votes%d" % b], src=sv, dst=place))
+        remote(tr, len(efar) + len(near) * len(near_mask(0)), "votes%d" % b, arrivals(len), SV, ["votes"], OPT["vote"])
+        mm(384, [(ps[7][:, 0:64], win(T.Reb, -8 * hh), T.sv[:, 128 * b + hh:128 * b + 128:2], k + hh == 0, False)
+                 for k in range(3) for hh in range(2)], RR + SV, [7])
         for j in range(LG):
-            tt(T.tm[:, j::6], T.M[:, 256 * j:256 * j + 256], ps[5 + j // 2][:, 256 * (j % 2):256 * (j % 2) + 256], A.mult,
-               ["M%d" % k for k in range(4)] + ["ps%d" % (5 + j // 2)], ["tm%d" % j])
-        op("v", lambda: V.tensor_tensor_scan(T.S[:, :], T.rm[:, :], T.tm[:, :], 0.0, A.mult, A.add),
-           ["rm"] + ["tm%d" % j for j in range(LG)], ["S"])
-        op("v", lambda: V.tensor_tensor_scan(T.mn[:, :], T.rm[:, :], T.S[:, :], 0.0, A.mult, A.min), ["rm", "S"], ["mn"])
-        op("v", lambda: V.tensor_tensor_scan(T.mx[:, :], T.rm[:, :], T.S[:, :], 0.0, A.mult, A.max), ["rm", "S"], ["mx"])
-        tt(T.U[:, :], T.S[:, 5::6], T.mx[:, 5::6], A.subtract, ["S", "mx"], ["U"])
+            for h in range(2):
+                o, R = lists(LG * b + j, h, 0)
+                ts(64, T.kf[:, 64 * j + 32 * h:64 * j + 32 * h + 32], o, 1.0 / 1024, 192 - 0.4995, A.mult, A.add, R,
+                   ["kf%d%d" % (j, h)])
+        for k in range(4):
+            ts(192, T.M[:, k::4], T.kf[:, :], 192.0 + k, None, A.is_equal, None,
+               ["kf%d%d" % (j, h) for j in range(LG) for h in range(2)], ["M%d" % k])
+        others = [q for q in range(N) if q != me]
+        mm(896, [(ps[7][:, 0:64], win(T.Reb, -8 * hh), votes[:, 128 * q + hh:128 * q + 128:2], False,
+                  q == others[-1] and hh == 1) for q in others for hh in range(2)], RR + ["votes"], [7])
+        ts(64, T.t4[:, :], ps[7][:, 0:64], -1.0, 1.0, A.max, A.min, [], ["t4"], [7])
+        tb = (2, 3, 7)
+        for u in range(3):
+            mm(512, [(ps[tb[u]][:, 256 * e + k:256 * e + 256:4], win(T.Pb, -16 * (2 * u + e)), T.t4[:, :], True, True)
+                     for e in range(2) for k in range(4)], ["Pb", "t4"], [tb[u]])
 
-        def spread(c, bank, par, key, with_amounts):
-            items, R = [], ["B", "Pb", key]
-            for u in range(2):
-                i = 2 * c + u
-                o = ps[bank][:, 256 * u:256 * u + 256]
-                if with_amounts:
-                    items.append((o, I, T.slabP[:, i::16] if b == 0 else T.slabQ[:, 256 * i:256 * i + 256], True, False))
-                items.append((o, T.B[:, 128 * i:128 * i + 128], par, not with_amounts, True))
-            if with_amounts:
-                R += ["slabP%d" % k for k in range(4)] if b == 0 else ["slabQ%d" % c]
-            mm(items, R, ["ps%d" % bank])
+        for h in range(2):
+            c0, c1 = 768 * h, 768 * h + 768
+            for j in range(LG):
+                c = 256 * (j % 2) + 128 * h
+                tt(128, T.tm[:, c0 + j:c1:6], T.M[:, 256 * j + 128 * h:256 * j + 128 * h + 128], ps[tb[j // 2]][:, c:c + 128],
+                   A.mult, ["M%d" % k for k in range(4)], ["tm%d%d" % (j, h)], [tb[j // 2]])
+            scan(384, T.S[:, c0:c1], T.rm[:, :], T.tm[:, c0:c1], A.add, ["rm"] + ["tm%d%d" % (j, h) for j in range(LG)],
+                 ["S%d" % h])
+            scan(384, T.mn[:, c0:c1], T.rm[:, :], T.S[:, c0:c1], A.min, ["rm", "S%d" % h], ["mn%d" % h])
+            scan(384, T.mx[:, c0:c1], T.rm[:, :], T.S[:, c0:c1], A.max, ["rm", "S%d" % h], ["mx%d" % h])
+
+        ab, xb, yk, sb = [[int(c) for c in OPT[w]] for w in ("ab", "xb", "yb", "sb")]
+
+        def total(t, h):
+            return t[:, 768 * h + 5:768 * h + 768:6]
+
+        def span(h):
+            k = sb[h]
+            mm(256, [(ps[k][:, 0:128], I, total(T.S, h), True, False), (ps[k][:, 0:128], T.Pn[:, :], total(T.mx, h), False, True)],
+               ["Pb", "Pn", "S%d" % h, "mx%d" % h], [k])
+            act(128, T.U[:, 128 * h:128 * h + 128], ps[k][:, 0:128], F.Identity, [], ["U%d" % h], [k])
+
+        def spread(c, k, par, key, amounts_too):
+            h, items, R = c // 4, [], ["B", "Pb", key]
+            for u in range(4):
+                i, o = 4 * (c % 4) + u, ps[k][:, 128 * u:128 * u + 128]
+                if amounts_too:
+                    items.append((o, I, T.slabQ[:, 512 * c + 128 * u:512 * c + 128 * u + 128] if b
+                                  else T.slabP[:, 2048 * h + i:2048 * h + 2048:16], True, False))
+                items.append((o, T.B[:, 128 * i:128 * i + 128], par, not amounts_too, True))
+            if amounts_too:
+                R += ["slabQ%d" % c] if b else ["slabP%d" % (4 * h + u) for u in range(4)]
+            mm(128 * len(items), items, R, [k])
 
         def alive(c):
-            spread(c, 6 + c % 2, T.mn[:, 5::6], "mn", True)
-            act(T.rb[:, 512 * c:512 * c + 512], ps[6 + c % 2][:, :], F.Identity, ["ps%d" % (6 + c % 2)], ["rb%d" % c],
-                bias=225.0, scale=16.0)
+            spread(c, ab[c], total(T.mn, c // 4), "mn%d" % (c // 4), True)
+            act(512, T.rb[:, 512 * c:512 * c + 512], ps[ab[c]][:, :], F.Identity, [], ["rb%d" % c], [ab[c]], bias=225.0,
+                scale=16.0)
 
-        def moved(c):
-            spread(c, 2 + c % 2, T.S[:, 5::6], "S", True)
-
-        def ceiling(c):
-            spread(c, 4 + c % 2, T.U[:, :], "U", False)
-
-        moved(0), alive(0), alive(1), alive(2), ceiling(0), ceiling(1), moved(1), alive(3)
+        span(0)
+        for c in range(4):
+            alive(c)
         for c in range(8):
-            h = c % 2
-            yb = T.yb[:, 512 * h:512 * h + 512]
-            tt(yb, T.rb[:, 512 * c:512 * c + 512], ps[4 + h][:, :], A.min, ["rb%d" % c, "ps%d" % (4 + h)], ["yb%d" % h])
-            tt(T.slabQ[:, 512 * c:512 * c + 512], yb, ps[2 + h][:, :], A.min, ["yb%d" % h, "ps%d" % (2 + h)],
-               ["slabQ%d" % c])
+            h, low = c // 4, T.yb[:, 512 * (c % 2):512 * (c % 2) + 512]
+            if c == OPT["sp1"]:
+                span(1)
+            spread(c, yk[c], T.U[:, 128 * h:128 * h + 128], "U%d" % h, False)
+            spread(c, xb[c], total(T.S, h), "S%d" % h, True)
+            tt(512, low, T.rb[:, 512 * c:512 * c + 512], ps[yk[c]][:, :], A.min, ["rb%d" % c], ["yb%d" % (c % 2)], [yk[c]])
+            tt(512, T.slabQ[:, 512 * c:512 * c + 512], low, ps[xb[c]][:, :], A.min, ["yb%d" % (c % 2)], ["slabQ%d" % c],
+               [xb[c]])
             if c + 4 < 8:
                 alive(c + 4)
-            if c + 2 < 8:
-                ceiling(c + 2), moved(c + 2)
-        SQ = ["slabQ%d" % c for c in range(8)] + LL
-        act(T.slabN[:, 0:2048], T.slabQ[:, :].indirect(T.l16r[:, 256:384]), F.Relu, SQ, ["slabN0", "slabN1", "slabN_o"],
-            bias=15.0)
-        ts(T.slabN[:, 2048:4096], T.slabQ[:, :].indirect(T.l16r[:, 384:512]), 15.0, 0.0, A.add, A.max, SQ,
+        SQ = ["slabQ%d" % c for c in range(8)] + ["inv"]
+        act(picks(2048), T.slabN[:, 0:2048], T.slabQ[:, :].indirect(T.inv[:, 0:128]), F.Relu, SQ,
+            ["slabN0", "slabN1", "slabN_o"], bias=15.0)
+        ts(picks(2048), T.slabN[:, 2048:4096], T.slabQ[:, :].indirect(T.inv[:, 128:256]), 15.0, 0.0, A.add, A.max, SQ,
            ["slabN2", "slabN3"])
 
-    n = NB * LG - 1
+    n, b = NB * LG - 1, NB - 1
     for h in range(2):
-        kp_half()
-        kp_add()
-        for q in (2 * h, 2 * h + 1):
-            kp_quarter(n, q)
-            kp_add()
-    for h in range(2):
+        p = 512 * ((2 * n + h) % NP)
+        for u, (c0, c1) in enumerate(cuts):
+            o, R = lists(n, h, 1, c0, c1)
+            c0, c1 = 16 * c0, 16 * c1
+            tt(picks(c1 - c0), T.pk[:, p + c0:p + c1], T.kpT[:, :].indirect(o), amt(n, 512 * h + c0, 512 * h + c1), A.mult,
+               ["kpT", "kpT_o", akey(n, h, u)] + R, ["pk%d" % ((p + c) // 128) for c in range(c0, c1, 128)])
+            add_terms(n, h, c0, c1, u == 1)
         k, yo = "y%d" % h, T.yo[:, 512 * h:512 * h + 512]
-        act(yo, ps[h][:, :], F.Exp, ["ps%d" % h], ["yo%d" % h], scale=-1.0 / 128)
+        act(512, yo, ps[h][:, :], F.Exp, ["L%d" % h], ["yo%d" % h], [h], scale=-1.0 / 128)
         dma("s", "s_" + k, [(T["sg_" + k][:], yo)], ["yo%d" % h], ["sg_" + k])
         dma("s", "outs", [(T.yl[r0:r1, 512 * h:512 * h + 512], T.yo[r0:r1, 512 * h:512 * h + 512])], ["yo%d" % h], [])
         send(k)
-    for q in range(4):
-        st_quarter(n, q)
-    losses(LG - 1)
-    tt(En, En, D, A.subtract, [ke, "ps2"], [ke])
-    ts(T.ea[:, :], T.En[:, :], -OFF, 0.0, A.add, A.max, ["En%d" % b for b in range(NB)], ["ea"])
-    ts(T.eb[:, :], T.ea[:, :], 64.0, None, A.mult, None, ["ea"], ["eb"])
-    ts(T.ec[:, :], T.eb[:, :], 1023, None, A.bitwise_and, None, ["eb"], ["ec"])
-    cp(T.eo[:, :], T.ec[:, :], ["ec"], ["eo"])
+    for h in range(2):
+        losses(n, h)
+        spend(b, h)
+    for c0, c1, k in ((0, 256, 0), (256, 384, 1)):
+        R = ["ST%d%d" % (u, h) for u in range(c0 // 128, c1 // 128) for h in range(2)]
+        w = c1 - c0
+        ts(w, T.ea[:, c0:c1], T.SR[:, cST(0) + 2 * c0 + 1:cST(0) + 2 * c1:2], -OFF, 0.0, A.add, A.max, R, ["ea%d" % k])
+        ts(w, T.eb[:, c0:c1], T.ea[:, c0:c1], 64.0, None, A.mult, None, ["ea%d" % k], ["eb%d" % k])
+        ts(w, T.ec[:, c0:c1], T.eb[:, c0:c1], 1023, None, A.bitwise_and, None, ["eb%d" % k], ["ec%d" % k])
+        cp(w, T.ed[:, c0:c1], T.ec[:, c0:c1], ["ec%d" % k], ["ed%d" % k])
+    mm(384, [(ps[6][:, 0:192], win(T.Re, -8 * hh), T.ed[:, hh::2], hh == 0, hh == 1) for hh in range(2)],
+       RR + ["ed0", "ed1"], [6])
+    cp(192, T.eo[:, :], ps[6][:, 0:192], [], ["eo"], [6])
     dma("a", "s_ee", [(T.sg_ee[:], T.eo[:, :])], ["eo"], ["sg_ee"])
     dma("a", "outs", [(T.ye[r0:r1, :], T.eo[r0:r1, :])], ["eo"], [])
     send("ee")
     unload("s", "y0", T.yl, 0, 512, [], "outs")
     unload("s", "y1", T.yl, 512, 1024, [], "outs")
     unload("a", "ee", T.ye, 0, 192, [], "outs")
+    for n in arrange(jobs):
+        calls[n]()
     for s, v in cnt.items():
         g.wait_ge(T.sem[s], v)

@@ -7,14 +7,27 @@ MAGIC = 12582912.0
 OFF = -63.0 / 128.0
 XOFF = -15.0 / 32.0
 K64 = 12288.0
+K16 = 3072.0
 LIFT = 64
-NA, NK, NP = 4, 6, 14
-OPT = {"split": 5, "fw": 128, "aw": 128, "p1": 16, "ab": "64646464", "xb": "23232323", "yb": "57575757", "sb": "56", "sp1": 0,
-       "G": 1.5, "H": 130, "PE": 0.5, "vote": 6000}
+NA, NK, NP = 7, 8, 17
+OPT = {
+    "split": 4,
+    "hand": (140, 200, 240),
+    "lead": (800, 400, 800),
+    "lazy": (0, 1, 9, 10),
+    "fix": 45, "kw": (512, 512, 512), "fw": (512, 512, 512), "aw": 256, "whole": ((), (), ()), "tw": 256, "ka": (0, 0, 0),
+    "rounds": 7000, "true": 80, "step": 150, "afix": 200, "plat": 55,
+    "sv": (), "aftr": (0, 1, 2, 3, 4, 5, 9, 10, 11), "ov": 0, "kn": 2, "pa": 1, "fused": (4, 5, 11), "lq": "aasa", "l2": 9000, "sc": 4.0, "ends": (-0.3, 0.45),
+    "G": 1.56, "PE": 0.56, "vote": 7000, "pre": 2, "l1": 4500, "lkp": 8000, "ly": 6000, "le": 4000,
+    "ab": "64646464", "xb": "23232323", "yb": "57575757", "sb": "56",
+    "sq": ">q0 >q1 >q2 >q3 +el >el >sp -q0 +s0 -q1 >s0 ones -q2 -q3 -el -sp -s0 +kp >kp -kp +s1 >s1 +iv +iw >iv >iw -s1 -iv -iw",
+}
 
+ORDER = []
 PIECES = {"q0": ("bfloat16", 128), "q1": ("bfloat16", 128), "q2": ("bfloat16", 128), "q3": ("bfloat16", 128),
-          "sp": ("bfloat16", 128), "kp": ("bfloat16", 128), "el": ("uint16", 80), "s0": ("float32", 48),
-          "s1": ("float32", 224), "y0": ("float32", 64), "y1": ("float32", 64), "ee": ("float32", 24)}
+          "sp": ("bfloat16", 128), "kp": ("bfloat16", 128), "el": ("uint16", 80), "s0": ("float32", 64),
+          "s1": ("float32", 112), "iv": ("float32", 32), "iw": ("float32", 32), "y0": ("float32", 64),
+          "y1": ("float32", 64), "ee": ("float32", 8), "ef": ("float32", 16)}
 
 
 def _sb(n, d):
@@ -25,26 +38,26 @@ SCRATCH = {
     "slabN": _sb(4096, "bfloat16"), "slabP": _sb(4096, "bfloat16"), "slabQ": _sb(4096, "bfloat16"),
     "stT": _sb(1024, "bfloat16"), "kpT": _sb(1024, "bfloat16"), "amt": _sb(1024 * NA, "bfloat16"),
     "kg": _sb(512 * NK, "bfloat16"), "prod": _sb(1024, "bfloat16"), "pk": _sb(512 * NP, "float32"),
-    "pos0": _sb(512, "float32"), "posv": _sb(2048, "float32"), "invA": _sb(4096, "float32"),
-    "invB": _sb(4096, "float32"), "inv": _sb(256, "uint16"), "z32": _sb(256, "float32"),
+    "pos0": _sb(512, "float32"), "posv": _sb(2048, "float32"), "invA": _sb(8192, "float32"),
+    "inv": _sb(256, "uint16"), "ivr": _sb(768, "float32"),
     "lst": _sb(1088, "int32"), "raw": _sb(1088, "float32"), "corI": _sb(256, "int32"),
     "c1": _sb(256, "int32"), "c2": _sb(256, "int32"), "c3": _sb(256, "int32"), "corT": _sb(256, "uint16"),
-    "e16s": _sb(640, "uint16"), "e16r": _sb(640, "uint16"), "SS": _sb(2176, "float32"), "SR": _sb(2176, "float32"),
+    "e16s": _sb(640, "uint16"), "e16r": _sb(640, "uint16"), "SS": _sb(1664, "float32"), "SR": _sb(3712, "float32"),
     "ia": _sb(256, "float32"), "iab": _sb(256, "float32"), "ib": _sb(16, "float32"),
     "ir": _sb(128, "float32"), "it": _sb(64, "float32"), "ita": _sb(128, "float32"), "w1": _sb(16, "float32"),
     "w2": _sb(16, "float32"), "w3": _sb(16, "float32"), "r0": _sb(128, "float32"), "r1": _sb(128, "float32"),
     "r2": _sb(128, "float32"),
     "P32": _sb(256, "float32"), "Pb": _sb(256, "bfloat16"), "Pn": _sb(128, "bfloat16"), "W": _sb(256, "bfloat16"),
     "Re": _sb(256, "float16"), "Rq": _sb(256, "float16"), "Rk": _sb(256, "bfloat16"), "Reb": _sb(256, "bfloat16"),
-    "Tx": _sb(272, "float32"), "B": _sb(2048, "bfloat16"), "rm": _sb(768, "bfloat16"), "zb": _sb(512, "bfloat16"),
+    "Re32": _sb(256, "float32"), "Tx": _sb(272, "float32"), "B": _sb(2048, "bfloat16"), "rm": _sb(768, "bfloat16"),
+    "zb": _sb(512, "bfloat16"), "z32": _sb(512, "float32"),
     "qa": _sb(384, "int32"), "qb": _sb(192, "int32"), "qc": _sb(192, "int32"), "qd": _sb(192, "int32"),
     "VE": _sb(1920, "uint16"), "ri": _sb(128, "int32"), "Qh": _sb(256, "float16"), "Kk": _sb(256, "bfloat16"),
     "G": _sb(128, "float32"), "sv": _sb(256, "bfloat16"), "votes0": _sb(1024, "bfloat16"),
-    "votes1": _sb(1024, "bfloat16"), "t4": _sb(64, "bfloat16"), "kf": _sb(384, "bfloat16"), "M": _sb(1536, "bfloat16"),
+    "votes1": _sb(1024, "bfloat16"), "t4": _sb(64, "bfloat16"), "kf": _sb(768, "bfloat16"), "M": _sb(1536, "bfloat16"),
     "tm": _sb(1536, "bfloat16"), "S": _sb(1536, "bfloat16"), "mn": _sb(1536, "bfloat16"), "mx": _sb(1536, "bfloat16"),
-    "U": _sb(768, "bfloat16"), "ro": _sb(1024, "bfloat16"), "rb": _sb(4096, "bfloat16"), "yb": _sb(1024, "bfloat16"),
-    "yo": _sb(1024, "float32"), "ea": _sb(384, "float32"), "eb": _sb(384, "int32"), "ec": _sb(384, "int32"),
-    "ed": _sb(384, "float16"), "eo": _sb(192, "float32"),
+    "U": _sb(256, "bfloat16"), "rb": _sb(4096, "bfloat16"), "yb": _sb(1024, "bfloat16"),
+    "yo": _sb(1024, "float32"), "ea": _sb(384, "float32"), "ed": _sb(384, "bfloat16"), "eo": _sb(192, "float32"),
 }
 for _k in range(8):
     SCRATCH["ps%d" % _k] = ("psum", [128, 512], "float32")
@@ -52,20 +65,35 @@ for _k, (_d, _n) in PIECES.items():
     SCRATCH["sg_" + _k] = ("dram", [8, 128, _n], _d)
     SCRATCH["ld_" + _k] = ("dram", [8, 128, _n], _d)
 
-SEMAPHORES = (["cv", "ca", "ct", "cg", "sent", "inl", "zer", "inf", "own", "ownk", "inv", "votes0", "votes1", "outs"]
+SEMAPHORES = (["cv", "ca", "ct", "cg", "sent", "inc", "zer", "inl", "inf", "own", "votes0", "votes1", "outs"]
               + ["s_" + k for k in PIECES] + ["a_" + k for k in PIECES] + ["l_" + k for k in PIECES])
 
 
-def cST(b):
-    return 128 + 256 * b
+def sX(b):
+    return 512 + 256 * b if b else 0
 
 
-def cDX(b):
-    return 768 + 128 * b if b else 0
+def cE(b):
+    return 384 + 128 * b
 
 
 def cF(b):
-    return 1152 + 128 * b
+    return 1280 if b else 256
+
+
+def cL(b):
+    return 1408 + 128 * b
+
+
+def cX(b):
+    return 1664 + 256 * b
+
+
+def cDX(b):
+    return 2432 + 256 * b
+
+
+cZ = 3200
 
 
 def ways(T, topo, r):
@@ -82,49 +110,82 @@ def bits(es):
 
 
 def arrange(jobs):
-    hand = OPT["H"]
     wr, rd, last, before = {}, {}, {}, []
-    for n, (q, c, lag, R, W, banks, dma) in enumerate(jobs):
-        p = {}
-        for k in R:
+    for n, J in enumerate(jobs):
+        q, p = J["q"], {}
+        for k in J["R"]:
             p.update((m, True) for m in wr.get(k, []))
-        for k in W:
+        for k in J["W"]:
             p.update((m, True) for m in wr.get(k, []) + rd.get(k, []))
-        for k in [("bank", k) for k in banks if k > 1] + ([("dma", q)] if dma else []):
+        for k in [("bank", k) for k in J["banks"] if k > 1] + ([("dma", q)] if J["dma"] else []):
             if k in last:
-                p.setdefault(last[k], jobs[last[k]][0] != q)
+                p.setdefault(last[k], jobs[last[k]]["q"] != q)
             last[k] = n
-        for k in W:
+        for k in J["W"]:
             wr[k], rd[k] = [n], []
-        for k in R:
-            if k not in W:
+        for k in J["R"]:
+            if k not in J["W"]:
                 rd.setdefault(k, []).append(n)
-        before.append({m: (jobs[m][2] + hand if w and not q == jobs[m][0] == "t" else 0) for m, w in p.items()})
-    tail, after = [0] * len(jobs), [[] for _ in jobs]
-    for n in range(len(jobs) - 1, -1, -1):
-        tail[n] += jobs[n][1]
-        for m, gap in before[n].items():
-            tail[m] = max(tail[m], gap + tail[n])
-            after[m].append(n)
-    left, ready = [len(p) for p in before], [0] * len(jobs)
-    free, end, order = {}, {}, []
-    open_ = [n for n in range(len(jobs)) if not left[n]]
-    while open_:
-        start = {n: max(ready[n], free.get(jobs[n][0], 0)) for n in open_}
-        n = min(open_, key=lambda m: (start[m], -tail[m], m))
-        q, t = jobs[n][0], start[n]
-        for m in open_:
-            if jobs[m][0] == q and start[m] < t + jobs[n][1] and tail[m] > tail[n]:
-                if max(start[m] + tail[m], start[m] + jobs[m][1] + tail[n]) < start[n] + jobs[n][1] + tail[m]:
-                    n = m
-        open_.remove(n)
-        order.append(n)
-        free[q] = end[n] = start[n] + jobs[n][1]
-        for m in after[n]:
-            ready[m] = max(ready[m], end[n] + before[m][n])
-            left[m] -= 1
-            if not left[m]:
-                open_.append(m)
+        before.append({m: (jobs[m]["lag"] + J["hand"] if w and not q == jobs[m]["q"] == "t" else 0) for m, w in p.items()})
+    push, hold = [J["lead"] for J in jobs], [0] * len(jobs)
+
+    def place():
+        tail = [0] * len(jobs)
+        for n in range(len(jobs) - 1, -1, -1):
+            tail[n] += jobs[n]["c"] + push[n]
+            for m, gap in before[n].items():
+                tail[m] = max(tail[m], tail[n] + (1 - jobs[m]["c"] if jobs[m]["lazy"] else gap))
+        start, taken = {}, {}
+        for n in sorted(range(len(jobs)), key=lambda m: (-tail[m], m)):
+            c, slots = jobs[n]["c"], taken.setdefault(jobs[n]["q"], [])
+            t = max([start[m] + jobs[m]["c"] + gap for m, gap in before[n].items()], default=0) + hold[n]
+            k = len(slots)
+            while k and slots[k - 1][1] > t:
+                k -= 1
+            while k < len(slots) and slots[k][0] < t + c:
+                t = max(t, slots[k][1])
+                k += 1
+            slots.insert(k, (t, t + c))
+            start[n] = t
+        return sorted(start, key=lambda m: (start[m], m))
+
+    def both(order, less):
+        ends = [run(order, less, [J["c"] + int(d * J["pick"]) for J in jobs]) for d in OPT["ends"]]
+        return sum(e[0] for e in ends), [n for e in ends for n in e[1]]
+
+    def run(order, less, cost):
+        end, why, prev = {}, {}, {}
+        for n in order:
+            q, t, w = jobs[n]["q"], 0, None
+            for m, gap in before[n].items():
+                e = end[m] + (gap - jobs[n]["hand"] + less if gap else 0)
+                if e > t:
+                    t, w = e, m
+            held = q in prev and end[prev[q]] > t and prev[q] not in before[n]
+            if held:
+                t, w = end[prev[q]], prev[q]
+            end[n], why[n], prev[q] = t + cost[n], (w, held), n
+        n = max(end, key=lambda m: end[m] + jobs[m]["lag"])
+        span, behind = end[n] + jobs[n]["lag"], []
+        while n is not None:
+            if why[n][1]:
+                behind.append((n, why[n][0]))
+            n = why[n][0]
+        return span, behind
+
+    order = place()
+    span, behind = both(order, OPT["true"])
+    for k in range(OPT["rounds"]):
+        (n, m), step = behind[k * 7919 % len(behind)], OPT["step"] * (1 + k % 4)
+        what, n = (hold, m) if k % 3 == 0 else (push, n)
+        what[n] += step
+        trial = place()
+        s, b = both(trial, OPT["true"])
+        if s <= span:
+            order, span, behind = trial, s, b
+        else:
+            what[n] -= step
+    OPT["span"] = span
     return order
 
 
@@ -136,7 +197,7 @@ def rank_program(g, core, T, topo):
     own = {"v": "cv", "a": "ca", "t": "ct", "g": "cg"}
     cnt, know, clock, wr, rd = {}, {q: {} for q in Q}, {}, {}, {}
     bank = [{} for _ in range(8)]
-    jobs, calls = [], []
+    jobs, calls, mode = [], [], {"hand": OPT["hand"][0], "lazy": False, "pick": 0}
 
     def merge(q, ev):
         k = know[q]
@@ -144,7 +205,7 @@ def rank_program(g, core, T, topo):
             if k.get(s, 0) < v:
                 k[s] = v
 
-    def deps(q, R, W, banks=()):
+    def deps(q, R, W, banks):
         evs = []
         for k in R:
             evs += wr.get(k, [])
@@ -159,7 +220,7 @@ def rank_program(g, core, T, topo):
                 Q[q].wait_ge(T.sem[ev[0]], ev[1])
                 merge(q, ev)
 
-    def done(q, ev, R, W, banks=()):
+    def done(q, ev, R, W, banks):
         if q != "g" or ev[0] == "cg":
             clock[ev] = dict(know[q])
         for k in W:
@@ -171,7 +232,8 @@ def rank_program(g, core, T, topo):
             bank[k][q] = ev
 
     def job(q, call, cycles, lag, R, W, banks=(), dma=False):
-        jobs.append((q, cycles, lag, R, W, banks, dma))
+        jobs.append(dict(mode, q=q, c=cycles, lag=lag, R=R, W=W, banks=banks, dma=dma, lead=0))
+        mode["pick"] = 0
 
         def issue():
             deps(q, R, W, banks)
@@ -185,7 +247,9 @@ def rank_program(g, core, T, topo):
             cnt[own[q]] = cnt.get(own[q], 0) + 1
             ins.then_inc(T.sem[own[q]], 1)
             return own[q], cnt[own[q]]
-        job(q, call, cycles, 0, R, W, banks, q == "g")
+        cycles += OPT["fix"] if q in "va" else 0
+        cycles += OPT["afix"] if q == "a" and not mode["pick"] else 0
+        job(q, call, cycles, OPT["plat"] if q == "t" else 0, R, W, banks, q == "g")
 
     def dma(q, sem, moves, R, W, lag=3000):
         def call():
@@ -245,7 +309,12 @@ def rank_program(g, core, T, topo):
     V, S_, PE = g.vector, g.scalar, g.tensor
 
     def picks(n):
-        return 70 + int(OPT["G"] * n)
+        mode["pick"] = n
+        return 70 - OPT["fix"] + int(OPT["G"] * n)
+
+    def puts(n):
+        mode["pick"] = 4 * n
+        return int(OPT["sc"] * n)
 
     def ts(n, out, in0, s1, s2, o0, o1, R, W, banks=()):
         if o1 is None:
@@ -281,21 +350,21 @@ def rank_program(g, core, T, topo):
 
     ps = [T["ps%d" % k] for k in range(8)]
 
-    def stage(q, k, src):
-        dma(q, "s_" + k, [(T["sg_" + k][:], src)], [], ["sg_" + k])
-
-    def hand(k, src, dstbuf, c0, c1, R):
-        dma("s", "s_" + k, [(T["sg_" + k][:], src[:, c0:c1]), (dstbuf[r0:r1, c0:c1], src[r0:r1, c0:c1])], R,
-            ["sg_" + k, k + "_o"])
+    def stage(k, src):
+        dma("s", "s_" + k, [(T["sg_" + k][:], src)], [], ["sg_" + k])
 
     state = (T.px, T.py, T.en, T.vx, T.vy, T.fm)
     loads = [(T.lst[:, 192 * k:192 * k + t.shape[1]], t[:, :]) for k, t in enumerate(state)]
-    dma("a", "inl", loads[:3] + [(T.corI[:, :], T.cor[:, :])], [], ["lst", "corI"], 5000)
-    stage("s", "q0", T.slab[:, 0:1024])
-    dma("s", "inf", loads[3:], [], ["lst2"], 5000)
-    for k in range(1, 4):
-        stage("s", "q%d" % k, T.slab[:, 1024 * k:1024 * k + 1024])
-    stage("s", "sp", T.spow[:, :])
+    stage("q0", T.slab[:, 0:1024])
+    dma(OPT["lq"][0], "inc", [(T.corI[:, :], T.cor[:, :])], [], ["corI"], 2500)
+    dma(OPT["lq"][1], "inl", loads[:3], [], ["lst"], OPT["l1"])
+    fill(512, T.z32[:, :], 0.0, ["z32"])
+    dma(OPT["lq"][2], "zer", [(T.invA[0::16, :], T.z32[:, :])], ["z32"], ["invA", "invB"])
+    stage("q1", T.slab[:, 1024:2048])
+    dma(OPT["lq"][3], "inf", loads[3:], [], ["lst2"], OPT["l2"])
+    stage("q2", T.slab[:, 2048:3072])
+    stage("q3", T.slab[:, 3072:4096])
+    stage("sp", T.spow[:, :])
     dma("s", "own", [(T.slabN[r0:r1, :], T.slab[r0:r1, :]), (T.stT[r0:r1, :], T.spow[r0:r1, :])], [], ["slabN_o"])
 
     def iota(n, out, pattern, base, cm, W):
@@ -307,15 +376,10 @@ def rank_program(g, core, T, topo):
     iota(256, T.ia[:, :], [[0, 2], [-1, 128]], 0, 1, ["ia"])
     iota(512, T.pos0[:, :], [[1, 32], [128, 16]], LIFT, 0, ["pos0"])
 
-    fill(256, T.z32[:, :], 0.0, ["z32"])
-    dma("a", "zer", [(T.invA[0::16, :], T.z32[:, :]), (T.invB[0::16, :], T.z32[:, :])], ["z32"], ["invA", "invB"])
+    fill(256, T.zb[:, :], 0.0, ["zb"])
     fill(272, T.Tx[:, :], 0.0, ["Tx0", "Tx1"])
     fill(128, T.W[:, :], 0.0, ["W0", "W1"])
-    fill(128, T.Kk[:, :], K64, ["K0", "K1"])
-    fill(256, T.zb[:, :], 0.0, ["zb"])
-    fill(1024, T.B[:, :], 1.0, ["B"])
-    fill(384, T.rm[:, :], 1.0, ["rm"])
-    fill(64, T.rm[:, 0::6], 0.0, ["rm"])
+    fill(128, T.Kk[:, :], 65 * K64, ["K0", "K1", "Re0"])
 
     for hh in range(2):
         ita = T.ita[:, 64 * hh:64 * hh + 64]
@@ -340,6 +404,7 @@ def rank_program(g, core, T, topo):
         cp(128, T.Re[:, 128 * u:128 * u + 128], T.r0[:, :], ["r0"], ["Re%d" % u])
         cp(128, T.Rq[:, 128 * u:128 * u + 128], T.r1[:, :], ["r1"], ["Rq%d" % u])
         act(128, T.Reb[:, 128 * u:128 * u + 128], T.r0[:, :], F.Identity, ["r0"], ["Reb%d" % u])
+        act(128, T.Re32[:, 128 * u:128 * u + 128], T.r0[:, :], F.Identity, ["r0"], ["Rf%d" % u])
         act(128, T.Rk[:, 128 * u:128 * u + 128], T.r1[:, :], F.Identity, ["r1"], ["Rk%d" % u], scale=-1.0)
     RR = ["Re0", "Re1", "Rq0", "Rq1", "Rk0", "Rk1", "Reb0", "Reb1"]
 
@@ -351,7 +416,6 @@ def rank_program(g, core, T, topo):
     for k in range(4):
         cp(64, T.e16s[:, 384 + k:640:4], T.corI[:, 64 * k:64 * k + 64], ["corI"], ["e16s%d" % k])
     cp(192, T.e16s[:, 0:192], T.qd[:, :], ["qd"], ["e16sv"])
-    hand("el", T.e16s, T.e16r, 0, 640, ["e16sv", "e16se"] + ["e16s%d" % k for k in range(4)])
     cp(1088, T.raw[:, :], T.lst[:, :], ["lst", "lst2"], ["raw"])
 
     def settle(b, k):
@@ -359,26 +423,22 @@ def rank_program(g, core, T, topo):
         items = []
         for hh in range(2):
             t0, t1 = T.Tx[:, 136 * hh + 1:136 * hh + 129], T.Tx[:, 136 * hh:136 * hh + 128]
-            pX, pE, pD = ps[k][:, 2 * hh:256:4], ps[k][:, 2 * hh + 1:256:4], ps[k][:, 256 + hh:384:2]
+            pX, pE, pD = ps[k][:, hh:128:2], ps[k][:, 128 + hh:256:2], ps[k][:, 256 + hh:384:2]
             items += [(pX, t0, x, True, False), (pX, t1, y, False, True), (pE, t0, E, True, True),
                       (pD, t0, dx, True, False), (pD, t1, dy, False, True)]
             if b < NB - 1:
                 items.append((ps[k][:, 384 + hh:512:2], t0, T.raw[:, 960 + 64 * b:1024 + 64 * b], True, True))
         mm(3072, items, ["Tx0", "Tx1", "raw"], [k])
-        c = cST(b)
-        act(128, T.SS[:, c:c + 256:2], ps[k][:, 0:256:2], F.Identity, [], ["SSx%d" % b], [k], bias=XOFF, scale=1.0 / 16)
-        act(128, T.SS[:, c + 1:c + 256:2], ps[k][:, 1:256:2], F.Identity, [], ["SSe%d" % b], [k], bias=OFF, scale=1.0 / 64)
-        act(128, T.SS[:, cDX(b):cDX(b) + 128], ps[k][:, 256:384], F.Identity, [], ["SSd%d" % b], [k], scale=1.0 / 8)
-        if b < NB - 1:
-            act(128, T.SS[:, cF(b):cF(b) + 128], ps[k][:, 384:512], F.Identity, [], ["SSf%d" % b], [k], bias=OFF,
-                scale=1.0 / 64)
-            act(128, T.SS[:, cF(b) + 256:cF(b) + 384], ps[k][:, 384:512], F.Sign, [], ["SSl%d" % b], [k], scale=-1.0)
+        ways_out = [("x", sX(b), 1.0 / 16, XOFF), ("e", cE(b), 1.0 / 64, OFF), ("d", sX(b) + 128, 1.0 / 8, 0.0),
+                    ("f", cF(b), 1.0 / 64, OFF)]
+        for u, (key, c, scale, bias) in enumerate(ways_out[:4 if b < NB - 1 else 3]):
+            o, i, W = T.SS[:, c:c + 128], ps[k][:, 128 * u:128 * u + 128], ["SS%s%d" % (key, b)]
+            if b in OPT["sv"]:
+                ts(128, o, i, scale, bias, A.mult, A.add, [], W, [k])
+            else:
+                act(128, o, i, F.Identity, [], W, [k], bias=bias, scale=scale)
 
     settle(0, 2)
-    hand("s0", T.SS, T.SR, 0, 384, ["SSx0", "SSe0", "SSd0"])
-    stage("s", "kp", T.kap[:, :])
-    settle(1, 6)
-    settle(2, 7)
 
     ts(256, T.c1[:, :], T.corI[:, :], 15, None, A.bitwise_and, None, ["corI"], ["c1"])
     ts(256, T.c2[:, :], T.corI[:, :], 4, None, A.arith_shift_right, None, ["corI"], ["c2"])
@@ -389,35 +449,60 @@ def rank_program(g, core, T, topo):
     CT = ["corT%d" % k for k in range(4)]
     base = [float(2048 * (u // 4) + 32 * (u % 4)) for u in range(8)]
     split = OPT["split"]
+    for u in range(split):
+        ts(puts(512), T.invA[:, 0:4096].indirect(T.corT[:, 32 * u:32 * u + 32]), T.pos0[:, :], 1.0, base[u], A.mult, A.add,
+           CT + ["pos0"], ["invA", "warm2"])
     for u in range(split, 8):
         act(512, T.posv[:, 512 * (u - split):512 * (u - split) + 512], T.pos0[:, :], F.Identity, ["pos0"], ["posv%d" % u],
             bias=base[u])
-    for u in range(split):
-        ts(2000, T.invA[:, :].indirect(T.corT[:, 32 * u:32 * u + 32]), T.pos0[:, :], 1.0, base[u], A.mult, A.add,
-           CT + ["pos0"], ["invA"])
-    act(1600 + 2000 * (8 - split), T.invB[:, :].indirect(T.corT[:, 32 * split:256]), T.posv[:, 0:512 * (8 - split)], F.Silu,
-        CT + ["posv%d" % u for u in range(split, 8)], ["invB", "w2"])
-    act(1800, T.w2[:, :], T.w3[:, :], F.Exp, ["w3"], ["w2", "warm"])
+    act(1600 + puts(512 * (8 - split)), T.invA[:, 4096:8192].indirect(T.corT[:, 32 * split:256]), T.posv[:, 0:512 * (8 - split)],
+        F.Silu, CT + ["posv%d" % u for u in range(split, 8)], ["invB", "warm"])
+    settle(1, 6)
+    settle(2, 7)
 
-    for k in ("q0", "q1", "q2", "q3", "el", "sp", "s0", "kp"):
-        send(k)
+    made = {"el": (T.e16s, T.e16r, 0, 640, ["e16sv", "e16se"] + ["e16s%d" % k for k in range(4)]),
+            "s0": (T.SS, T.SR, 0, 512, ["SSx0", "SSe0", "SSd0", "SSf0"]),
+            "s1": (T.SS, T.SR, 512, 1408, ["SSf1"] + ["SS%s%d" % (u, b) for u in "xed" for b in (1, 2)])}
+    home = {"sp": (T.stT, 0, 1024), "kp": (T.kpT, 0, 1024), "iv": (T.ivr, 0, 256), "iw": (T.ivr, 256, 512)}
+    home.update({"q%d" % k: (T.slabN, 1024 * k, 1024 * k + 1024) for k in range(4)})
+    home.update({k: v[1:4] for k, v in made.items()})
+
+    def ready(k):
+        buf, c0, c1 = home[k]
+        if k in made:
+            whole, mine, R = made[k][0][:, c0:c1], made[k][0][r0:r1, c0:c1], made[k][4]
+        elif k == "kp":
+            whole, mine, R = T.kap[:, :], T.kap[r0:r1, :], []
+        else:
+            whole, mine = T.invA[0::16, 16 * c0:16 * c1], T.invA[r0:r0 + 1, 16 * c0:16 * c1]
+            R = ["invB" if c0 else "invA"]
+        dma("s", "s_" + k, [(T["sg_" + k][:], whole), (buf[r0:r1, c0:c1], mine)], R, ["sg_" + k, k + "_o"])
+
+    for w in OPT["sq"].split():
+        k = w[1:]
+        if w == "ones":
+            iota(2048, T.B[:, :], [[0, 2048]], 1, 0, ["B"])
+            op("g", lambda: g.affine_select(T.rm[:, :], T.B[:, 0:768], [[0, 128], [1, 6]], A.not_equal, 0.0, 0, 0), 1750,
+               ["B"], ["rm"])
+        elif w[0] == "+":
+            ready(k)
+        elif w[0] == ">":
+            send(k, OPT["lkp"] if k == "kp" else 5000)
+        else:
+            unload("s", k, home[k][0], home[k][1], home[k][2], [k])
     op("g", lambda: g.affine_select(T.B[:, :], T.B[:, :], [[-1, 16], [-16, 8], [0, 16]], A.is_equal, 0.0, 0, 1), 4300,
        ["B"], ["B"])
-    for k in range(4):
-        unload("s", "q%d" % k, T.slabN, 1024 * k, 1024 * k + 1024, ["slabN%d" % k])
-    unload("s", "el", T.e16r, 0, 640, ["el"])
-    unload("s", "sp", T.stT, 0, 1024, ["stT"])
-    unload("s", "s0", T.SR, 0, 384, ["s0"])
-    dma("s", "ownk", [(T.kpT[r0:r1, :], T.kap[r0:r1, :])], [], ["kpT_o"])
-    unload("s", "kp", T.kpT, 0, 1024, ["kpT"])
-    dma("s", "inv", [(T.SS[:, 1664:1920], T.invA[0::16, :]), (T.SS[:, 1920:2176], T.invB[0::16, :])], ["invA", "invB"],
-        ["invl"])
-    hand("s1", T.SS, T.SR, 384, 2176, ["invl", "SSf0", "SSl0", "SSf1", "SSl1"]
-         + ["SS%s%d" % (u, b) for u in "xed" for b in (1, 2)])
-    send("s1")
-    unload("s", "s1", T.SR, 384, 2176, ["s1"])
-    EL, S0, S1 = ["el", "el_o", "warm"], ["s0", "s0_o"], ["s1", "s1_o"]
-    SN = ["slabN0", "slabN1", "slabN2", "slabN3", "slabN_o"]
+    EL, S0, S1 = ["el", "el_o", "warm", "warm2"], ["s0", "s0_o"], ["s1", "s1_o"]
+    fill(768, T.SR[:, cDX(0):cDX(NB)], 0.0, ["dx0"])
+
+    def pair(b, R):
+        R = R + (S1 if b else S0)
+        cp(128, T.SR[:, cX(b) + 1:cX(b) + 256:2], T.SR[:, sX(b):sX(b) + 128], R, ["x%d" % b])
+        cp(128, T.SR[:, cDX(b) + 1:cDX(b) + 256:2], T.SR[:, sX(b) + 128:sX(b) + 256], R + ["dx0"], ["d%d" % b])
+        if b < NB - 1:
+            ts(128, T.SR[:, cL(b):cL(b) + 128], T.SR[:, cF(b):cF(b) + 128], OFF, -1.0, A.is_gt, A.mult, R, ["lo%d" % b])
+
+    SN, KP = ["q0", "q1", "q2", "q3", "slabN_o"], ["kp", "kp_o"]
 
     def lists(n, h, u, c0=0, c1=32):
         b, j = divmod(n, LG)
@@ -427,9 +512,8 @@ def rank_program(g, core, T, topo):
         c = 192 * u + 64 * b + 32 * h
         return T.e16r[:, c + c0:c + c1], EL
 
-    def st(b, h, u=None):
-        c = cST(b) + 128 * h
-        return T.SR[:, c:c + 128] if u is None else T.SR[:, c + u:c + 128:2]
+    def energy(b, h):
+        return T.SR[:, cE(b) + 64 * h:cE(b) + 64 * h + 64]
 
     def amt(n, c0, c1):
         return T.amt[:, 1024 * (n % NA) + c0:1024 * (n % NA) + c1]
@@ -437,94 +521,132 @@ def rank_program(g, core, T, topo):
     def akey(n, h, u):
         return "amt%d_%d%d" % (n % NA, h, u)
 
-    cuts = ((0, OPT["p1"]), (OPT["p1"], 32))
+    def parts(n, what):
+        return [(0, 1)] if what in OPT["whole"][n // LG] else [(0,), (1,)]
 
     def amounts(n, h):
-        for u, (c0, c1) in enumerate(cuts):
-            o, R = lists(n, h, 0, c0, c1)
-            act(picks(16 * (c1 - c0)), amt(n, 512 * h + 16 * c0, 512 * h + 16 * c1), T.slabN[:, :].indirect(o), F.Copy,
-                SN + R, [akey(n, h, u)])
+        for us in parts(n, "a%d" % h):
+            o, R = lists(n, h, 0, 16 * us[0], 16 * us[-1] + 16)
+            c, w = 512 * h + 256 * us[0], 256 * len(us)
+            act(picks(w), amt(n, c, c + w), T.slabN[:, :].indirect(o), F.Copy, SN + R, [akey(n, h, u) for u in us])
 
     def losses(n, h):
-        for u, (c0, c1) in enumerate(cuts):
-            o, R = lists(n, h, 1, c0, c1)
-            c0, c1 = 512 * h + 16 * c0, 512 * h + 16 * c1
-            tt(picks(c1 - c0), T.prod[:, c0:c1], T.stT[:, :].indirect(o), amt(n, c0, c1), A.mult,
-               ["stT", "slabN_o", akey(n, h, u)] + R, ["prod%d%d" % (h, u)])
-        mm(512, [(ps[2 + h][:, 1:128:2], win(T.W, 16 * (n % LG) - 2 * i), T.prod[:, 512 * h + i:512 * h + 512:8], i == 0,
+        for us in parts(n, "s%d" % h):
+            o, R = lists(n, h, 1, 16 * us[0], 16 * us[-1] + 16)
+            c, w = 512 * h + 256 * us[0], 256 * len(us)
+            tt(picks(w), T.prod[:, c:c + w], T.stT[:, :].indirect(o), amt(n, c, c + w), A.mult,
+               ["sp", "slabN_o"] + [akey(n, h, u) for u in us] + R, ["prod%d%d" % (h, u) for u in us])
+        mm(512, [(ps[2 + h][:, 0:64], win(T.W, 16 * (n % LG) - 2 * i), T.prod[:, 512 * h + i:512 * h + 512:8], i == 0,
                   i == 7) for i in range(8)], ["W0", "W1", "prod%d0" % h, "prod%d1" % h], [2 + h])
+
+    def spend(b, h):
+        ks = "E%d%d" % (b, h)
+        tt(64, energy(b, h), energy(b, h), ps[2 + h][:, 0:64], A.add, [ks] + (S1 if b else S0), [ks], [2 + h])
 
     def move(n, h):
         b, j = divmod(n, LG)
-        p, k, ks, SB = ps[2 + h], [2 + h], "ST%d%d" % (b, h), S1 if b else S0
+        p, k, SB = ps[2 + h], [2 + h], ["x%d" % b, "d%d" % b]
         ri, c = T.ri[:, 64 * h:64 * h + 64], 128 * h
-        ts(64, ri, p[:, 1:128:2], 0.32, 5.4975, A.mult, A.add, [], ["ri%d" % h], k)
-        ts(64, p[:, 128:192], ri, 0.5, 2.0, A.max, A.min, ["ri%d" % h], ["m%d" % h], k)
-        tt(64, p[:, 0:128:2], p[:, 128:192], T.SR[:, cDX(b) + 64 * h:cDX(b) + 64 * h + 64], A.mult, ["m%d" % h] + SB,
-           ["P%d" % h], k)
-        tt(128, st(b, h), st(b, h), p[:, 0:128], A.add, [ks, "P%d" % h] + SB, [ks], k)
-        ts(64, T.Kk[:, c:c + 64], st(b, h, 0), K64 - 31.5, None, A.add, None, [ks], ["K%d" % h])
-        ts(128, T.Qh[:, c:c + 128], st(b, h), MAGIC, MAGIC, A.add, A.subtract, [ks], ["Q%d" % h])
+        z0, z1 = c + (cZ + 256 * (j % 2) if j else cX(b)), c + cZ + 256 * ((j + 1) % 2)
+        kz0, kz1 = "Z%d%d" % (j % 2, h), "Z%d%d" % ((j + 1) % 2, h)
+        ts(64, ri, p[:, 0:64], 0.32, 5.4975, A.mult, A.add, [], ["ri%d" % h], k)
+        spend(b, h)
+        ts(64, T.SR[:, z0:z0 + 128:2], ri, 0.5, 2.0, A.max, A.min, ["ri%d" % h] + SB, ["m%d" % h])
         o = [-16 * (j + 1) - 8 * hh for hh in range(2)]
-        mm(384, [(p[:, 192:256], win(T.Rk, o[hh]), T.Kk[:, c + hh:c + 128:2], hh == 0, False) for hh in range(2)]
-           + [(p[:, 192:224], win(T.Rq, o[hh]), T.Qh[:, c + 2 * hh:c + 128:4], False, False) for hh in range(2)]
-           + [(p[:, 224:256], win(T.Re, o[hh]), T.Qh[:, c + 2 * hh + 1:c + 128:4], False, hh == 1) for hh in range(2)],
-           RR + ["Q%d" % h, "K%d" % h], k)
+        ts(64, T.Qh[:, c + 64:c + 128], energy(b, h), MAGIC, MAGIC, A.add, A.subtract, ["E%d%d" % (b, h)], ["QE%d" % h])
+        scan(128, T.SR[:, z1:z1 + 128], T.SR[:, cDX(b) + c:cDX(b) + c + 128], T.SR[:, z0:z0 + 128], A.add,
+             ["m%d" % h, kz0] + SB, [kz1])
+        if OPT["ka"][b]:
+            act(64, T.Kk[:, c:c + 64], T.SR[:, z1 + 1:z1 + 128:2], F.Identity, [kz1], ["K%d" % h], bias=K64 - 31.5)
+        else:
+            ts(64, T.Kk[:, c:c + 64], T.SR[:, z1 + 1:z1 + 128:2], K64 - 31.5, None, A.add, None, [kz1], ["K%d" % h])
+        ts(64, T.Qh[:, c:c + 64], T.SR[:, z1 + 1:z1 + 128:2], MAGIC, MAGIC, A.add, A.subtract, [kz1], ["Q%d" % h])
+        mm(192, [(p[:, 224:256], win(T.Re, o[hh]), T.Qh[:, c + 64 + hh:c + 128:2], hh == 0, hh == 1) for hh in range(2)]
+           + [(p[:, 192:224], I, T.Kk[:, 64:96], True, False)], RR + ["Pb", "QE%d" % h], k)
+        mm(128, [(p[:, 192:224], win(T.Rk, o[hh]), T.Kk[:, c + hh:c + 64:2], False, False) for hh in range(2)],
+           RR + ["K%d" % h], k)
+        mm(128, [(p[:, 192:224], win(T.Rq, o[hh]), T.Qh[:, c + hh:c + 64:2], False, hh == 1) for hh in range(2)],
+           RR + ["Q%d" % h], k)
         c = 128 * (5 * b + j) + 64 * h
-        ts(64, T.VE[:, c:c + 64], p[:, 192:256], 65 * K64, None, A.add, None, [], ["VE%d_%d" % (n + 1, h)], k)
-
-    def spend(b, h):
-        ks = "ST%d%d" % (b, h)
-        tt(64, st(b, h, 1), st(b, h, 1), ps[2 + h][:, 1:128:2], A.add, [ks], [ks], [2 + h])
+        cp(64, T.VE[:, c:c + 64], p[:, 192:256], [], ["VE%d_%d" % (n + 1, h)], k)
+        if b < NB - 1:
+            mode["lazy"] = True
+            ts(32, T.kf[:, 384 * b + 64 * (j + 1) + 32 * h:384 * b + 64 * (j + 1) + 32 * h + 32], T.VE[:, c:c + 32],
+               1.0 / 1024, 192 - 0.4995, A.mult, A.add, ["VE%d_%d" % (n + 1, h)], ["kf%d%d" % (n + 1, h)])
+            mode["lazy"] = False
 
     def vote(b, h):
         p, k, G = ps[2 + h], [2 + h], T.G[:, 64 * h:64 * h + 64]
-        tt(128, G, st(b, h, 1), T.SR[:, cF(b) + 64 * h:cF(b) + 64 * h + 64], A.subtract, ["ST%d%d" % (b, h)] + S1,
+        tt(128, G, energy(b, h), T.SR[:, cF(b) + 64 * h:cF(b) + 64 * h + 64], A.subtract, ["E%d%d" % (b, h), "lo%d" % b],
            ["G%d" % h])
-        tt(64, p[:, 128:192], G, p[:, 1:128:2], A.add, ["G%d" % h], ["m%d" % h], k)
+        tt(64, p[:, 128:192], G, p[:, 0:64], A.add, ["G%d" % h], ["m%d" % h], k)
         ts(64, p[:, 192:256], p[:, 128:192], 64.0, 1.0, A.mult, A.min, ["m%d" % h], ["P%d" % h], k)
-        tt(64, T.sv[:, 128 * b + 64 * h:128 * b + 64 * h + 64], T.SR[:, cF(b) + 256 + 64 * h:cF(b) + 320 + 64 * h],
-           p[:, 192:256], A.max, ["P%d" % h] + S1, ["sv%d%d" % (b, h)], k)
+        tt(64, T.sv[:, 128 * b + 64 * h:128 * b + 64 * h + 64], T.SR[:, cL(b) + 64 * h:cL(b) + 64 * h + 64],
+           p[:, 192:256], A.max, ["P%d" % h, "lo%d" % b], ["sv%d%d" % (b, h)], k)
+        jobs[-1]["lead"] = 0 if h else OPT["lead"][b]
         spend(b, h)
 
-    def add_terms(n, h, c0, c1, close=False):
+    waiting = []
+
+    def add_terms(n, h, c0, c1, close=False, late=[]):
         p = 512 * ((2 * n + h) % NP)
+        if n in OPT["aftr"] and not late:
+            waiting.append((n, h, c0, c1))
+            return
         key = ["L%d" % h]
         mm(4 * (c1 - c0), [(ps[h][:, c0:c1], win(T.P32, 16 * (n % LG)), T.pk[:, p + c0:p + c1], False, close)],
-           ["P32"] + ["pk%d" % ((p + c) // 128) for c in range(c0, c1, 128)] + ([] if close else key), [h],
+           ["P32"] + ["pk%d" % ((p + c) // 128) for c in range(c0, c1, 128)] + ([] if close else key) + late, [h],
            key if close else [])
 
-    def terms(n, h):
-        s, p, k = (2 * n + h) % NK, 512 * ((2 * n + h) % NP), 4 + h
-        o, R = lists(n, h, 1)
-        act(picks(512), T.kg[:, 512 * s:512 * s + 512], T.kpT[:, :].indirect(o), F.Copy, ["kpT", "kpT_o"] + R, ["kg%d" % s])
-        mm(512, [(ps[k][:, :], I, amt(n, 512 * h, 512 * h + 512), True, True)], ["Pb", akey(n, h, 0), akey(n, h, 1)], [k])
-        w = OPT["fw"]
+    def terms(n, h, late=[]):
+        s, p, k = 512 * ((2 * n + h) % NK), 512 * ((2 * n + h) % NP), 4 + h
+        mode["lazy"] = n in OPT["lazy"]
+        w = OPT["kw"][n // LG]
+        if n in OPT["fused"]:
+            o, R = lists(n, h, 1)
+            tt(picks(512), T.pk[:, p:p + 512], T.kpT[:, :].indirect(o), amt(n, 512 * h, 512 * h + 512), A.mult,
+               KP + R + late + [akey(n, h, 0), akey(n, h, 1)], ["pk%d" % (p // 128 + e) for e in range(4)])
+            for c in range(0, 512, OPT["aw"]):
+                add_terms(n, h, c, c + OPT["aw"])
+            mode["lazy"] = False
+            return
         for c in range(0, 512, w):
-            tt(w, T.pk[:, p + c:p + c + w], T.kg[:, 512 * s + c:512 * s + c + w], ps[k][:, c:c + w], A.mult, ["kg%d" % s],
+            o, R = lists(n, h, 1, c // 16, (c + w) // 16)
+            act(picks(w), T.kg[:, s + c:s + c + w], T.kpT[:, :].indirect(o), F.Copy, KP + R + late,
+                ["kg%d" % ((s + e) // 128) for e in range(c, c + w, 128)])
+        mm(512, [(ps[k][:, :], I, amt(n, 512 * h, 512 * h + 512), True, True)], ["Pb", akey(n, h, 0), akey(n, h, 1)], [k])
+        w = OPT["fw"][n // LG]
+        for c in range(0, 512, w):
+            tt(w, T.pk[:, p + c:p + c + w], T.kg[:, s + c:s + c + w], ps[k][:, c:c + w], A.mult,
+               ["kg%d" % ((s + e) // 128) for e in range(c, c + w, 128)],
                ["pk%d" % ((p + e) // 128) for e in range(c, c + w, 128)], [k])
         for c in range(0, 512, OPT["aw"]):
             add_terms(n, h, c, c + OPT["aw"])
+        mode["lazy"] = False
 
-    for k in range(8):
+    for k in range(OPT["ov"], 8):
         act(picks(512), T.slabP[:, 512 * k:512 * k + 512], T.slabN[:, :].indirect(T.e16r[:, 384 + 32 * k:416 + 32 * k]),
             F.Identity, SN + EL, ["slabP%d" % k], bias=-15.0)
-    tt(512, T.SS[:, 0:256], T.SR[:, 1664:1920], T.SR[:, 1920:2176], A.add, S1, ["SSx0", "SSe0", "SSd0"])
-    ts(256, T.inv[:, :], T.SS[:, 0:256], MAGIC - LIFT, MAGIC, A.add, A.subtract, ["SSx0"], ["inv"])
 
     for b in range(NB):
+        mode["hand"] = OPT["hand"][b]
         for j in range(LG):
             n = LG * b + j
-            for h in range(2):
-                amounts(n, h)
-                if n == NB * LG - 1:
-                    continue
+            amounts(n, 0)
+            amounts(n, 1)
+            for h in range(2 * (n < NB * LG - 1)):
                 losses(n, h)
+                if n + h == 0:
+                    pair(0, ["prod01"])
                 if j < LG - 1:
                     move(n, h)
                 else:
                     vote(b, h)
-                terms(n, h)
+                if n >= OPT["kn"] and n not in OPT["fused"]:
+                    terms(n, h)
+            if n == OPT["kn"] - 1:
+                for e in range(2 * OPT["kn"]):
+                    terms(e // 2, e % 2, ["VE%d_0" % (n + 1)])
         if b == NB - 1:
             break
 
@@ -537,16 +659,34 @@ def rank_program(g, core, T, topo):
             tr.append(RemoteDMATransfer(dst_ids=[dst(q)], dma_engine_mask=bits(near_mask(k)),
                                         remote_sem=T.sem["votes%d" % b], src=sv, dst=place))
         remote(tr, len(efar) + len(near) * len(near_mask(0)), "votes%d" % b, arrivals(len), SV, ["votes"], OPT["vote"])
+        for k in range(0 if b else OPT["ov"]):
+            ts(picks(512), T.slabP[:, 512 * k:512 * k + 512], T.slabN[:, :].indirect(T.e16r[:, 384 + 32 * k:416 + 32 * k]),
+               -15.0, None, A.add, None, SN + EL + SV, ["slabP%d" % k])
+        for n in range(LG * b, LG * b + LG):
+            if n in OPT["fused"]:
+                terms(n, 0, SV)
+                terms(n, 1, SV)
+        if b == NB - 2:
+            act(1800, T.w2[:, :], T.w3[:, :], F.Exp, ["w3"] + SV, ["w2", "inv"])
+        pair(b + 1, SV)
+        if b == 0:
+            tt(512, T.ivr[:, 512:768], T.ivr[:, 0:256], T.ivr[:, 256:512], A.add, ["iv", "iv_o", "iw", "iw_o"] + SV, ["ivs"])
+            ts(256, T.inv[:, :], T.ivr[:, 512:768], MAGIC - LIFT, MAGIC, A.add, A.subtract, ["ivs"], ["inv"])
         mm(384, [(ps[7][:, 0:64], win(T.Reb, -8 * hh), T.sv[:, 128 * b + hh:128 * b + 128:2], k + hh == 0, False)
                  for k in range(3) for hh in range(2)], RR + SV, [7])
-        for j in range(LG):
-            for h in range(2):
-                o, R = lists(LG * b + j, h, 0)
-                ts(64, T.kf[:, 64 * j + 32 * h:64 * j + 32 * h + 32], o, 1.0 / 1024, 192 - 0.4995, A.mult, A.add, R,
-                   ["kf%d%d" % (j, h)])
+        ts(64, T.kf[:, 384 * b:384 * b + 64], T.e16r[:, 64 * b:64 * b + 64], 1.0 / 1024, 192 - 0.4995, A.mult, A.add, EL,
+           ["kf%d0" % (LG * b), "kf%d1" % (LG * b)])
         for k in range(4):
-            ts(192, T.M[:, k::4], T.kf[:, :], 192.0 + k, None, A.is_equal, None,
-               ["kf%d%d" % (j, h) for j in range(LG) for h in range(2)], ["M%d" % k])
+            ts(192, T.M[:, k::4], T.kf[:, 384 * b:384 * b + 384], 192.0 + k, None, A.is_equal, None,
+               ["kf%d%d" % (LG * b + j, h) for j in range(LG) for h in range(2)], ["M%d" % k])
+        ab, xb, yk, sb = [[int(c) for c in OPT[w]] for w in ("ab", "xb", "yb", "sb")]
+        for c in range(OPT["pre"]):
+            if b:
+                mm(512, [(ps[ab[c]][:, :], I, T.slabQ[:, 512 * c:512 * c + 512], True, False)], ["Pb", "slabQ%d" % c], [ab[c]])
+            else:
+                mm(1024, [(ps[ab[c]][:, :], I, T.zb[:, :], True, False)]
+                   + [(ps[ab[c]][:, 128 * u:128 * u + 128], I, T.slabP[:, 4 * c + u:2048:16], False, False) for u in range(4)],
+                   ["Pb", "zb"] + ["slabP%d" % u for u in range(4)], [ab[c]])
         others = [q for q in range(N) if q != me]
         mm(896, [(ps[7][:, 0:64], win(T.Reb, -8 * hh), votes[:, 128 * q + hh:128 * q + 128:2], False,
                   q == others[-1] and hh == 1) for q in others for hh in range(2)], RR + ["votes"], [7])
@@ -556,9 +696,12 @@ def rank_program(g, core, T, topo):
             mm(512, [(ps[tb[u]][:, 256 * e + k:256 * e + 256:4], win(T.Pb, -16 * (2 * u + e)), T.t4[:, :], True, True)
                      for e in range(2) for k in range(4)], ["Pb", "t4"], [tb[u]])
 
+        for j in range(LG if OPT["tw"] == 256 else 0):
+            tt(256, T.tm[:, j::6], T.M[:, 256 * j:256 * j + 256], ps[tb[j // 2]][:, 256 * (j % 2):256 * (j % 2) + 256],
+               A.mult, ["M%d" % k for k in range(4)], ["tm%d0" % j, "tm%d1" % j], [tb[j // 2]])
         for h in range(2):
             c0, c1 = 768 * h, 768 * h + 768
-            for j in range(LG):
+            for j in range(LG if OPT["tw"] == 128 else 0):
                 c = 256 * (j % 2) + 128 * h
                 tt(128, T.tm[:, c0 + j:c1:6], T.M[:, 256 * j + 128 * h:256 * j + 128 * h + 128], ps[tb[j // 2]][:, c:c + 128],
                    A.mult, ["M%d" % k for k in range(4)], ["tm%d%d" % (j, h)], [tb[j // 2]])
@@ -567,88 +710,98 @@ def rank_program(g, core, T, topo):
             scan(384, T.mn[:, c0:c1], T.rm[:, :], T.S[:, c0:c1], A.min, ["rm", "S%d" % h], ["mn%d" % h])
             scan(384, T.mx[:, c0:c1], T.rm[:, :], T.S[:, c0:c1], A.max, ["rm", "S%d" % h], ["mx%d" % h])
 
-        ab, xb, yk, sb = [[int(c) for c in OPT[w]] for w in ("ab", "xb", "yb", "sb")]
-
         def total(t, h):
             return t[:, 768 * h + 5:768 * h + 768:6]
 
         def span(h):
             k = sb[h]
-            mm(256, [(ps[k][:, 0:128], I, total(T.S, h), True, False), (ps[k][:, 0:128], T.Pn[:, :], total(T.mx, h), False, True)],
+            mm(256, [(ps[k][:, 0:128], I, total(T.S, h), True, False),
+                     (ps[k][:, 0:128], T.Pn[:, :], total(T.mx, h), False, True)],
                ["Pb", "Pn", "S%d" % h, "mx%d" % h], [k])
             act(128, T.U[:, 128 * h:128 * h + 128], ps[k][:, 0:128], F.Identity, [], ["U%d" % h], [k])
 
-        def spread(c, k, par, key, amounts_too):
+        def spread(c, k, par, key, onto):
             h, items, R = c // 4, [], ["B", "Pb", key]
             for u in range(4):
                 i, o = 4 * (c % 4) + u, ps[k][:, 128 * u:128 * u + 128]
-                if amounts_too:
+                if onto == 1:
                     items.append((o, I, T.slabQ[:, 512 * c + 128 * u:512 * c + 128 * u + 128] if b
                                   else T.slabP[:, 2048 * h + i:2048 * h + 2048:16], True, False))
-                items.append((o, T.B[:, 128 * i:128 * i + 128], par, not amounts_too, True))
-            if amounts_too:
+                items.append((o, T.B[:, 128 * i:128 * i + 128], par, onto == 0, onto < 2 or u == 3))
+            if onto == 1:
                 R += ["slabQ%d" % c] if b else ["slabP%d" % (4 * h + u) for u in range(4)]
             mm(128 * len(items), items, R, [k])
 
         def alive(c):
-            spread(c, ab[c], total(T.mn, c // 4), "mn%d" % (c // 4), True)
+            spread(c, ab[c], total(T.mn, c // 4), "mn%d" % (c // 4), 2 if c < OPT["pre"] else 1)
             act(512, T.rb[:, 512 * c:512 * c + 512], ps[ab[c]][:, :], F.Identity, [], ["rb%d" % c], [ab[c]], bias=225.0,
                 scale=16.0)
 
         span(0)
         for c in range(4):
             alive(c)
+        span(1)
         for c in range(8):
             h, low = c // 4, T.yb[:, 512 * (c % 2):512 * (c % 2) + 512]
-            if c == OPT["sp1"]:
-                span(1)
-            spread(c, yk[c], T.U[:, 128 * h:128 * h + 128], "U%d" % h, False)
-            spread(c, xb[c], total(T.S, h), "S%d" % h, True)
+            spread(c, yk[c], T.U[:, 128 * h:128 * h + 128], "U%d" % h, 0)
+            spread(c, xb[c], total(T.S, h), "S%d" % h, 1)
             tt(512, low, T.rb[:, 512 * c:512 * c + 512], ps[yk[c]][:, :], A.min, ["rb%d" % c], ["yb%d" % (c % 2)], [yk[c]])
             tt(512, T.slabQ[:, 512 * c:512 * c + 512], low, ps[xb[c]][:, :], A.min, ["yb%d" % (c % 2)], ["slabQ%d" % c],
                [xb[c]])
             if c + 4 < 8:
                 alive(c + 4)
+        mode["lazy"] = True
+        while waiting:
+            add_terms(*waiting.pop(0), late=["slabQ6"])
+        mode["lazy"] = False
         SQ = ["slabQ%d" % c for c in range(8)] + ["inv"]
-        act(picks(2048), T.slabN[:, 0:2048], T.slabQ[:, :].indirect(T.inv[:, 0:128]), F.Relu, SQ,
-            ["slabN0", "slabN1", "slabN_o"], bias=15.0)
+        act(picks(2048), T.slabN[:, 0:2048], T.slabQ[:, :].indirect(T.inv[:, 0:128]), F.Relu, SQ, ["q0", "q1", "slabN_o"],
+            bias=15.0)
         ts(picks(2048), T.slabN[:, 2048:4096], T.slabQ[:, :].indirect(T.inv[:, 128:256]), 15.0, 0.0, A.add, A.max, SQ,
-           ["slabN2", "slabN3"])
+           ["q2", "q3"])
+
+    def remainders(c0, c1, k):
+        R = ["E%d%d" % (u, h) for u in range(c0 // 128, c1 // 128) for h in range(2)]
+        w, E, o = c1 - c0, T.SR[:, cE(0) + c0:cE(0) + c1], ps[6][:, c0 // 2:c1 // 2]
+        ts(w, T.ea[:, c0:c1], E, OFF, -1.0, A.max, A.mult, R, ["ea%d" % k])
+        ts(w, T.ed[:, c0:c1], E, OFF, K16 - 7.5, A.max, A.add, R, ["ed%d" % k])
+        mm(5 * w, [(o, win(T.Reb, -8 * hh), T.ed[:, c0 + hh:c1:2], hh == 0, False) for hh in range(2)]
+           + [(o, win(T.Re32, -8 * hh), T.ea[:, c0 + hh:c1:2], False, hh == 1) for hh in range(2)],
+           RR + ["Rf0", "Rf1", "ea%d" % k, "ed%d" % k], [6])
+        ts(w // 2, T.eo[:, c0 // 2:c1 // 2], o, -64.0, 64 * (K16 - OFF), A.mult, A.add, [], ["eo%d" % k], [6])
 
     n, b = NB * LG - 1, NB - 1
+    remainders(0, 256, 0)
+    dma("s", "s_ef", [(T.sg_ef[:], T.eo[:, 0:128])], ["eo0"], ["sg_ef"])
+    send("ef")
+    unload("s", "ef", T.ye, 0, 128, [], "outs")
     for h in range(2):
         p = 512 * ((2 * n + h) % NP)
-        for u, (c0, c1) in enumerate(cuts):
-            o, R = lists(n, h, 1, c0, c1)
-            c0, c1 = 16 * c0, 16 * c1
-            tt(picks(c1 - c0), T.pk[:, p + c0:p + c1], T.kpT[:, :].indirect(o), amt(n, 512 * h + c0, 512 * h + c1), A.mult,
-               ["kpT", "kpT_o", akey(n, h, u)] + R, ["pk%d" % ((p + c) // 128) for c in range(c0, c1, 128)])
-            add_terms(n, h, c0, c1, u == 1)
+        for u in range(2):
+            o, R = lists(n, h, 1, 16 * u, 16 * u + 16)
+            c = 256 * u
+            tt(picks(256), T.pk[:, p + c:p + c + 256], T.kpT[:, :].indirect(o), amt(n, 512 * h + c, 512 * h + c + 256), A.mult,
+               KP + [akey(n, h, u)] + R, ["pk%d" % ((p + c) // 128 + e) for e in range(2)])
+            add_terms(n, h, c, c + 256, u == 1)
         k, yo = "y%d" % h, T.yo[:, 512 * h:512 * h + 512]
         act(512, yo, ps[h][:, :], F.Exp, ["L%d" % h], ["yo%d" % h], [h], scale=-1.0 / 128)
+        jobs[-1]["lead"] = 0 if h else OPT["lead"][b]
         dma("s", "s_" + k, [(T["sg_" + k][:], yo)], ["yo%d" % h], ["sg_" + k])
-        dma("s", "outs", [(T.yl[r0:r1, 512 * h:512 * h + 512], T.yo[r0:r1, 512 * h:512 * h + 512])], ["yo%d" % h], [])
-        send(k)
+        send(k, OPT["ly"])
     for h in range(2):
         losses(n, h)
         spend(b, h)
-    for c0, c1, k in ((0, 256, 0), (256, 384, 1)):
-        R = ["ST%d%d" % (u, h) for u in range(c0 // 128, c1 // 128) for h in range(2)]
-        w = c1 - c0
-        ts(w, T.ea[:, c0:c1], T.SR[:, cST(0) + 2 * c0 + 1:cST(0) + 2 * c1:2], -OFF, 0.0, A.add, A.max, R, ["ea%d" % k])
-        ts(w, T.eb[:, c0:c1], T.ea[:, c0:c1], 64.0, None, A.mult, None, ["ea%d" % k], ["eb%d" % k])
-        ts(w, T.ec[:, c0:c1], T.eb[:, c0:c1], 1023, None, A.bitwise_and, None, ["eb%d" % k], ["ec%d" % k])
-        cp(w, T.ed[:, c0:c1], T.ec[:, c0:c1], ["ec%d" % k], ["ed%d" % k])
-    mm(384, [(ps[6][:, 0:192], win(T.Re, -8 * hh), T.ed[:, hh::2], hh == 0, hh == 1) for hh in range(2)],
-       RR + ["ed0", "ed1"], [6])
-    cp(192, T.eo[:, :], ps[6][:, 0:192], [], ["eo"], [6])
-    dma("a", "s_ee", [(T.sg_ee[:], T.eo[:, :])], ["eo"], ["sg_ee"])
-    dma("a", "outs", [(T.ye[r0:r1, :], T.eo[r0:r1, :])], ["eo"], [])
-    send("ee")
+    remainders(256, 384, 1)
+    dma("a", "s_ee", [(T.sg_ee[:], T.eo[:, 128:192])], ["eo1"], ["sg_ee"], 2500)
+    dma("a", "outs", [(T.ye[r0:r1, :], T.eo[r0:r1, :])], ["eo0", "eo1"], [])
+    send("ee", OPT["le"])
+    dma("s", "outs", [(T.yl[r0:r1, :], T.yo[r0:r1, :])], ["yo0", "yo1"], [])
     unload("s", "y0", T.yl, 0, 512, [], "outs")
     unload("s", "y1", T.yl, 512, 1024, [], "outs")
-    unload("a", "ee", T.ye, 0, 192, [], "outs")
-    for n in arrange(jobs):
+    unload("a", "ee", T.ye, 128, 192, [], "outs")
+    if not ORDER:
+        ORDER.extend(arrange(jobs))
+    for n in ORDER:
         calls[n]()
     for s, v in cnt.items():
         g.wait_ge(T.sem[s], v)

from concourse.bass import DstId, RemoteDMATransfer
from concourse.mybir import AluOpType as A, ActivationFunctionType as F

N = 8
NB, LG = 3, 6
MAGIC = 12582912.0
OFF = -63.0 / 128.0
XOFF = -15.0 / 32.0
K64 = 12288.0
K16 = 3072.0
LIFT = 64
NA, NK, NP = 7, 8, 17
OPT = {
    "split": 4,
    "hand": (140, 200, 240),
    "lead": (800, 400, 800),
    "lazy": (0, 1, 9, 10),
    "fix": 45, "kw": (512, 512, 512), "fw": (512, 512, 512), "aw": 256, "whole": ((), (), ()), "tw": 256, "ka": (0, 0, 0),
    "rounds": 7000, "true": 80, "step": 150, "afix": 200, "plat": 55,
    "sv": (), "aftr": (0, 1, 2, 3, 4, 5, 9, 10, 11), "ov": 0, "kn": 2, "pa": 1, "fused": (4, 5, 11), "lq": "aasa", "l2": 9000, "sc": 4.0, "ends": (-0.3, 0.45),
    "G": 1.56, "PE": 0.56, "vote": 7000, "pre": 2, "l1": 4500, "lkp": 8000, "ly": 6000, "le": 4000,
    "ab": "64646464", "xb": "23232323", "yb": "57575757", "sb": "56",
    "sq": ">q0 >q1 >q2 >q3 +el >el >sp -q0 +s0 -q1 >s0 ones -q2 -q3 -el -sp -s0 +kp >kp -kp +s1 >s1 +iv +iw >iv >iw -s1 -iv -iw",
}

ORDER = []
PIECES = {"q0": ("bfloat16", 128), "q1": ("bfloat16", 128), "q2": ("bfloat16", 128), "q3": ("bfloat16", 128),
          "sp": ("bfloat16", 128), "kp": ("bfloat16", 128), "el": ("uint16", 80), "s0": ("float32", 64),
          "s1": ("float32", 112), "iv": ("float32", 32), "iw": ("float32", 32), "y0": ("float32", 64),
          "y1": ("float32", 64), "ee": ("float32", 8), "ef": ("float32", 16)}


def _sb(n, d):
    return ("sbuf", [128, n], d)


SCRATCH = {
    "slabN": _sb(4096, "bfloat16"), "slabP": _sb(4096, "bfloat16"), "slabQ": _sb(4096, "bfloat16"),
    "stT": _sb(1024, "bfloat16"), "kpT": _sb(1024, "bfloat16"), "amt": _sb(1024 * NA, "bfloat16"),
    "kg": _sb(512 * NK, "bfloat16"), "prod": _sb(1024, "bfloat16"), "pk": _sb(512 * NP, "float32"),
    "pos0": _sb(512, "float32"), "posv": _sb(2048, "float32"), "invA": _sb(8192, "float32"),
    "inv": _sb(256, "uint16"), "ivr": _sb(768, "float32"),
    "lst": _sb(1088, "int32"), "raw": _sb(1088, "float32"), "corI": _sb(256, "int32"),
    "c1": _sb(256, "int32"), "c2": _sb(256, "int32"), "c3": _sb(256, "int32"), "corT": _sb(256, "uint16"),
    "e16s": _sb(640, "uint16"), "e16r": _sb(640, "uint16"), "SS": _sb(1664, "float32"), "SR": _sb(3712, "float32"),
    "ia": _sb(256, "float32"), "iab": _sb(256, "float32"), "ib": _sb(16, "float32"),
    "ir": _sb(128, "float32"), "it": _sb(64, "float32"), "ita": _sb(128, "float32"), "w1": _sb(16, "float32"),
    "w2": _sb(16, "float32"), "w3": _sb(16, "float32"), "r0": _sb(128, "float32"), "r1": _sb(128, "float32"),
    "r2": _sb(128, "float32"),
    "P32": _sb(256, "float32"), "Pb": _sb(256, "bfloat16"), "Pn": _sb(128, "bfloat16"), "W": _sb(256, "bfloat16"),
    "Re": _sb(256, "float16"), "Rq": _sb(256, "float16"), "Rk": _sb(256, "bfloat16"), "Reb": _sb(256, "bfloat16"),
    "Re32": _sb(256, "float32"), "Tx": _sb(272, "float32"), "B": _sb(2048, "bfloat16"), "rm": _sb(768, "bfloat16"),
    "zb": _sb(512, "bfloat16"), "z32": _sb(512, "float32"),
    "qa": _sb(384, "int32"), "qb": _sb(192, "int32"), "qc": _sb(192, "int32"), "qd": _sb(192, "int32"),
    "VE": _sb(1920, "uint16"), "ri": _sb(128, "int32"), "Qh": _sb(256, "float16"), "Kk": _sb(256, "bfloat16"),
    "G": _sb(128, "float32"), "sv": _sb(256, "bfloat16"), "votes0": _sb(1024, "bfloat16"),
    "votes1": _sb(1024, "bfloat16"), "t4": _sb(64, "bfloat16"), "kf": _sb(768, "bfloat16"), "M": _sb(1536, "bfloat16"),
    "tm": _sb(1536, "bfloat16"), "S": _sb(1536, "bfloat16"), "mn": _sb(1536, "bfloat16"), "mx": _sb(1536, "bfloat16"),
    "U": _sb(256, "bfloat16"), "rb": _sb(4096, "bfloat16"), "yb": _sb(1024, "bfloat16"),
    "yo": _sb(1024, "float32"), "ea": _sb(384, "float32"), "ed": _sb(384, "bfloat16"), "eo": _sb(192, "float32"),
}
for _k in range(8):
    SCRATCH["ps%d" % _k] = ("psum", [128, 512], "float32")
for _k, (_d, _n) in PIECES.items():
    SCRATCH["sg_" + _k] = ("dram", [8, 128, _n], _d)
    SCRATCH["ld_" + _k] = ("dram", [8, 128, _n], _d)

SEMAPHORES = (["cv", "ca", "ct", "cg", "sent", "inc", "zer", "inl", "inf", "own", "votes0", "votes1", "outs"]
              + ["s_" + k for k in PIECES] + ["a_" + k for k in PIECES] + ["l_" + k for k in PIECES])


def sX(b):
    return 512 + 256 * b if b else 0


def cE(b):
    return 384 + 128 * b


def cF(b):
    return 1280 if b else 256


def cL(b):
    return 1408 + 128 * b


def cX(b):
    return 1664 + 256 * b


def cDX(b):
    return 2432 + 256 * b


cZ = 3200


def ways(T, topo, r):
    c = T.cores[r]
    far = [q for q in range(N) if topo.chip(T.cores[q]) != topo.chip(c)]
    near = [q for q in range(N) if q != r and topo.chip(T.cores[q]) == topo.chip(c)]
    efar = topo.engines(c, T.cores[far[0]])
    enear = [e for e in topo.engines(c, T.cores[near[0]]) if e not in efar] if near else []
    return far, near, efar, enear


def bits(es):
    return sum(1 << e for e in es)


def arrange(jobs):
    wr, rd, last, before = {}, {}, {}, []
    for n, J in enumerate(jobs):
        q, p = J["q"], {}
        for k in J["R"]:
            p.update((m, True) for m in wr.get(k, []))
        for k in J["W"]:
            p.update((m, True) for m in wr.get(k, []) + rd.get(k, []))
        for k in [("bank", k) for k in J["banks"] if k > 1] + ([("dma", q)] if J["dma"] else []):
            if k in last:
                p.setdefault(last[k], jobs[last[k]]["q"] != q)
            last[k] = n
        for k in J["W"]:
            wr[k], rd[k] = [n], []
        for k in J["R"]:
            if k not in J["W"]:
                rd.setdefault(k, []).append(n)
        before.append({m: (jobs[m]["lag"] + J["hand"] if w and not q == jobs[m]["q"] == "t" else 0) for m, w in p.items()})
    push, hold = [J["lead"] for J in jobs], [0] * len(jobs)

    def place():
        tail = [0] * len(jobs)
        for n in range(len(jobs) - 1, -1, -1):
            tail[n] += jobs[n]["c"] + push[n]
            for m, gap in before[n].items():
                tail[m] = max(tail[m], tail[n] + (1 - jobs[m]["c"] if jobs[m]["lazy"] else gap))
        start, taken = {}, {}
        for n in sorted(range(len(jobs)), key=lambda m: (-tail[m], m)):
            c, slots = jobs[n]["c"], taken.setdefault(jobs[n]["q"], [])
            t = max([start[m] + jobs[m]["c"] + gap for m, gap in before[n].items()], default=0) + hold[n]
            k = len(slots)
            while k and slots[k - 1][1] > t:
                k -= 1
            while k < len(slots) and slots[k][0] < t + c:
                t = max(t, slots[k][1])
                k += 1
            slots.insert(k, (t, t + c))
            start[n] = t
        return sorted(start, key=lambda m: (start[m], m))

    def both(order, less):
        ends = [run(order, less, [J["c"] + int(d * J["pick"]) for J in jobs]) for d in OPT["ends"]]
        return sum(e[0] for e in ends), [n for e in ends for n in e[1]]

    def run(order, less, cost):
        end, why, prev = {}, {}, {}
        for n in order:
            q, t, w = jobs[n]["q"], 0, None
            for m, gap in before[n].items():
                e = end[m] + (gap - jobs[n]["hand"] + less if gap else 0)
                if e > t:
                    t, w = e, m
            held = q in prev and end[prev[q]] > t and prev[q] not in before[n]
            if held:
                t, w = end[prev[q]], prev[q]
            end[n], why[n], prev[q] = t + cost[n], (w, held), n
        n = max(end, key=lambda m: end[m] + jobs[m]["lag"])
        span, behind = end[n] + jobs[n]["lag"], []
        while n is not None:
            if why[n][1]:
                behind.append((n, why[n][0]))
            n = why[n][0]
        return span, behind

    order = place()
    span, behind = both(order, OPT["true"])
    for k in range(OPT["rounds"]):
        (n, m), step = behind[k * 7919 % len(behind)], OPT["step"] * (1 + k % 4)
        what, n = (hold, m) if k % 3 == 0 else (push, n)
        what[n] += step
        trial = place()
        s, b = both(trial, OPT["true"])
        if s <= span:
            order, span, behind = trial, s, b
        else:
            what[n] -= step
    OPT["span"] = span
    return order


def rank_program(g, core, T, topo):
    me = T.rank_of(core)
    if me is None:
        return
    Q = {"v": g.vector, "a": g.scalar, "t": g.tensor, "g": g, "s": g.sync}
    own = {"v": "cv", "a": "ca", "t": "ct", "g": "cg"}
    cnt, know, clock, wr, rd = {}, {q: {} for q in Q}, {}, {}, {}
    bank = [{} for _ in range(8)]
    jobs, calls, mode = [], [], {"hand": OPT["hand"][0], "lazy": False, "pick": 0}

    def merge(q, ev):
        k = know[q]
        for s, v in list(clock.get(ev, {}).items()) + [ev]:
            if k.get(s, 0) < v:
                k[s] = v

    def deps(q, R, W, banks):
        evs = []
        for k in R:
            evs += wr.get(k, [])
        for k in W:
            evs += wr.get(k, []) + rd.get(k, [])
        for k in banks:
            evs += [e for p, e in bank[k].items() if p != q]
        if q == "t":
            evs = [e for e in evs if e[0] != "ct"]
        for ev in sorted(set(evs), key=lambda e: -e[1]):
            if know[q].get(ev[0], 0) < ev[1]:
                Q[q].wait_ge(T.sem[ev[0]], ev[1])
                merge(q, ev)

    def done(q, ev, R, W, banks):
        if q != "g" or ev[0] == "cg":
            clock[ev] = dict(know[q])
        for k in W:
            wr[k], rd[k] = [ev], []
        for k in R:
            if k not in W:
                rd.setdefault(k, []).append(ev)
        for k in banks:
            bank[k][q] = ev

    def job(q, call, cycles, lag, R, W, banks=(), dma=False):
        jobs.append(dict(mode, q=q, c=cycles, lag=lag, R=R, W=W, banks=banks, dma=dma, lead=0))
        mode["pick"] = 0

        def issue():
            deps(q, R, W, banks)
            done(q, call(), R, W, banks)
        calls.append(issue)

    def op(q, fns, cycles, R, W, banks=()):
        def call():
            for f in (fns if isinstance(fns, list) else [fns]):
                ins = f()
            cnt[own[q]] = cnt.get(own[q], 0) + 1
            ins.then_inc(T.sem[own[q]], 1)
            return own[q], cnt[own[q]]
        cycles += OPT["fix"] if q in "va" else 0
        cycles += OPT["afix"] if q == "a" and not mode["pick"] else 0
        job(q, call, cycles, OPT["plat"] if q == "t" else 0, R, W, banks, q == "g")

    def dma(q, sem, moves, R, W, lag=3000):
        def call():
            for o, i in moves:
                Q[q].dma_start(o, i).then_inc(T.sem[sem], 16)
                cnt[sem] = cnt.get(sem, 0) + 16
            return sem, cnt[sem]
        job(q, call, 100, lag, R, W, (), True)

    far, near, efar, enear = ways(T, topo, me)
    turn = [0]

    def dst(q):
        a = topo.addr(T.cores[q])
        return DstId(rid=a[0], pnc=a[1])

    def arrivals(per_far):
        n = 0
        for q in range(N):
            if q != me:
                f2, n2, ef2, en2 = ways(T, topo, q)
                n += per_far(ef2) if me in f2 else len(en2) // len(n2)
        return n

    def near_mask(k):
        w = len(enear) // len(near)
        return enear[k * w:(k + 1) * w]

    def remote(tr, engines, sem, count, R, W, lag):
        def call():
            g.remote_dma_fused(tr, local_sem=T.sem.sent)
            cnt["sent"] = cnt.get("sent", 0) + engines
            cnt[sem] = count
            return sem, count
        job("g", call, 1200, lag, R, W, (), True)

    def send(k, lag=5000):
        tr = []
        for q in far:
            tr.append(RemoteDMATransfer(dst_ids=[dst(q)], dma_engine_mask=1 << efar[turn[0] % len(efar)],
                                        remote_sem=T.sem["a_" + k], src=T["sg_" + k][q], dst=T["ld_" + k][me]))
            turn[0] += 1
        for n, q in enumerate(near):
            tr.append(RemoteDMATransfer(dst_ids=[dst(q)], dma_engine_mask=bits(near_mask(n)), remote_sem=T.sem["a_" + k],
                                        src=T["sg_" + k][q], dst=T["ld_" + k][me]))
        remote(tr, len(far) + len(near) * len(near_mask(0)), "a_" + k, arrivals(lambda ef: 1), ["sg_" + k], ["ld_" + k], lag)

    def unload(q, k, buf, c0, c1, W, sem=None):
        mv = []
        if me > 0:
            mv.append((buf[0:16 * me, c0:c1], T["ld_" + k][0:me]))
        if me < N - 1:
            mv.append((buf[16 * me + 16:128, c0:c1], T["ld_" + k][me + 1:N]))
        dma(q, sem or "l_" + k, mv, ["ld_" + k], W)

    r0, r1 = 16 * me, 16 * me + 16
    V, S_, PE = g.vector, g.scalar, g.tensor

    def picks(n):
        mode["pick"] = n
        return 70 - OPT["fix"] + int(OPT["G"] * n)

    def puts(n):
        mode["pick"] = 4 * n
        return int(OPT["sc"] * n)

    def ts(n, out, in0, s1, s2, o0, o1, R, W, banks=()):
        if o1 is None:
            op("v", lambda: V.tensor_scalar(out, in0, s1, None, o0), n, R, W, banks)
        else:
            op("v", lambda: V.tensor_scalar(out, in0, s1, s2, o0, o1), n, R, W, banks)

    def tt(n, out, a, b, o, R, W, banks=()):
        op("v", lambda: V.tensor_tensor(out, a, b, o), n, R, W, banks)

    def cp(n, out, a, R, W, banks=()):
        op("v", lambda: V.tensor_copy(out, a), n, R, W, banks)

    def fill(n, out, c, W):
        op("v", lambda: V.memset(out, c), n, [], W)

    def scan(n, out, d0, d1, o1, R, W):
        op("v", lambda: V.tensor_tensor_scan(out, d0, d1, 0.0, A.mult, o1), n, R, W)

    def act(n, out, a, f, R, W, banks=(), bias=None, scale=None):
        kw = {}
        if bias is not None:
            kw["bias"] = bias
        if scale is not None:
            kw["scale"] = scale
        op("a", lambda: S_.activation(out, a, f, **kw), n, R, W, banks)

    def mm(n, items, R, banks, W=()):
        op("t", [(lambda it=it: PE.matmul(*it)) for it in items], int(OPT["PE"] * n), R, list(W), banks)

    def win(t, o):
        return t[:, o % 128:o % 128 + 128]

    ps = [T["ps%d" % k] for k in range(8)]

    def stage(k, src):
        dma("s", "s_" + k, [(T["sg_" + k][:], src)], [], ["sg_" + k])

    state = (T.px, T.py, T.en, T.vx, T.vy, T.fm)
    loads = [(T.lst[:, 192 * k:192 * k + t.shape[1]], t[:, :]) for k, t in enumerate(state)]
    stage("q0", T.slab[:, 0:1024])
    dma(OPT["lq"][0], "inc", [(T.corI[:, :], T.cor[:, :])], [], ["corI"], 2500)
    dma(OPT["lq"][1], "inl", loads[:3], [], ["lst"], OPT["l1"])
    fill(512, T.z32[:, :], 0.0, ["z32"])
    dma(OPT["lq"][2], "zer", [(T.invA[0::16, :], T.z32[:, :])], ["z32"], ["invA", "invB"])
    stage("q1", T.slab[:, 1024:2048])
    dma(OPT["lq"][3], "inf", loads[3:], [], ["lst2"], OPT["l2"])
    stage("q2", T.slab[:, 2048:3072])
    stage("q3", T.slab[:, 3072:4096])
    stage("sp", T.spow[:, :])
    dma("s", "own", [(T.slabN[r0:r1, :], T.slab[r0:r1, :]), (T.stT[r0:r1, :], T.spow[r0:r1, :])], [], ["slabN_o"])

    def iota(n, out, pattern, base, cm, W):
        op("g", lambda: g.iota(out, pattern, base, cm, allow_small_or_imprecise_dtypes=True), 160 + 2 * n, [], W)

    iota(64, T.it[:, :], [[-16, 8], [-1, 8]], 0, 1, ["it"])
    iota(128, T.ir[:, :], [[-16, 8], [-1000, 2], [-2, 8]], 0, 1, ["ir"])
    iota(16, T.ib[:, :], [[0, 2], [-16, 8]], 0, 1, ["ib"])
    iota(256, T.ia[:, :], [[0, 2], [-1, 128]], 0, 1, ["ia"])
    iota(512, T.pos0[:, :], [[1, 32], [128, 16]], LIFT, 0, ["pos0"])

    fill(256, T.zb[:, :], 0.0, ["zb"])
    fill(272, T.Tx[:, :], 0.0, ["Tx0", "Tx1"])
    fill(128, T.W[:, :], 0.0, ["W0", "W1"])
    fill(128, T.Kk[:, :], 65 * K64, ["K0", "K1", "Re0"])

    for hh in range(2):
        ita = T.ita[:, 64 * hh:64 * hh + 64]
        act(64, ita, T.it[:, :], F.Abs, ["it"], ["ita%d" % hh], bias=-8.0 * hh)
        act(64, T.Tx[:, 136 * hh + 1:136 * hh + 129:2], ita, F.Relu, ["ita%d" % hh], ["Tx%d" % hh], bias=1.0, scale=-1.0)
    act(64, T.w1[:, :], T.ib[:, :], F.Abs, ["ib"], ["w1"], bias=-7.5)
    act(64, T.w2[:, :], T.w1[:, :], F.Relu, ["w1"], ["w2"], bias=8.0, scale=-1.0)
    act(64, T.w3[:, :], T.w2[:, :], F.Sign, ["w2"], ["w3"])
    act(256, T.iab[:, :], T.ia[:, :], F.Abs, ["ia"], ["iab"])
    act(256, T.P32[:, :], T.iab[:, :], F.Relu, ["iab"], ["P32"], bias=1.0, scale=-1.0)
    act(256, T.Pb[:, :], T.iab[:, :], F.Relu, ["iab"], ["Pb"], bias=1.0, scale=-1.0)
    act(128, T.Pn[:, :], T.P32[:, 0:128], F.Identity, ["P32"], ["Pn"], scale=-1.0)
    for c in range(2):
        act(64, T.W[:, c::16], T.w3[:, :], F.Identity, ["w3"], ["W%d" % c], scale=-1.0 / 64)
    I = win(T.Pb, 0)
    for h in range(2):
        mm(512, [(ps[h][:, :], I, T.zb[:, :], True, False)], ["Pb", "zb"], [h], ["L%d" % h])
    ts(128, T.r0[:, :], T.ir[:, :], 0.0, None, A.is_equal, None, ["ir"], ["r0"])
    ts(128, T.r2[:, :], T.ir[:, :], 1.0, 64.0, A.is_equal, A.mult, ["ir"], ["r2"])
    tt(256, T.r1[:, :], T.r2[:, :], T.r0[:, :], A.add, ["r0", "r2"], ["r1"])
    for u in range(2):
        cp(128, T.Re[:, 128 * u:128 * u + 128], T.r0[:, :], ["r0"], ["Re%d" % u])
        cp(128, T.Rq[:, 128 * u:128 * u + 128], T.r1[:, :], ["r1"], ["Rq%d" % u])
        act(128, T.Reb[:, 128 * u:128 * u + 128], T.r0[:, :], F.Identity, ["r0"], ["Reb%d" % u])
        act(128, T.Re32[:, 128 * u:128 * u + 128], T.r0[:, :], F.Identity, ["r0"], ["Rf%d" % u])
        act(128, T.Rk[:, 128 * u:128 * u + 128], T.r1[:, :], F.Identity, ["r1"], ["Rk%d" % u], scale=-1.0)
    RR = ["Re0", "Re1", "Rq0", "Rq1", "Rk0", "Rk1", "Reb0", "Reb1"]

    ts(384, T.qa[:, :], T.lst[:, 0:384], 4, None, A.arith_shift_right, None, ["lst"], ["qa"])
    ts(192, T.qc[:, :], T.lst[:, 384:576], 6, None, A.arith_shift_right, None, ["lst"], ["qc"])
    ts(192, T.qb[:, :], T.qa[:, 192:384], 64.0, None, A.mult, None, ["qa"], ["qb"])
    cp(192, T.e16s[:, 192:384], T.qc[:, :], ["qc"], ["e16se"])
    tt(384, T.qd[:, :], T.qb[:, :], T.qa[:, 0:192], A.add, ["qa", "qb"], ["qd"])
    for k in range(4):
        cp(64, T.e16s[:, 384 + k:640:4], T.corI[:, 64 * k:64 * k + 64], ["corI"], ["e16s%d" % k])
    cp(192, T.e16s[:, 0:192], T.qd[:, :], ["qd"], ["e16sv"])
    cp(1088, T.raw[:, :], T.lst[:, :], ["lst", "lst2"], ["raw"])

    def settle(b, k):
        x, y, E, dx, dy = [T.raw[:, 192 * u + 64 * b:192 * u + 64 * b + 64] for u in range(5)]
        items = []
        for hh in range(2):
            t0, t1 = T.Tx[:, 136 * hh + 1:136 * hh + 129], T.Tx[:, 136 * hh:136 * hh + 128]
            pX, pE, pD = ps[k][:, hh:128:2], ps[k][:, 128 + hh:256:2], ps[k][:, 256 + hh:384:2]
            items += [(pX, t0, x, True, False), (pX, t1, y, False, True), (pE, t0, E, True, True),
                      (pD, t0, dx, True, False), (pD, t1, dy, False, True)]
            if b < NB - 1:
                items.append((ps[k][:, 384 + hh:512:2], t0, T.raw[:, 960 + 64 * b:1024 + 64 * b], True, True))
        mm(3072, items, ["Tx0", "Tx1", "raw"], [k])
        ways_out = [("x", sX(b), 1.0 / 16, XOFF), ("e", cE(b), 1.0 / 64, OFF), ("d", sX(b) + 128, 1.0 / 8, 0.0),
                    ("f", cF(b), 1.0 / 64, OFF)]
        for u, (key, c, scale, bias) in enumerate(ways_out[:4 if b < NB - 1 else 3]):
            o, i, W = T.SS[:, c:c + 128], ps[k][:, 128 * u:128 * u + 128], ["SS%s%d" % (key, b)]
            if b in OPT["sv"]:
                ts(128, o, i, scale, bias, A.mult, A.add, [], W, [k])
            else:
                act(128, o, i, F.Identity, [], W, [k], bias=bias, scale=scale)

    settle(0, 2)

    ts(256, T.c1[:, :], T.corI[:, :], 15, None, A.bitwise_and, None, ["corI"], ["c1"])
    ts(256, T.c2[:, :], T.corI[:, :], 4, None, A.arith_shift_right, None, ["corI"], ["c2"])
    ts(256, T.c3[:, :], T.c1[:, :], 256.0, None, A.mult, None, ["c1"], ["c3"])
    tt(512, T.c1[:, :], T.c3[:, :], T.c2[:, :], A.add, ["c3", "c2"], ["c1"])
    for k in range(4):
        cp(64, T.corT[:, k::4], T.c1[:, 64 * k:64 * k + 64], ["c1"], ["corT%d" % k])
    CT = ["corT%d" % k for k in range(4)]
    base = [float(2048 * (u // 4) + 32 * (u % 4)) for u in range(8)]
    split = OPT["split"]
    for u in range(split):
        ts(puts(512), T.invA[:, 0:4096].indirect(T.corT[:, 32 * u:32 * u + 32]), T.pos0[:, :], 1.0, base[u], A.mult, A.add,
           CT + ["pos0"], ["invA", "warm2"])
    for u in range(split, 8):
        act(512, T.posv[:, 512 * (u - split):512 * (u - split) + 512], T.pos0[:, :], F.Identity, ["pos0"], ["posv%d" % u],
            bias=base[u])
    act(1600 + puts(512 * (8 - split)), T.invA[:, 4096:8192].indirect(T.corT[:, 32 * split:256]), T.posv[:, 0:512 * (8 - split)],
        F.Silu, CT + ["posv%d" % u for u in range(split, 8)], ["invB", "warm"])
    settle(1, 6)
    settle(2, 7)

    made = {"el": (T.e16s, T.e16r, 0, 640, ["e16sv", "e16se"] + ["e16s%d" % k for k in range(4)]),
            "s0": (T.SS, T.SR, 0, 512, ["SSx0", "SSe0", "SSd0", "SSf0"]),
            "s1": (T.SS, T.SR, 512, 1408, ["SSf1"] + ["SS%s%d" % (u, b) for u in "xed" for b in (1, 2)])}
    home = {"sp": (T.stT, 0, 1024), "kp": (T.kpT, 0, 1024), "iv": (T.ivr, 0, 256), "iw": (T.ivr, 256, 512)}
    home.update({"q%d" % k: (T.slabN, 1024 * k, 1024 * k + 1024) for k in range(4)})
    home.update({k: v[1:4] for k, v in made.items()})

    def ready(k):
        buf, c0, c1 = home[k]
        if k in made:
            whole, mine, R = made[k][0][:, c0:c1], made[k][0][r0:r1, c0:c1], made[k][4]
        elif k == "kp":
            whole, mine, R = T.kap[:, :], T.kap[r0:r1, :], []
        else:
            whole, mine = T.invA[0::16, 16 * c0:16 * c1], T.invA[r0:r0 + 1, 16 * c0:16 * c1]
            R = ["invB" if c0 else "invA"]
        dma("s", "s_" + k, [(T["sg_" + k][:], whole), (buf[r0:r1, c0:c1], mine)], R, ["sg_" + k, k + "_o"])

    for w in OPT["sq"].split():
        k = w[1:]
        if w == "ones":
            iota(2048, T.B[:, :], [[0, 2048]], 1, 0, ["B"])
            op("g", lambda: g.affine_select(T.rm[:, :], T.B[:, 0:768], [[0, 128], [1, 6]], A.not_equal, 0.0, 0, 0), 1750,
               ["B"], ["rm"])
        elif w[0] == "+":
            ready(k)
        elif w[0] == ">":
            send(k, OPT["lkp"] if k == "kp" else 5000)
        else:
            unload("s", k, home[k][0], home[k][1], home[k][2], [k])
    op("g", lambda: g.affine_select(T.B[:, :], T.B[:, :], [[-1, 16], [-16, 8], [0, 16]], A.is_equal, 0.0, 0, 1), 4300,
       ["B"], ["B"])
    EL, S0, S1 = ["el", "el_o", "warm", "warm2"], ["s0", "s0_o"], ["s1", "s1_o"]
    fill(768, T.SR[:, cDX(0):cDX(NB)], 0.0, ["dx0"])

    def pair(b, R):
        R = R + (S1 if b else S0)
        cp(128, T.SR[:, cX(b) + 1:cX(b) + 256:2], T.SR[:, sX(b):sX(b) + 128], R, ["x%d" % b])
        cp(128, T.SR[:, cDX(b) + 1:cDX(b) + 256:2], T.SR[:, sX(b) + 128:sX(b) + 256], R + ["dx0"], ["d%d" % b])
        if b < NB - 1:
            ts(128, T.SR[:, cL(b):cL(b) + 128], T.SR[:, cF(b):cF(b) + 128], OFF, -1.0, A.is_gt, A.mult, R, ["lo%d" % b])

    SN, KP = ["q0", "q1", "q2", "q3", "slabN_o"], ["kp", "kp_o"]

    def lists(n, h, u, c0=0, c1=32):
        b, j = divmod(n, LG)
        if j:
            c = 128 * (5 * b + j - 1) + 64 * h + 32 * u
            return T.VE[:, c + c0:c + c1], ["VE%d_%d" % (n, h)]
        c = 192 * u + 64 * b + 32 * h
        return T.e16r[:, c + c0:c + c1], EL

    def energy(b, h):
        return T.SR[:, cE(b) + 64 * h:cE(b) + 64 * h + 64]

    def amt(n, c0, c1):
        return T.amt[:, 1024 * (n % NA) + c0:1024 * (n % NA) + c1]

    def akey(n, h, u):
        return "amt%d_%d%d" % (n % NA, h, u)

    def parts(n, what):
        return [(0, 1)] if what in OPT["whole"][n // LG] else [(0,), (1,)]

    def amounts(n, h):
        for us in parts(n, "a%d" % h):
            o, R = lists(n, h, 0, 16 * us[0], 16 * us[-1] + 16)
            c, w = 512 * h + 256 * us[0], 256 * len(us)
            act(picks(w), amt(n, c, c + w), T.slabN[:, :].indirect(o), F.Copy, SN + R, [akey(n, h, u) for u in us])

    def losses(n, h):
        for us in parts(n, "s%d" % h):
            o, R = lists(n, h, 1, 16 * us[0], 16 * us[-1] + 16)
            c, w = 512 * h + 256 * us[0], 256 * len(us)
            tt(picks(w), T.prod[:, c:c + w], T.stT[:, :].indirect(o), amt(n, c, c + w), A.mult,
               ["sp", "slabN_o"] + [akey(n, h, u) for u in us] + R, ["prod%d%d" % (h, u) for u in us])
        mm(512, [(ps[2 + h][:, 0:64], win(T.W, 16 * (n % LG) - 2 * i), T.prod[:, 512 * h + i:512 * h + 512:8], i == 0,
                  i == 7) for i in range(8)], ["W0", "W1", "prod%d0" % h, "prod%d1" % h], [2 + h])

    def spend(b, h):
        ks = "E%d%d" % (b, h)
        tt(64, energy(b, h), energy(b, h), ps[2 + h][:, 0:64], A.add, [ks] + (S1 if b else S0), [ks], [2 + h])

    def move(n, h):
        b, j = divmod(n, LG)
        p, k, SB = ps[2 + h], [2 + h], ["x%d" % b, "d%d" % b]
        ri, c = T.ri[:, 64 * h:64 * h + 64], 128 * h
        z0, z1 = c + (cZ + 256 * (j % 2) if j else cX(b)), c + cZ + 256 * ((j + 1) % 2)
        kz0, kz1 = "Z%d%d" % (j % 2, h), "Z%d%d" % ((j + 1) % 2, h)
        ts(64, ri, p[:, 0:64], 0.32, 5.4975, A.mult, A.add, [], ["ri%d" % h], k)
        spend(b, h)
        ts(64, T.SR[:, z0:z0 + 128:2], ri, 0.5, 2.0, A.max, A.min, ["ri%d" % h] + SB, ["m%d" % h])
        o = [-16 * (j + 1) - 8 * hh for hh in range(2)]
        ts(64, T.Qh[:, c + 64:c + 128], energy(b, h), MAGIC, MAGIC, A.add, A.subtract, ["E%d%d" % (b, h)], ["QE%d" % h])
        scan(128, T.SR[:, z1:z1 + 128], T.SR[:, cDX(b) + c:cDX(b) + c + 128], T.SR[:, z0:z0 + 128], A.add,
             ["m%d" % h, kz0] + SB, [kz1])
        if OPT["ka"][b]:
            act(64, T.Kk[:, c:c + 64], T.SR[:, z1 + 1:z1 + 128:2], F.Identity, [kz1], ["K%d" % h], bias=K64 - 31.5)
        else:
            ts(64, T.Kk[:, c:c + 64], T.SR[:, z1 + 1:z1 + 128:2], K64 - 31.5, None, A.add, None, [kz1], ["K%d" % h])
        ts(64, T.Qh[:, c:c + 64], T.SR[:, z1 + 1:z1 + 128:2], MAGIC, MAGIC, A.add, A.subtract, [kz1], ["Q%d" % h])
        mm(192, [(p[:, 224:256], win(T.Re, o[hh]), T.Qh[:, c + 64 + hh:c + 128:2], hh == 0, hh == 1) for hh in range(2)]
           + [(p[:, 192:224], I, T.Kk[:, 64:96], True, False)], RR + ["Pb", "QE%d" % h], k)
        mm(128, [(p[:, 192:224], win(T.Rk, o[hh]), T.Kk[:, c + hh:c + 64:2], False, False) for hh in range(2)],
           RR + ["K%d" % h], k)
        mm(128, [(p[:, 192:224], win(T.Rq, o[hh]), T.Qh[:, c + hh:c + 64:2], False, hh == 1) for hh in range(2)],
           RR + ["Q%d" % h], k)
        c = 128 * (5 * b + j) + 64 * h
        cp(64, T.VE[:, c:c + 64], p[:, 192:256], [], ["VE%d_%d" % (n + 1, h)], k)
        if b < NB - 1:
            mode["lazy"] = True
            ts(32, T.kf[:, 384 * b + 64 * (j + 1) + 32 * h:384 * b + 64 * (j + 1) + 32 * h + 32], T.VE[:, c:c + 32],
               1.0 / 1024, 192 - 0.4995, A.mult, A.add, ["VE%d_%d" % (n + 1, h)], ["kf%d%d" % (n + 1, h)])
            mode["lazy"] = False

    def vote(b, h):
        p, k, G = ps[2 + h], [2 + h], T.G[:, 64 * h:64 * h + 64]
        tt(128, G, energy(b, h), T.SR[:, cF(b) + 64 * h:cF(b) + 64 * h + 64], A.subtract, ["E%d%d" % (b, h), "lo%d" % b],
           ["G%d" % h])
        tt(64, p[:, 128:192], G, p[:, 0:64], A.add, ["G%d" % h], ["m%d" % h], k)
        ts(64, p[:, 192:256], p[:, 128:192], 64.0, 1.0, A.mult, A.min, ["m%d" % h], ["P%d" % h], k)
        tt(64, T.sv[:, 128 * b + 64 * h:128 * b + 64 * h + 64], T.SR[:, cL(b) + 64 * h:cL(b) + 64 * h + 64],
           p[:, 192:256], A.max, ["P%d" % h, "lo%d" % b], ["sv%d%d" % (b, h)], k)
        jobs[-1]["lead"] = 0 if h else OPT["lead"][b]
        spend(b, h)

    waiting = []

    def add_terms(n, h, c0, c1, close=False, late=[]):
        p = 512 * ((2 * n + h) % NP)
        if n in OPT["aftr"] and not late:
            waiting.append((n, h, c0, c1))
            return
        key = ["L%d" % h]
        mm(4 * (c1 - c0), [(ps[h][:, c0:c1], win(T.P32, 16 * (n % LG)), T.pk[:, p + c0:p + c1], False, close)],
           ["P32"] + ["pk%d" % ((p + c) // 128) for c in range(c0, c1, 128)] + ([] if close else key) + late, [h],
           key if close else [])

    def terms(n, h, late=[]):
        s, p, k = 512 * ((2 * n + h) % NK), 512 * ((2 * n + h) % NP), 4 + h
        mode["lazy"] = n in OPT["lazy"]
        w = OPT["kw"][n // LG]
        if n in OPT["fused"]:
            o, R = lists(n, h, 1)
            tt(picks(512), T.pk[:, p:p + 512], T.kpT[:, :].indirect(o), amt(n, 512 * h, 512 * h + 512), A.mult,
               KP + R + late + [akey(n, h, 0), akey(n, h, 1)], ["pk%d" % (p // 128 + e) for e in range(4)])
            for c in range(0, 512, OPT["aw"]):
                add_terms(n, h, c, c + OPT["aw"])
            mode["lazy"] = False
            return
        for c in range(0, 512, w):
            o, R = lists(n, h, 1, c // 16, (c + w) // 16)
            act(picks(w), T.kg[:, s + c:s + c + w], T.kpT[:, :].indirect(o), F.Copy, KP + R + late,
                ["kg%d" % ((s + e) // 128) for e in range(c, c + w, 128)])
        mm(512, [(ps[k][:, :], I, amt(n, 512 * h, 512 * h + 512), True, True)], ["Pb", akey(n, h, 0), akey(n, h, 1)], [k])
        w = OPT["fw"][n // LG]
        for c in range(0, 512, w):
            tt(w, T.pk[:, p + c:p + c + w], T.kg[:, s + c:s + c + w], ps[k][:, c:c + w], A.mult,
               ["kg%d" % ((s + e) // 128) for e in range(c, c + w, 128)],
               ["pk%d" % ((p + e) // 128) for e in range(c, c + w, 128)], [k])
        for c in range(0, 512, OPT["aw"]):
            add_terms(n, h, c, c + OPT["aw"])
        mode["lazy"] = False

    for k in range(OPT["ov"], 8):
        act(picks(512), T.slabP[:, 512 * k:512 * k + 512], T.slabN[:, :].indirect(T.e16r[:, 384 + 32 * k:416 + 32 * k]),
            F.Identity, SN + EL, ["slabP%d" % k], bias=-15.0)

    for b in range(NB):
        mode["hand"] = OPT["hand"][b]
        for j in range(LG):
            n = LG * b + j
            amounts(n, 0)
            amounts(n, 1)
            for h in range(2 * (n < NB * LG - 1)):
                losses(n, h)
                if n + h == 0:
                    pair(0, ["prod01"])
                if j < LG - 1:
                    move(n, h)
                else:
                    vote(b, h)
                if n >= OPT["kn"] and n not in OPT["fused"]:
                    terms(n, h)
            if n == OPT["kn"] - 1:
                for e in range(2 * OPT["kn"]):
                    terms(e // 2, e % 2, ["VE%d_0" % (n + 1)])
        if b == NB - 1:
            break

        sv, votes = T.sv[:, 128 * b:128 * b + 128], T["votes%d" % b]
        SV = ["sv%d0" % b, "sv%d1" % b]
        place = votes[:, 128 * me:128 * me + 128]
        tr = [RemoteDMATransfer(dst_ids=[dst(q) for q in far], dma_engine_mask=bits(efar), remote_sem=T.sem["votes%d" % b],
                                srcs=[sv], dsts=[place for q in far])]
        for k, q in enumerate(near):
            tr.append(RemoteDMATransfer(dst_ids=[dst(q)], dma_engine_mask=bits(near_mask(k)),
                                        remote_sem=T.sem["votes%d" % b], src=sv, dst=place))
        remote(tr, len(efar) + len(near) * len(near_mask(0)), "votes%d" % b, arrivals(len), SV, ["votes"], OPT["vote"])
        for k in range(0 if b else OPT["ov"]):
            ts(picks(512), T.slabP[:, 512 * k:512 * k + 512], T.slabN[:, :].indirect(T.e16r[:, 384 + 32 * k:416 + 32 * k]),
               -15.0, None, A.add, None, SN + EL + SV, ["slabP%d" % k])
        for n in range(LG * b, LG * b + LG):
            if n in OPT["fused"]:
                terms(n, 0, SV)
                terms(n, 1, SV)
        if b == NB - 2:
            act(1800, T.w2[:, :], T.w3[:, :], F.Exp, ["w3"] + SV, ["w2", "inv"])
        pair(b + 1, SV)
        if b == 0:
            tt(512, T.ivr[:, 512:768], T.ivr[:, 0:256], T.ivr[:, 256:512], A.add, ["iv", "iv_o", "iw", "iw_o"] + SV, ["ivs"])
            ts(256, T.inv[:, :], T.ivr[:, 512:768], MAGIC - LIFT, MAGIC, A.add, A.subtract, ["ivs"], ["inv"])
        mm(384, [(ps[7][:, 0:64], win(T.Reb, -8 * hh), T.sv[:, 128 * b + hh:128 * b + 128:2], k + hh == 0, False)
                 for k in range(3) for hh in range(2)], RR + SV, [7])
        ts(64, T.kf[:, 384 * b:384 * b + 64], T.e16r[:, 64 * b:64 * b + 64], 1.0 / 1024, 192 - 0.4995, A.mult, A.add, EL,
           ["kf%d0" % (LG * b), "kf%d1" % (LG * b)])
        for k in range(4):
            ts(192, T.M[:, k::4], T.kf[:, 384 * b:384 * b + 384], 192.0 + k, None, A.is_equal, None,
               ["kf%d%d" % (LG * b + j, h) for j in range(LG) for h in range(2)], ["M%d" % k])
        ab, xb, yk, sb = [[int(c) for c in OPT[w]] for w in ("ab", "xb", "yb", "sb")]
        for c in range(OPT["pre"]):
            if b:
                mm(512, [(ps[ab[c]][:, :], I, T.slabQ[:, 512 * c:512 * c + 512], True, False)], ["Pb", "slabQ%d" % c], [ab[c]])
            else:
                mm(1024, [(ps[ab[c]][:, :], I, T.zb[:, :], True, False)]
                   + [(ps[ab[c]][:, 128 * u:128 * u + 128], I, T.slabP[:, 4 * c + u:2048:16], False, False) for u in range(4)],
                   ["Pb", "zb"] + ["slabP%d" % u for u in range(4)], [ab[c]])
        others = [q for q in range(N) if q != me]
        mm(896, [(ps[7][:, 0:64], win(T.Reb, -8 * hh), votes[:, 128 * q + hh:128 * q + 128:2], False,
                  q == others[-1] and hh == 1) for q in others for hh in range(2)], RR + ["votes"], [7])
        ts(64, T.t4[:, :], ps[7][:, 0:64], -1.0, 1.0, A.max, A.min, [], ["t4"], [7])
        tb = (2, 3, 7)
        for u in range(3):
            mm(512, [(ps[tb[u]][:, 256 * e + k:256 * e + 256:4], win(T.Pb, -16 * (2 * u + e)), T.t4[:, :], True, True)
                     for e in range(2) for k in range(4)], ["Pb", "t4"], [tb[u]])

        for j in range(LG if OPT["tw"] == 256 else 0):
            tt(256, T.tm[:, j::6], T.M[:, 256 * j:256 * j + 256], ps[tb[j // 2]][:, 256 * (j % 2):256 * (j % 2) + 256],
               A.mult, ["M%d" % k for k in range(4)], ["tm%d0" % j, "tm%d1" % j], [tb[j // 2]])
        for h in range(2):
            c0, c1 = 768 * h, 768 * h + 768
            for j in range(LG if OPT["tw"] == 128 else 0):
                c = 256 * (j % 2) + 128 * h
                tt(128, T.tm[:, c0 + j:c1:6], T.M[:, 256 * j + 128 * h:256 * j + 128 * h + 128], ps[tb[j // 2]][:, c:c + 128],
                   A.mult, ["M%d" % k for k in range(4)], ["tm%d%d" % (j, h)], [tb[j // 2]])
            scan(384, T.S[:, c0:c1], T.rm[:, :], T.tm[:, c0:c1], A.add, ["rm"] + ["tm%d%d" % (j, h) for j in range(LG)],
                 ["S%d" % h])
            scan(384, T.mn[:, c0:c1], T.rm[:, :], T.S[:, c0:c1], A.min, ["rm", "S%d" % h], ["mn%d" % h])
            scan(384, T.mx[:, c0:c1], T.rm[:, :], T.S[:, c0:c1], A.max, ["rm", "S%d" % h], ["mx%d" % h])

        def total(t, h):
            return t[:, 768 * h + 5:768 * h + 768:6]

        def span(h):
            k = sb[h]
            mm(256, [(ps[k][:, 0:128], I, total(T.S, h), True, False),
                     (ps[k][:, 0:128], T.Pn[:, :], total(T.mx, h), False, True)],
               ["Pb", "Pn", "S%d" % h, "mx%d" % h], [k])
            act(128, T.U[:, 128 * h:128 * h + 128], ps[k][:, 0:128], F.Identity, [], ["U%d" % h], [k])

        def spread(c, k, par, key, onto):
            h, items, R = c // 4, [], ["B", "Pb", key]
            for u in range(4):
                i, o = 4 * (c % 4) + u, ps[k][:, 128 * u:128 * u + 128]
                if onto == 1:
                    items.append((o, I, T.slabQ[:, 512 * c + 128 * u:512 * c + 128 * u + 128] if b
                                  else T.slabP[:, 2048 * h + i:2048 * h + 2048:16], True, False))
                items.append((o, T.B[:, 128 * i:128 * i + 128], par, onto == 0, onto < 2 or u == 3))
            if onto == 1:
                R += ["slabQ%d" % c] if b else ["slabP%d" % (4 * h + u) for u in range(4)]
            mm(128 * len(items), items, R, [k])

        def alive(c):
            spread(c, ab[c], total(T.mn, c // 4), "mn%d" % (c // 4), 2 if c < OPT["pre"] else 1)
            act(512, T.rb[:, 512 * c:512 * c + 512], ps[ab[c]][:, :], F.Identity, [], ["rb%d" % c], [ab[c]], bias=225.0,
                scale=16.0)

        span(0)
        for c in range(4):
            alive(c)
        span(1)
        for c in range(8):
            h, low = c // 4, T.yb[:, 512 * (c % 2):512 * (c % 2) + 512]
            spread(c, yk[c], T.U[:, 128 * h:128 * h + 128], "U%d" % h, 0)
            spread(c, xb[c], total(T.S, h), "S%d" % h, 1)
            tt(512, low, T.rb[:, 512 * c:512 * c + 512], ps[yk[c]][:, :], A.min, ["rb%d" % c], ["yb%d" % (c % 2)], [yk[c]])
            tt(512, T.slabQ[:, 512 * c:512 * c + 512], low, ps[xb[c]][:, :], A.min, ["yb%d" % (c % 2)], ["slabQ%d" % c],
               [xb[c]])
            if c + 4 < 8:
                alive(c + 4)
        mode["lazy"] = True
        while waiting:
            add_terms(*waiting.pop(0), late=["slabQ6"])
        mode["lazy"] = False
        SQ = ["slabQ%d" % c for c in range(8)] + ["inv"]
        act(picks(2048), T.slabN[:, 0:2048], T.slabQ[:, :].indirect(T.inv[:, 0:128]), F.Relu, SQ, ["q0", "q1", "slabN_o"],
            bias=15.0)
        ts(picks(2048), T.slabN[:, 2048:4096], T.slabQ[:, :].indirect(T.inv[:, 128:256]), 15.0, 0.0, A.add, A.max, SQ,
           ["q2", "q3"])

    def remainders(c0, c1, k):
        R = ["E%d%d" % (u, h) for u in range(c0 // 128, c1 // 128) for h in range(2)]
        w, E, o = c1 - c0, T.SR[:, cE(0) + c0:cE(0) + c1], ps[6][:, c0 // 2:c1 // 2]
        ts(w, T.ea[:, c0:c1], E, OFF, -1.0, A.max, A.mult, R, ["ea%d" % k])
        ts(w, T.ed[:, c0:c1], E, OFF, K16 - 7.5, A.max, A.add, R, ["ed%d" % k])
        mm(5 * w, [(o, win(T.Reb, -8 * hh), T.ed[:, c0 + hh:c1:2], hh == 0, False) for hh in range(2)]
           + [(o, win(T.Re32, -8 * hh), T.ea[:, c0 + hh:c1:2], False, hh == 1) for hh in range(2)],
           RR + ["Rf0", "Rf1", "ea%d" % k, "ed%d" % k], [6])
        ts(w // 2, T.eo[:, c0 // 2:c1 // 2], o, -64.0, 64 * (K16 - OFF), A.mult, A.add, [], ["eo%d" % k], [6])

    n, b = NB * LG - 1, NB - 1
    remainders(0, 256, 0)
    dma("s", "s_ef", [(T.sg_ef[:], T.eo[:, 0:128])], ["eo0"], ["sg_ef"])
    send("ef")
    unload("s", "ef", T.ye, 0, 128, [], "outs")
    for h in range(2):
        p = 512 * ((2 * n + h) % NP)
        for u in range(2):
            o, R = lists(n, h, 1, 16 * u, 16 * u + 16)
            c = 256 * u
            tt(picks(256), T.pk[:, p + c:p + c + 256], T.kpT[:, :].indirect(o), amt(n, 512 * h + c, 512 * h + c + 256), A.mult,
               KP + [akey(n, h, u)] + R, ["pk%d" % ((p + c) // 128 + e) for e in range(2)])
            add_terms(n, h, c, c + 256, u == 1)
        k, yo = "y%d" % h, T.yo[:, 512 * h:512 * h + 512]
        act(512, yo, ps[h][:, :], F.Exp, ["L%d" % h], ["yo%d" % h], [h], scale=-1.0 / 128)
        jobs[-1]["lead"] = 0 if h else OPT["lead"][b]
        dma("s", "s_" + k, [(T["sg_" + k][:], yo)], ["yo%d" % h], ["sg_" + k])
        send(k, OPT["ly"])
    for h in range(2):
        losses(n, h)
        spend(b, h)
    remainders(256, 384, 1)
    dma("a", "s_ee", [(T.sg_ee[:], T.eo[:, 128:192])], ["eo1"], ["sg_ee"], 2500)
    dma("a", "outs", [(T.ye[r0:r1, :], T.eo[r0:r1, :])], ["eo0", "eo1"], [])
    send("ee", OPT["le"])
    dma("s", "outs", [(T.yl[r0:r1, :], T.yo[r0:r1, :])], ["yo0", "yo1"], [])
    unload("s", "y0", T.yl, 0, 512, [], "outs")
    unload("s", "y1", T.yl, 512, 1024, [], "outs")
    unload("a", "ee", T.ye, 128, 192, [], "outs")
    if not ORDER:
        ORDER.extend(arrange(jobs))
    for n in ORDER:
        calls[n]()
    for s, v in cnt.items():
        g.wait_ge(T.sem[s], v)
